import numpy as np
import ml_dtypes


def mxq(x, axis, fmt="e4m3"):
    dtype, down = {"e4m3": (ml_dtypes.float8_e4m3fn, 7), "e5m2": (ml_dtypes.float8_e5m2, 14)}[fmt]
    v = np.moveaxis(np.asarray(x, np.float32).astype(ml_dtypes.bfloat16).astype(np.float64), axis, -1)
    blocks = v.reshape(v.shape[:-1] + (-1, 32))
    amax = np.abs(blocks).max(-1, keepdims=True)
    byte = np.maximum(np.where(amax > 0, np.frexp(amax)[1] - 1 + 127, 0) - down, 1)
    scale = np.exp2(byte - 127.0)
    codes = (blocks / scale).astype(np.float32).astype(dtype).astype(np.float64)
    return np.moveaxis((codes * scale).reshape(v.shape), -1, axis)


WIDE = False


def mx_kscale(k):
    if not WIDE:
        return np.ones(k)
    levels = np.array([10, -10, 5, -5, 0])
    if k % 512:
        return np.exp2(np.random.permutation(np.resize(levels, k // 32))).repeat(32)
    a = np.empty((k // 512, 16))
    for p in range(k // 512):
        a[p, :8] = np.random.permutation(np.resize(levels, 8))
        for g in range(8):
            far = levels[np.abs(levels - a[p, g]) >= 10]
            a[p, g + 8] = far[np.random.randint(len(far))]
    return np.exp2(a.ravel()).repeat(32)


def f64(x):
    return np.asarray(x).astype(np.float64)


def striped(idx):
    return np.tile(idx.reshape(-1, 16).T, (8, 1)).astype(np.uint16)


def unstriped(offs):
    return offs[:16].T.reshape(-1).astype(np.int64)


def striped8(idx):
    return np.concatenate([x.reshape(-1, 16).T for x in idx]).astype(np.uint16)


def runs(offs, k):
    lists = np.stack([offs[16 * r : 16 * r + 16].T.reshape(-1) for r in range(8)]).astype(np.int64)
    return lists[np.arange(k) % 512 // 64]


def pack_weight(w):
    k, n = w.shape
    w = f64(np.asarray(w, np.float32).astype(ml_dtypes.bfloat16)).reshape(k // 32, 32, n)
    amax = np.abs(w).max(1)
    byte = np.clip(np.where(amax > 0, np.frexp(amax)[1] - 1 + 127 - 7, 1), 1, 254)
    scaled = (w * np.exp2(127.0 - byte)[:, None, :]).reshape(k, n).astype(np.float32)
    words = np.ascontiguousarray(scaled.reshape(k // 512, 128, 4, n).transpose(0, 1, 3, 2)).astype(ml_dtypes.float8_e4m3fn).view(np.uint8)
    return words, np.ascontiguousarray(byte.astype(np.uint8).reshape(k // 512, 16, n))


def unpack_weight(words, scales):
    g, p, n, _ = words.shape
    vals = np.ascontiguousarray(words).view(ml_dtypes.float8_e4m3fn).astype(np.float64) * np.repeat(np.exp2(scales.astype(np.float64) - 127.0), 8, axis=1)[..., None]
    return vals.transpose(0, 1, 3, 2).reshape(g * 512, n)

def planes(y):
    n, m = y.shape
    v = y.astype(np.float32).astype(ml_dtypes.bfloat16).astype(np.float64).reshape(n // 32, 32, m)
    top = np.abs(v).max(1)
    byte = np.clip(np.where(top > 0, np.frexp(top)[1] - 1 + 127 - 7, 1), 1, 254)
    codes = (v * np.exp2(127.0 - byte)[:, None, :]).reshape(n, m).astype(np.float32).astype(ml_dtypes.float8_e4m3fn).view(np.uint8)
    words = codes.reshape(n // 512, 128, 4, m).transpose(0, 1, 3, 2)
    return np.ascontiguousarray(words), np.ascontiguousarray(byte.astype(np.uint8).reshape(n // 512, 16, m))


K, T, S, N, H, U = 512, 2048, 512, 512, 512, 512


def setup_inputs():
    n = np.random.standard_normal
    s = mx_kscale(K)[:, None]
    u = mx_kscale(H)
    packed_xT = pack_weight(n((K, T)) * s)
    packed_w1 = pack_weight(n((K, H)) / np.sqrt(K) / s)
    packed_w2 = pack_weight(n((H, N)) / np.sqrt(2 * H) / u[:, None])
    packed_w3 = pack_weight(n((H, N)) / np.sqrt(2 * H) / u[:, None])
    return {
        "x_words": packed_xT[0],
        "x_scales": packed_xT[1],
        "w1_words": packed_w1[0],
        "w1_scales": packed_w1[1],
        "mu": (0.5 * n((H, U))).astype(np.float32),
        "rs": np.random.uniform(0.5, 1.5, (H, U)).astype(np.float32),
        "g1": (np.random.uniform(0.5, 1.5, (H, 1)) * u[:, None]).astype(np.float32),
        "g2": (np.random.uniform(0.5, 1.5, (H, 1)) * u[:, None]).astype(np.float32),
        "w2_words": packed_w2[0],
        "w2_scales": packed_w2[1],
        "w3_words": packed_w3[0],
        "w3_scales": packed_w3[1],
        "offs": striped(np.random.permutation(T)[:S]),
        "k1": striped8(np.random.randint(0, U, (8, S))),
    }


def reference(x_words, x_scales, w1_words, w1_scales, mu, rs, g1, g2, w2_words, w2_scales, w3_words, w3_scales, offs, k1):
    xq = unpack_weight(x_words, x_scales)[:, unstriped(offs)]
    y = unpack_weight(w1_words, w1_scales).T @ xq
    d = (y - (f64(mu)[np.arange(H)[:, None], runs(k1, H)])) * (f64(rs)[np.arange(H)[:, None], runs(k1, H)])
    z = f64(g1) * d
    z2 = f64(g2) * ((d) ** 2 + -1.0)
    out_0 = unpack_weight(w2_words, w2_scales).T @ mxq(z, 0, "e4m3") + unpack_weight(w3_words, w3_scales).T @ mxq(z2, 0, "e4m3")
    return (out_0,) + planes(out_0)

@@ -1,0 +1,255 @@
+from contextlib import ExitStack
+
+import concourse.mybir as mybir
+
+K, T, S, N, H, U = 512, 2048, 512, 512, 512, 512
+FLOPS = 2 * S * (K * H + 2 * H * N)
+
+F32 = mybir.dt.float32
+BF16 = mybir.dt.bfloat16
+I32 = mybir.dt.int32
+U32 = mybir.dt.uint32
+U16 = mybir.dt.uint16
+U8 = mybir.dt.uint8
+FP8X4 = mybir.dt.float8_e4m3fn_x4
+ALU = mybir.AluOpType
+ACT = mybir.ActivationFunctionType
+
+P = 128
+PACK = 4
+CHUNK = 256
+BLOCK = 128
+LANES = 16
+
+
+def word_rows(words):
+    return words[0].rearrange("p c r -> p (c r)").bitcast(I32)
+
+
+def load_scale_rows(queue, plane, first, scales):
+    for q in range(4):
+        queue.dma_start(
+            out=plane[32 * q + first : 32 * q + first + 4, :].bitcast(I32),
+            in_=scales[0, 4 * q : 4 * q + 4, :].bitcast(I32),
+        )
+
+
+def deal_columns(nc, dealt, raw, run):
+    nc.vector.tensor_copy(
+        out=dealt[:].rearrange("p (t c i) -> p c t i", t=PACK, i=run),
+        in_=raw[:].rearrange("p (c i t) -> p c t i", t=PACK, i=run),
+    )
+
+
+def weave_views(woven, planar):
+    return (
+        woven.rearrange("p (c i t) -> p c t i", t=PACK, i=4),
+        planar.rearrange("p t (c i) -> p c t i", i=4),
+    )
+
+
+def tile_picked_fisher8_none_po_kernel(
+    tc, x_words, x_scales, w1_words, w1_scales, mu, rs, g1, g2, w2_words, w2_scales, w3_words, w3_scales,
+    offs, k1, out_0, out_1, out_2,
+):
+    nc = tc.nc
+    chunks = S // CHUNK
+    cols = CHUNK // LANES
+
+    with ExitStack() as ctx:
+        keep = ctx.enter_context(tc.tile_pool(name="keep", bufs=1))
+        psum = ctx.enter_context(tc.psum_pool(name="psum", bufs=1))
+
+        def sb(name, shape, dtype):
+            return keep.tile(shape, dtype, name=name, align_bytes=64)
+
+        def bank(number, name, shape):
+            return psum.tile(shape, F32, name=name, tag="bank%d" % number)
+
+        offs_sb = sb("offs_sb", [P, S // LANES], U16)
+        k1_sb = sb("k1_sb", [P, S // LANES], U16)
+        x_plane = sb("x_plane", [P, T], U8)
+        w1_plane = sb("w1_plane", [P, H], U8)
+        w23_plane = sb("w23_plane", [P, N], U8)
+        x_sb = sb("x_sb", [P, T], I32)
+        w1_raw = sb("w1_raw", [P, H], I32)
+        w2_raw = sb("w2_raw", [P, N], I32)
+        w3_raw = sb("w3_raw", [P, N], I32)
+        mu_sb = [sb("mu%d" % t, [P, U], F32) for t in range(PACK)]
+        rs_sb = [sb("rs%d" % t, [P, U], F32) for t in range(PACK)]
+        g1_sb = sb("g1_sb", [P, PACK], F32)
+        g2_sb = sb("g2_sb", [P, PACK], F32)
+
+        nc.vector.memset(x_plane[:, : T // 2].bitcast(I32), 0)
+        nc.gpsimd.memset(x_plane[:, T // 2 :].bitcast(I32), 0)
+        nc.vector.memset(w1_plane[:].bitcast(I32), 0)
+        nc.gpsimd.memset(w23_plane[:].bitcast(I32), 0)
+
+        nc.sync.dma_start(offs_sb[:], offs)
+        nc.sync.dma_start(k1_sb[:], k1)
+        nc.sync.dma_start(out=w1_raw[:], in_=word_rows(w1_words))
+        load_scale_rows(nc.sync, x_plane, 0, x_scales)
+        nc.sync.dma_start(out=x_sb[:], in_=word_rows(x_words))
+        load_scale_rows(nc.sync, w1_plane, 0, w1_scales)
+        mu_rows = mu.rearrange("(p t) u -> p t u", t=PACK)
+        rs_rows = rs.rearrange("(p t) u -> p t u", t=PACK)
+        for t in range(PACK):
+            nc.sync.dma_start(out=mu_sb[t][:], in_=mu_rows[:, t, :])
+            nc.sync.dma_start(out=rs_sb[t][:], in_=rs_rows[:, t, :])
+            if t == 0:
+                nc.sync.dma_start(out=g1_sb[:], in_=g1.rearrange("(p t) o -> p (t o)", t=PACK))
+                nc.sync.dma_start(out=g2_sb[:], in_=g2.rearrange("(p t) o -> p (t o)", t=PACK))
+        nc.sync.dma_start(out=w2_raw[:], in_=word_rows(w2_words))
+        nc.sync.dma_start(out=w3_raw[:], in_=word_rows(w3_words))
+        load_scale_rows(nc.sync, w23_plane, 0, w2_scales)
+        load_scale_rows(nc.sync, w23_plane, 4, w3_scales)
+
+        picked_plane = sb("picked_plane", [P, S], U8)
+        nc.vector.tensor_copy(out=picked_plane[:], in_=x_plane[:].indirect(offs_sb[:]))
+        w1_codes = sb("w1_codes", [P, H], I32)
+        w1_dealt = sb("w1_dealt", [P, H], U8)
+        deal_columns(nc, w1_codes, w1_raw, 4)
+        deal_columns(nc, w1_dealt, w1_plane, 16)
+
+        picked = []
+        for c in range(chunks):
+            codes = sb("picked%d" % c, [P, CHUNK], U32)
+            nc.vector.tensor_copy(
+                out=codes[:], in_=x_sb[:].bitcast(U32).indirect(offs_sb[:, c * cols : (c + 1) * cols])
+            )
+            picked.append(codes)
+
+        def first_product(c, t, dest):
+            nc.tensor.matmul_mx(
+                out=dest,
+                lhsT=w1_codes[:, t * P : (t + 1) * P].bitcast(FP8X4),
+                lhsT_scale=w1_dealt[:, t * P : (t + 1) * P],
+                rhs=picked[c][:].bitcast(FP8X4),
+                rhs_scale=picked_plane[:, c * CHUNK : (c + 1) * CHUNK],
+                start=True,
+                stop=True,
+            )
+
+        y_sb = {}
+        for t in range(PACK):
+            acc = bank(t, "y0_%d" % t, [P, CHUNK])
+            first_product(0, t, acc[:])
+            y_t = sb("y_sb0_%d" % t, [P, CHUNK], F32)
+            nc.scalar.copy(out=y_t[:], in_=acc[:])
+            y_sb[0, t] = y_t[:]
+        for h in range(2):
+            acc = bank(4 + h, "y1_%d" % h, [P, 2, CHUNK])
+            for j in range(2):
+                first_product(1, 2 * h + j, acc[:, j, :])
+            y_h = sb("y_sb1_%d" % h, [P, 2, CHUNK], F32)
+            nc.scalar.copy(out=y_h[:], in_=acc[:])
+            for j in range(2):
+                y_sb[1, 2 * h + j] = y_h[:, j, :]
+
+        neg_g1 = sb("neg_g1", [P, PACK], F32)
+        neg_g2 = sb("neg_g2", [P, PACK], F32)
+        nc.scalar.activation(out=neg_g1[:], in_=g1_sb[:], func=ACT.Copy, scale=-1.0)
+        nc.scalar.activation(out=neg_g2[:], in_=g2_sb[:], func=ACT.Copy, scale=-1.0)
+
+        gap, neg_d, z_planar, z2_planar = {}, {}, {}, {}
+
+        def subtract(c, t):
+            gap[c, t] = sb("gap%d_%d" % (c, t), [P, CHUNK], F32)
+            nc.vector.tensor_tensor(
+                gap[c, t][:], mu_sb[t][:].indirect(k1_sb[:, c * cols : (c + 1) * cols]), y_sb[c, t], ALU.subtract
+            )
+
+        def whiten(c, t):
+            neg_d[c, t] = sb("negd%d_%d" % (c, t), [P, CHUNK], F32)
+            nc.vector.tensor_tensor(
+                neg_d[c, t][:], rs_sb[t][:].indirect(k1_sb[:, c * cols : (c + 1) * cols]), gap[c, t][:], ALU.mult
+            )
+            square = sb("square%d_%d" % (c, t), [P, CHUNK], F32)
+            nc.scalar.activation(out=square[:], in_=neg_d[c, t][:], func=ACT.Square)
+            nc.scalar.activation(
+                out=z_planar[c][:, t, :], in_=neg_d[c, t][:], func=ACT.Copy, scale=neg_g1[:, t : t + 1]
+            )
+            nc.scalar.activation(
+                out=z2_planar[c][:, t, :], in_=square[:], func=ACT.Identity,
+                scale=g2_sb[:, t : t + 1], bias=neg_g2[:, t : t + 1],
+            )
+
+        def look_up(c):
+            z_planar[c] = sb("z_planar%d" % c, [P, PACK, CHUNK], BF16)
+            z2_planar[c] = sb("z2_planar%d" % c, [P, PACK, CHUNK], BF16)
+            subtract(c, 0)
+            for t in range(PACK):
+                if t + 1 < PACK:
+                    subtract(c, t + 1)
+                whiten(c, t)
+
+        woven = {}
+
+        def weave(c):
+            for j, planar in enumerate((z_planar[c], z2_planar[c])):
+                tile = sb("woven%d_%d" % (c, j), [P, CHUNK * PACK], BF16)
+                dst, src = weave_views(tile[:], planar[:])
+                if c == 0:
+                    nc.scalar.copy(out=dst, in_=src)
+                else:
+                    nc.vector.tensor_copy(out=dst, in_=src)
+                woven[c, j] = tile
+
+        look_up(0)
+        weave(0)
+        w2_codes = sb("w2_codes", [P, N], I32)
+        w3_codes = sb("w3_codes", [P, N], I32)
+        w23_dealt = sb("w23_dealt", [P, N], U8)
+        deal_columns(nc, w2_codes, w2_raw, 4)
+        deal_columns(nc, w3_codes, w3_raw, 4)
+        deal_columns(nc, w23_dealt, w23_plane, 16)
+        look_up(1)
+        weave(1)
+
+        out_codes = sb("out_codes", [P, S], U32)
+        out_plane = sb("out_plane", [P, S], U8)
+        out_rows = out_0.rearrange("(p t) n -> p t n", t=PACK)
+        out_words = word_rows(out_1)
+
+        for c in range(chunks):
+            codes, plane = [], []
+            for name in ("z", "z2"):
+                codes.append(sb("%s_codes%d" % (name, c), [P, CHUNK], U32))
+                plane.append(sb("%s_plane%d" % (name, c), [P, CHUNK], U8))
+            for j in range(2):
+                nc.vector.quantize_mx(out=codes[j][:].bitcast(FP8X4), scales=plane[j][:], in_=woven[c, j][:])
+
+            for b in range(CHUNK // BLOCK):
+                n = c * (CHUNK // BLOCK) + b
+                local = slice(b * BLOCK, (b + 1) * BLOCK)
+                tokens = slice(n * BLOCK, (n + 1) * BLOCK)
+                acc = bank((6 + n) % 8, "out%d" % n, [P, PACK, BLOCK])
+                for t in range(PACK):
+                    for j, w_codes in enumerate((w2_codes, w3_codes)):
+                        nc.tensor.matmul_mx(
+                            out=acc[:, t, :],
+                            lhsT=w_codes[:, t * P : (t + 1) * P].bitcast(FP8X4),
+                            lhsT_scale=w23_dealt[4 * j : P, t * P : (t + 1) * P],
+                            rhs=codes[j][:, local].bitcast(FP8X4),
+                            rhs_scale=plane[j][:, local],
+                            start=(j == 0),
+                            stop=(j == 1),
+                        )
+                result = sb("result%d" % n, [P, PACK, BLOCK], F32)
+                nc.scalar.copy(out=result[:], in_=acc[:])
+                nc.sync.dma_start(out=out_rows[:, :, tokens], in_=result[:])
+                rounded = sb("rounded%d" % n, [P, BLOCK * PACK], BF16)
+                dst, src = weave_views(rounded[:], result[:])
+                nc.vector.tensor_copy(out=dst, in_=src)
+                nc.vector.quantize_mx(
+                    out=out_codes[:, tokens].bitcast(FP8X4), scales=out_plane[:, tokens], in_=rounded[:]
+                )
+            span = slice(c * CHUNK, (c + 1) * CHUNK)
+            nc.sync.dma_start(out=out_words[:, span], in_=out_codes[:, span].bitcast(I32))
+
+        for q in range(4):
+            queue = nc.scalar if q % 2 else nc.sync
+            queue.dma_start(
+                out=out_2[0, 4 * q : 4 * q + 4, :].bitcast(I32),
+                in_=out_plane[32 * q : 32 * q + 4, :].bitcast(I32),
+            )

@@ -60,8 +60,8 @@ def tile_picked_fisher8_none_po_kernel(
         keep = ctx.enter_context(tc.tile_pool(name="keep", bufs=1))
         psum = ctx.enter_context(tc.psum_pool(name="psum", bufs=1))
 
-        def sb(name, shape, dtype):
-            return keep.tile(shape, dtype, name=name, align_bytes=64)
+        def sb(name, shape, dtype, tag=None):
+            return keep.tile(shape, dtype, name=name, tag=tag or name, align_bytes=64)
 
         def bank(number, name, shape):
             return psum.tile(shape, F32, name=name, tag="bank%d" % number)
@@ -111,79 +111,59 @@ def tile_picked_fisher8_none_po_kernel(
         deal_columns(nc, w1_codes, w1_raw, 4)
         deal_columns(nc, w1_dealt, w1_plane, 16)
 
-        picked = []
-        for c in range(chunks):
-            codes = sb("picked%d" % c, [P, CHUNK], U32)
+
+        y_banks = {}
+
+        def first_products(c):
+            picked = sb("picked%d" % c, [P, CHUNK], U32, "w1_plane" if c else None)
             nc.vector.tensor_copy(
-                out=codes[:], in_=x_sb[:].bitcast(U32).indirect(offs_sb[:, c * cols : (c + 1) * cols])
+                out=picked[:], in_=x_sb[:].bitcast(U32).indirect(offs_sb[:, c * cols : (c + 1) * cols])
             )
-            picked.append(codes)
+            for t in range(PACK):
+                acc = bank(PACK * c + t, "y%d_%d" % (c, t), [P, CHUNK])
+                nc.tensor.matmul_mx(
+                    out=acc[:],
+                    lhsT=w1_codes[:, t * P : (t + 1) * P].bitcast(FP8X4),
+                    lhsT_scale=w1_dealt[:, t * P : (t + 1) * P],
+                    rhs=picked[:].bitcast(FP8X4),
+                    rhs_scale=picked_plane[:, c * CHUNK : (c + 1) * CHUNK],
+                    start=True,
+                    stop=True,
+                )
+                y_banks[c, t] = acc
 
-        def first_product(c, t, dest):
-            nc.tensor.matmul_mx(
-                out=dest,
-                lhsT=w1_codes[:, t * P : (t + 1) * P].bitcast(FP8X4),
-                lhsT_scale=w1_dealt[:, t * P : (t + 1) * P],
-                rhs=picked[c][:].bitcast(FP8X4),
-                rhs_scale=picked_plane[:, c * CHUNK : (c + 1) * CHUNK],
-                start=True,
-                stop=True,
-            )
-
-        y_sb = {}
-        for t in range(PACK):
-            acc = bank(t, "y0_%d" % t, [P, CHUNK])
-            first_product(0, t, acc[:])
-            y_t = sb("y_sb0_%d" % t, [P, CHUNK], F32)
-            nc.scalar.copy(out=y_t[:], in_=acc[:])
-            y_sb[0, t] = y_t[:]
-        for h in range(2):
-            acc = bank(4 + h, "y1_%d" % h, [P, 2, CHUNK])
-            for j in range(2):
-                first_product(1, 2 * h + j, acc[:, j, :])
-            y_h = sb("y_sb1_%d" % h, [P, 2, CHUNK], F32)
-            nc.scalar.copy(out=y_h[:], in_=acc[:])
-            for j in range(2):
-                y_sb[1, 2 * h + j] = y_h[:, j, :]
-
-        neg_g1 = sb("neg_g1", [P, PACK], F32)
+        first_products(0)
         neg_g2 = sb("neg_g2", [P, PACK], F32)
-        nc.scalar.activation(out=neg_g1[:], in_=g1_sb[:], func=ACT.Copy, scale=-1.0)
         nc.scalar.activation(out=neg_g2[:], in_=g2_sb[:], func=ACT.Copy, scale=-1.0)
 
-        gap, neg_d, z_planar, z2_planar = {}, {}, {}, {}
-
-        def subtract(c, t):
-            gap[c, t] = sb("gap%d_%d" % (c, t), [P, CHUNK], F32)
-            nc.vector.tensor_tensor(
-                gap[c, t][:], mu_sb[t][:].indirect(k1_sb[:, c * cols : (c + 1) * cols]), y_sb[c, t], ALU.subtract
-            )
-
-        def whiten(c, t):
-            neg_d[c, t] = sb("negd%d_%d" % (c, t), [P, CHUNK], F32)
-            nc.vector.tensor_tensor(
-                neg_d[c, t][:], rs_sb[t][:].indirect(k1_sb[:, c * cols : (c + 1) * cols]), gap[c, t][:], ALU.mult
-            )
-            square = sb("square%d_%d" % (c, t), [P, CHUNK], F32)
-            nc.scalar.activation(out=square[:], in_=neg_d[c, t][:], func=ACT.Square)
-            nc.scalar.activation(
-                out=z_planar[c][:, t, :], in_=neg_d[c, t][:], func=ACT.Copy, scale=neg_g1[:, t : t + 1]
-            )
-            nc.scalar.activation(
-                out=z2_planar[c][:, t, :], in_=square[:], func=ACT.Identity,
-                scale=g2_sb[:, t : t + 1], bias=neg_g2[:, t : t + 1],
-            )
+        z_planar, z2_planar, woven = {}, {}, {}
 
         def look_up(c):
             z_planar[c] = sb("z_planar%d" % c, [P, PACK, CHUNK], BF16)
             z2_planar[c] = sb("z2_planar%d" % c, [P, PACK, CHUNK], BF16)
-            subtract(c, 0)
+            if c == 0:
+                mu_picked = sb("mu_picked", [P, 2 * PACK, CHUNK], F32, "looked_up")
+                rs_picked = sb("rs_picked", [P, PACK, CHUNK], F32)
+                rs_first = 0
+            else:
+                mu_picked = sb("both_picked", [P, 2 * PACK, CHUNK], F32, "looked_up")
+                rs_picked = mu_picked
+                rs_first = PACK
+            entries = k1_sb[:, c * cols : (c + 1) * cols]
             for t in range(PACK):
-                if t + 1 < PACK:
-                    subtract(c, t + 1)
-                whiten(c, t)
-
-        woven = {}
+                nc.vector.tensor_copy(out=mu_picked[:, t, :], in_=mu_sb[t][:].indirect(entries))
+                nc.vector.tensor_copy(out=rs_picked[:, rs_first + t, :], in_=rs_sb[t][:].indirect(entries))
+                gap = sb("gap%d_%d" % (c, t), [P, CHUNK], F32)
+                nc.vector.tensor_tensor(gap[:], y_banks[c, t][:], mu_picked[:, t, :], ALU.subtract)
+                d = sb("d%d_%d" % (c, t), [P, CHUNK], F32)
+                nc.gpsimd.tensor_tensor(d[:], gap[:], rs_picked[:, rs_first + t, :], ALU.mult)
+                square = sb("square%d_%d" % (c, t), [P, CHUNK], F32)
+                nc.scalar.activation(out=z_planar[c][:, t, :], in_=d[:], func=ACT.Copy, scale=g1_sb[:, t : t + 1])
+                nc.scalar.activation(out=square[:], in_=d[:], func=ACT.Square)
+                nc.scalar.activation(
+                    out=z2_planar[c][:, t, :], in_=square[:], func=ACT.Identity,
+                    scale=g2_sb[:, t : t + 1], bias=neg_g2[:, t : t + 1],
+                )
 
         def weave(c):
             for j, planar in enumerate((z_planar[c], z2_planar[c])):
@@ -196,6 +176,7 @@ def tile_picked_fisher8_none_po_kernel(
                 woven[c, j] = tile
 
         look_up(0)
+        first_products(1)
         weave(0)
         w2_codes = sb("w2_codes", [P, N], I32)
         w3_codes = sb("w3_codes", [P, N], I32)
@@ -204,48 +185,49 @@ def tile_picked_fisher8_none_po_kernel(
         deal_columns(nc, w3_codes, w3_raw, 4)
         deal_columns(nc, w23_dealt, w23_plane, 16)
         look_up(1)
-        weave(1)
 
         out_codes = sb("out_codes", [P, S], U32)
         out_plane = sb("out_plane", [P, S], U8)
         out_rows = out_0.rearrange("(p t) n -> p t n", t=PACK)
         out_words = word_rows(out_1)
+        result = {}
 
-        for c in range(chunks):
-            codes, plane = [], []
-            for name in ("z", "z2"):
-                codes.append(sb("%s_codes%d" % (name, c), [P, CHUNK], U32))
-                plane.append(sb("%s_plane%d" % (name, c), [P, CHUNK], U8))
-            for j in range(2):
-                nc.vector.quantize_mx(out=codes[j][:].bitcast(FP8X4), scales=plane[j][:], in_=woven[c, j][:])
-
-            for b in range(CHUNK // BLOCK):
-                n = c * (CHUNK // BLOCK) + b
-                local = slice(b * BLOCK, (b + 1) * BLOCK)
-                tokens = slice(n * BLOCK, (n + 1) * BLOCK)
-                acc = bank((6 + n) % 8, "out%d" % n, [P, PACK, BLOCK])
-                for t in range(PACK):
-                    for j, w_codes in enumerate((w2_codes, w3_codes)):
-                        nc.tensor.matmul_mx(
-                            out=acc[:, t, :],
-                            lhsT=w_codes[:, t * P : (t + 1) * P].bitcast(FP8X4),
-                            lhsT_scale=w23_dealt[4 * j : P, t * P : (t + 1) * P],
-                            rhs=codes[j][:, local].bitcast(FP8X4),
-                            rhs_scale=plane[j][:, local],
-                            start=(j == 0),
-                            stop=(j == 1),
-                        )
-                result = sb("result%d" % n, [P, PACK, BLOCK], F32)
-                nc.scalar.copy(out=result[:], in_=acc[:])
-                nc.sync.dma_start(out=out_rows[:, :, tokens], in_=result[:])
-                rounded = sb("rounded%d" % n, [P, BLOCK * PACK], BF16)
-                dst, src = weave_views(rounded[:], result[:])
-                nc.vector.tensor_copy(out=dst, in_=src)
-                nc.vector.quantize_mx(
-                    out=out_codes[:, tokens].bitcast(FP8X4), scales=out_plane[:, tokens], in_=rounded[:]
-                )
+        def second_products(c):
             span = slice(c * CHUNK, (c + 1) * CHUNK)
+            accs = [bank(PACK * c + t, "out%d_%d" % (c, t), [P, CHUNK]) for t in range(PACK)]
+            for j, w_codes in enumerate((w2_codes, w3_codes)):
+                codes = sb("z_codes%d_%d" % (c, j), [P, CHUNK], U32)
+                plane = sb("z_plane%d_%d" % (c, j), [P, CHUNK], U8)
+                nc.vector.quantize_mx(out=codes[:].bitcast(FP8X4), scales=plane[:], in_=woven[c, j][:])
+                for t in range(PACK):
+                    nc.tensor.matmul_mx(
+                        out=accs[t][:],
+                        lhsT=w_codes[:, t * P : (t + 1) * P].bitcast(FP8X4),
+                        lhsT_scale=w23_dealt[4 * j : P, t * P : (t + 1) * P],
+                        rhs=codes[:].bitcast(FP8X4),
+                        rhs_scale=plane[:],
+                        start=(j == 0),
+                        stop=(j == 1),
+                    )
+            result[c] = sb("result%d" % c, [P, PACK, CHUNK], F32)
+            for t in range(PACK):
+                nc.scalar.copy(out=result[c][:, t, :], in_=accs[t][:])
+                if t % 2 == 1:
+                    nc.sync.dma_start(out=out_rows[:, t - 1 : t + 1, span], in_=result[c][:, t - 1 : t + 1, :])
+
+        def hand_on(c):
+            span = slice(c * CHUNK, (c + 1) * CHUNK)
+            rounded = sb("rounded%d" % c, [P, CHUNK * PACK], BF16)
+            dst, src = weave_views(rounded[:], result[c][:])
+            nc.vector.tensor_copy(out=dst, in_=src)
+            nc.vector.quantize_mx(out=out_codes[:, span].bitcast(FP8X4), scales=out_plane[:, span], in_=rounded[:])
             nc.sync.dma_start(out=out_words[:, span], in_=out_codes[:, span].bitcast(I32))
+
+        second_products(0)
+        weave(1)
+        second_products(1)
+        hand_on(0)
+        hand_on(1)
 
         for q in range(4):
             queue = nc.scalar if q % 2 else nc.sync

@@ -16,35 +16,41 @@ ALU = mybir.AluOpType
 ACT = mybir.ActivationFunctionType
 
 P = 128
-PACK = 4
+SLOTS = 4
+QUADRANT = 32
+SCALE_ROWS = 4
+GROUP = 16
+LINE = 16
 CHUNK = 256
-BLOCK = 128
-LANES = 16
+CHUNKS = S // CHUNK
+LAST = CHUNKS - 1
+VECTOR_SLOT = 2
 
 
 def word_rows(words):
     return words[0].rearrange("p c r -> p (c r)").bitcast(I32)
 
 
-def load_scale_rows(queue, plane, first, scales):
-    for q in range(4):
-        queue.dma_start(
-            out=plane[32 * q + first : 32 * q + first + 4, :].bitcast(I32),
-            in_=scales[0, 4 * q : 4 * q + 4, :].bitcast(I32),
+def load_plane(nc, plane, first, scales):
+    for r in range(SCALE_ROWS):
+        nc.sync.dma_start(
+            out=plane[first + r : P : QUADRANT, :].bitcast(I32),
+            in_=scales[0, r : SCALE_ROWS * (P // QUADRANT) : SCALE_ROWS, :].bitcast(I32),
         )
 
 
-def deal_columns(nc, dealt, raw, run):
+def deal_columns(nc, dealt, raw, element_bytes):
+    run = LINE // element_bytes
     nc.vector.tensor_copy(
-        out=dealt[:].rearrange("p (t c i) -> p c t i", t=PACK, i=run),
-        in_=raw[:].rearrange("p (c i t) -> p c t i", t=PACK, i=run),
+        out=dealt[:].rearrange("p (t c i) -> p c t i", t=SLOTS, i=run),
+        in_=raw[:].rearrange("p (c i t) -> p c t i", t=SLOTS, i=run),
     )
 
 
-def weave_views(woven, planar):
-    return (
-        woven.rearrange("p (c i t) -> p c t i", t=PACK, i=4),
-        planar.rearrange("p t (c i) -> p c t i", i=4),
+def weave(copy, woven, planar):
+    copy(
+        out=woven[:].rearrange("p (c i t) -> p c t i", t=SLOTS, i=4),
+        in_=planar[:].rearrange("p t (c i) -> p c t i", i=4),
     )
 
 
@@ -53,185 +59,211 @@ def tile_picked_fisher8_none_po_kernel(
     offs, k1, out_0, out_1, out_2,
 ):
     nc = tc.nc
-    chunks = S // CHUNK
-    cols = CHUNK // LANES
 
     with ExitStack() as ctx:
         keep = ctx.enter_context(tc.tile_pool(name="keep", bufs=1))
         psum = ctx.enter_context(tc.psum_pool(name="psum", bufs=1))
 
-        def sb(name, shape, dtype, tag=None):
+        def sbuf(name, shape, dtype, tag=None):
             return keep.tile(shape, dtype, name=name, tag=tag or name, align_bytes=64)
 
-        def bank(number, name, shape):
-            return psum.tile(shape, F32, name=name, tag="bank%d" % number)
+        def bank(c, t, name, shape):
+            return psum.tile(shape, F32, name=name, tag="bank%d" % (SLOTS * c + t))
 
-        offs_sb = sb("offs_sb", [P, S // LANES], U16)
-        k1_sb = sb("k1_sb", [P, S // LANES], U16)
-        x_plane = sb("x_plane", [P, T], U8)
-        w1_plane = sb("w1_plane", [P, H], U8)
-        w23_plane = sb("w23_plane", [P, N], U8)
-        x_sb = sb("x_sb", [P, T], I32)
-        w1_raw = sb("w1_raw", [P, H], I32)
-        w2_raw = sb("w2_raw", [P, N], I32)
-        w3_raw = sb("w3_raw", [P, N], I32)
-        mu_sb = [sb("mu%d" % t, [P, U], F32) for t in range(PACK)]
-        rs_sb = [sb("rs%d" % t, [P, U], F32) for t in range(PACK)]
-        g1_sb = sb("g1_sb", [P, PACK], F32)
-        g2_sb = sb("g2_sb", [P, PACK], F32)
+        def columns(c):
+            return slice(c * CHUNK, (c + 1) * CHUNK)
+
+        def entries(list_tile, c):
+            return list_tile[:, c * CHUNK // GROUP : (c + 1) * CHUNK // GROUP]
+
+        def places(t):
+            return slice(t * P, (t + 1) * P)
+
+        offs_sb = sbuf("offs_sb", [P, S // GROUP], U16)
+        k1_sb = sbuf("k1_sb", [P, S // GROUP], U16)
+        x_plane = sbuf("x_plane", [P, T], U8)
+        w1_plane = sbuf("w1_plane", [P, H], U8)
+        w23_plane = sbuf("w23_plane", [P, N], U8)
+        x_sb = sbuf("x_sb", [P, T], I32)
+        w1_raw = sbuf("w1_raw", [P, H], I32)
+        w2_raw = sbuf("w2_raw", [P, N], I32)
+        w3_raw = sbuf("w3_raw", [P, N], I32)
+        mu_sb = [sbuf("mu%d" % t, [P, U], F32) for t in range(SLOTS)]
+        rs_sb = [sbuf("rs%d" % t, [P, U], F32) for t in range(SLOTS)]
+        g1_sb = sbuf("g1_sb", [P, SLOTS], F32)
+        g2_sb = sbuf("g2_sb", [P, SLOTS], F32)
 
         nc.vector.memset(x_plane[:, : T // 2].bitcast(I32), 0)
         nc.gpsimd.memset(x_plane[:, T // 2 :].bitcast(I32), 0)
         nc.vector.memset(w1_plane[:].bitcast(I32), 0)
         nc.gpsimd.memset(w23_plane[:].bitcast(I32), 0)
 
-        nc.sync.dma_start(offs_sb[:], offs)
+        mu_rows = mu.rearrange("(p t) u -> p t u", t=SLOTS)
+        rs_rows = rs.rearrange("(p t) u -> p t u", t=SLOTS)
         nc.sync.dma_start(k1_sb[:], k1)
-        nc.sync.dma_start(out=w1_raw[:], in_=word_rows(w1_words))
-        load_scale_rows(nc.sync, x_plane, 0, x_scales)
+        nc.sync.dma_start(out=mu_sb[0][:], in_=mu_rows[:, 0, :])
+        nc.sync.dma_start(offs_sb[:], offs)
+        load_plane(nc, x_plane, 0, x_scales)
         nc.sync.dma_start(out=x_sb[:], in_=word_rows(x_words))
-        load_scale_rows(nc.sync, w1_plane, 0, w1_scales)
-        mu_rows = mu.rearrange("(p t) u -> p t u", t=PACK)
-        rs_rows = rs.rearrange("(p t) u -> p t u", t=PACK)
-        for t in range(PACK):
-            nc.sync.dma_start(out=mu_sb[t][:], in_=mu_rows[:, t, :])
+        nc.sync.dma_start(out=w1_raw[:], in_=word_rows(w1_words))
+        load_plane(nc, w1_plane, 0, w1_scales)
+        for t in range(SLOTS):
+            if t + 1 < SLOTS:
+                nc.sync.dma_start(out=mu_sb[t + 1][:], in_=mu_rows[:, t + 1, :])
             nc.sync.dma_start(out=rs_sb[t][:], in_=rs_rows[:, t, :])
             if t == 0:
-                nc.sync.dma_start(out=g1_sb[:], in_=g1.rearrange("(p t) o -> p (t o)", t=PACK))
-                nc.sync.dma_start(out=g2_sb[:], in_=g2.rearrange("(p t) o -> p (t o)", t=PACK))
+                nc.sync.dma_start(out=g1_sb[:], in_=g1.rearrange("(p t) o -> p (t o)", t=SLOTS))
+                nc.sync.dma_start(out=g2_sb[:], in_=g2.rearrange("(p t) o -> p (t o)", t=SLOTS))
+        load_plane(nc, w23_plane, 0, w2_scales)
+        load_plane(nc, w23_plane, SCALE_ROWS, w3_scales)
         nc.sync.dma_start(out=w2_raw[:], in_=word_rows(w2_words))
         nc.sync.dma_start(out=w3_raw[:], in_=word_rows(w3_words))
-        load_scale_rows(nc.sync, w23_plane, 0, w2_scales)
-        load_scale_rows(nc.sync, w23_plane, 4, w3_scales)
 
-        picked_plane = sb("picked_plane", [P, S], U8)
+        mu0_picked = sbuf("mu0_picked", [P, S], F32)
+        for c in range(CHUNKS):
+            nc.vector.tensor_copy(out=mu0_picked[:, columns(c)], in_=mu_sb[0][:].indirect(entries(k1_sb, c)))
+        picked_plane = sbuf("picked_plane", [P, S], U8)
         nc.vector.tensor_copy(out=picked_plane[:], in_=x_plane[:].indirect(offs_sb[:]))
-        w1_codes = sb("w1_codes", [P, H], I32)
-        w1_dealt = sb("w1_dealt", [P, H], U8)
+        w1_codes = sbuf("w1_codes", [P, H], I32)
+        w1_dealt_plane = sbuf("w1_dealt_plane", [P, H], U8)
         deal_columns(nc, w1_codes, w1_raw, 4)
-        deal_columns(nc, w1_dealt, w1_plane, 16)
+        deal_columns(nc, w1_dealt_plane, w1_plane, 1)
 
+        y = {}
 
-        y_banks = {}
+        def first_product(c):
+            picked = sbuf("picked%d" % c, [P, CHUNK], U32, "w1_plane" if c else None)
+            nc.vector.tensor_copy(out=picked[:], in_=x_sb[:].bitcast(U32).indirect(entries(offs_sb, c)))
+            for slots in ((0,), (1,), (2, 3)):
+                shape = [P, len(slots), CHUNK]
+                acc = bank(c, slots[0], "y%d_%d" % (c, slots[0]), shape)
+                held = sbuf("y_sb%d_%d" % (c, slots[0]), shape, F32) if slots[0] else acc
+                for j, t in enumerate(slots):
+                    nc.tensor.matmul_mx(
+                        out=acc[:, j, :],
+                        lhsT=w1_codes[:, places(t)].bitcast(FP8X4),
+                        lhsT_scale=w1_dealt_plane[:, places(t)],
+                        rhs=picked[:].bitcast(FP8X4),
+                        rhs_scale=picked_plane[:, columns(c)],
+                        start=True,
+                        stop=True,
+                    )
+                    y[c, t] = held[:, j, :]
+                if slots[0]:
+                    nc.scalar.copy(out=held[:], in_=acc[:])
 
-        def first_products(c):
-            picked = sb("picked%d" % c, [P, CHUNK], U32, "w1_plane" if c else None)
-            nc.vector.tensor_copy(
-                out=picked[:], in_=x_sb[:].bitcast(U32).indirect(offs_sb[:, c * cols : (c + 1) * cols])
-            )
-            for t in range(PACK):
-                acc = bank(PACK * c + t, "y%d_%d" % (c, t), [P, CHUNK])
-                nc.tensor.matmul_mx(
-                    out=acc[:],
-                    lhsT=w1_codes[:, t * P : (t + 1) * P].bitcast(FP8X4),
-                    lhsT_scale=w1_dealt[:, t * P : (t + 1) * P],
-                    rhs=picked[:].bitcast(FP8X4),
-                    rhs_scale=picked_plane[:, c * CHUNK : (c + 1) * CHUNK],
-                    start=True,
-                    stop=True,
-                )
-                y_banks[c, t] = acc
+        for c in range(CHUNKS):
+            first_product(c)
 
-        first_products(0)
-        neg_g2 = sb("neg_g2", [P, PACK], F32)
-        nc.scalar.activation(out=neg_g2[:], in_=g2_sb[:], func=ACT.Copy, scale=-1.0)
+        neg_g1 = sbuf("neg_g1", [P, SLOTS], F32)
+        neg_g2 = sbuf("neg_g2", [P, SLOTS], F32)
+        nc.gpsimd.tensor_scalar(neg_g1[:], g1_sb[:], -1.0, 0.0, ALU.mult, ALU.add)
+        nc.gpsimd.tensor_scalar(neg_g2[:], g2_sb[:], -1.0, 0.0, ALU.mult, ALU.add)
 
-        z_planar, z2_planar, woven = {}, {}, {}
+        def two_orders(c):
+            z = sbuf("z_planar%d" % c, [P, SLOTS, CHUNK], BF16)
+            z2 = sbuf("z2_planar%d" % c, [P, SLOTS, CHUNK], BF16)
+            gap = sbuf("gap%d" % c, [P, SLOTS, CHUNK], F32, "gap")
 
-        def look_up(c):
-            z_planar[c] = sb("z_planar%d" % c, [P, PACK, CHUNK], BF16)
-            z2_planar[c] = sb("z2_planar%d" % c, [P, PACK, CHUNK], BF16)
-            if c == 0:
-                mu_picked = sb("mu_picked", [P, 2 * PACK, CHUNK], F32, "looked_up")
-                rs_picked = sb("rs_picked", [P, PACK, CHUNK], F32)
-                rs_first = 0
-            else:
-                mu_picked = sb("both_picked", [P, 2 * PACK, CHUNK], F32, "looked_up")
-                rs_picked = mu_picked
-                rs_first = PACK
-            entries = k1_sb[:, c * cols : (c + 1) * cols]
-            for t in range(PACK):
-                nc.vector.tensor_copy(out=mu_picked[:, t, :], in_=mu_sb[t][:].indirect(entries))
-                nc.vector.tensor_copy(out=rs_picked[:, rs_first + t, :], in_=rs_sb[t][:].indirect(entries))
-                gap = sb("gap%d_%d" % (c, t), [P, CHUNK], F32)
-                nc.vector.tensor_tensor(gap[:], y_banks[c, t][:], mu_picked[:, t, :], ALU.subtract)
-                d = sb("d%d_%d" % (c, t), [P, CHUNK], F32)
-                nc.gpsimd.tensor_tensor(d[:], gap[:], rs_picked[:, rs_first + t, :], ALU.mult)
-                square = sb("square%d_%d" % (c, t), [P, CHUNK], F32)
-                nc.scalar.activation(out=z_planar[c][:, t, :], in_=d[:], func=ACT.Copy, scale=g1_sb[:, t : t + 1])
-                nc.scalar.activation(out=square[:], in_=d[:], func=ACT.Square)
-                nc.scalar.activation(
-                    out=z2_planar[c][:, t, :], in_=square[:], func=ACT.Identity,
-                    scale=g2_sb[:, t : t + 1], bias=neg_g2[:, t : t + 1],
-                )
+            def subtract(t):
+                means = mu_sb[t][:].indirect(entries(k1_sb, c)) if t else mu0_picked[:, columns(c)]
+                nc.vector.tensor_tensor(gap[:, t, :], means, y[c, t], ALU.subtract)
 
-        def weave(c):
-            for j, planar in enumerate((z_planar[c], z2_planar[c])):
-                tile = sb("woven%d_%d" % (c, j), [P, CHUNK * PACK], BF16)
-                dst, src = weave_views(tile[:], planar[:])
-                if c == 0:
-                    nc.scalar.copy(out=dst, in_=src)
-                else:
-                    nc.vector.tensor_copy(out=dst, in_=src)
-                woven[c, j] = tile
+            groups = [(0, 1), (2,), (3,)] if c == LAST else [(0, 1), (2, 3)]
+            subtract(0)
+            for slots in groups:
+                shape = [P, len(slots), CHUNK]
+                neg_d = sbuf("neg_d%d_%d" % (c, slots[0]), shape, F32)
+                square = sbuf("square%d_%d" % (c, slots[0]), shape, F32)
+                for j, t in enumerate(slots):
+                    if t + 1 < SLOTS:
+                        subtract(t + 1)
+                    nc.vector.tensor_tensor(
+                        neg_d[:, j, :], rs_sb[t][:].indirect(entries(k1_sb, c)), gap[:, t, :], ALU.mult
+                    )
+                    if (c, t) == (LAST, SLOTS - 1):
+                        nc.vector.tensor_scalar(z[:, t, :], neg_d[:, j, :], neg_g1[:, t : t + 1], None, ALU.mult)
+                    else:
+                        nc.scalar.activation(
+                            out=z[:, t, :], in_=neg_d[:, j, :], func=ACT.Copy, scale=neg_g1[:, t : t + 1]
+                        )
+                nc.scalar.activation(out=square[:], in_=neg_d[:], func=ACT.Square)
+                for j, t in enumerate(slots):
+                    nc.scalar.activation(
+                        out=z2[:, t, :], in_=square[:, j, :], func=ACT.Identity,
+                        scale=g2_sb[:, t : t + 1], bias=neg_g2[:, t : t + 1],
+                    )
+            return z, z2
 
-        look_up(0)
-        first_products(1)
-        weave(0)
-        w2_codes = sb("w2_codes", [P, N], I32)
-        w3_codes = sb("w3_codes", [P, N], I32)
-        w23_dealt = sb("w23_dealt", [P, N], U8)
+        def weave_orders(c, orders, copy):
+            woven = []
+            for j, planar in enumerate(orders):
+                woven.append(sbuf("woven%d_%d" % (c, j), [P, CHUNK * SLOTS], BF16))
+                weave(copy, woven[j], planar)
+            return woven
+
+        def quantise_orders(c, woven):
+            quantised = []
+            for j, values in enumerate(woven):
+                codes = sbuf("z_codes%d_%d" % (c, j), [P, CHUNK], U32)
+                plane = sbuf("z_plane%d_%d" % (c, j), [P, CHUNK], U8)
+                nc.vector.quantize_mx(out=codes[:].bitcast(FP8X4), scales=plane[:], in_=values[:])
+                quantised.append((codes, plane))
+            return quantised
+
+        woven_first = weave_orders(0, two_orders(0), nc.scalar.copy)
+        w2_codes = sbuf("w2_codes", [P, N], I32)
+        w3_codes = sbuf("w3_codes", [P, N], I32)
+        w23_dealt_plane = sbuf("w23_dealt_plane", [P, N], U8)
         deal_columns(nc, w2_codes, w2_raw, 4)
         deal_columns(nc, w3_codes, w3_raw, 4)
-        deal_columns(nc, w23_dealt, w23_plane, 16)
-        look_up(1)
+        deal_columns(nc, w23_dealt_plane, w23_plane, 1)
+        quantised_first = quantise_orders(0, woven_first)
+        orders_last = two_orders(LAST)
 
-        out_codes = sb("out_codes", [P, S], U32)
-        out_plane = sb("out_plane", [P, S], U8)
-        out_rows = out_0.rearrange("(p t) n -> p t n", t=PACK)
+        out_codes = sbuf("out_codes", [P, S], U32)
+        out_plane = sbuf("out_plane", [P, S], U8)
+        out_rows = out_0.rearrange("(p t) n -> p t n", t=SLOTS)
         out_words = word_rows(out_1)
-        result = {}
 
-        def second_products(c):
-            span = slice(c * CHUNK, (c + 1) * CHUNK)
-            accs = [bank(PACK * c + t, "out%d_%d" % (c, t), [P, CHUNK]) for t in range(PACK)]
+        def second_product(c, quantised):
+            accs = [bank(c, t, "out%d_%d" % (c, t), [P, CHUNK]) for t in range(SLOTS)]
             for j, w_codes in enumerate((w2_codes, w3_codes)):
-                codes = sb("z_codes%d_%d" % (c, j), [P, CHUNK], U32)
-                plane = sb("z_plane%d_%d" % (c, j), [P, CHUNK], U8)
-                nc.vector.quantize_mx(out=codes[:].bitcast(FP8X4), scales=plane[:], in_=woven[c, j][:])
-                for t in range(PACK):
+                codes, plane = quantised[j]
+                for t in range(SLOTS):
                     nc.tensor.matmul_mx(
                         out=accs[t][:],
-                        lhsT=w_codes[:, t * P : (t + 1) * P].bitcast(FP8X4),
-                        lhsT_scale=w23_dealt[4 * j : P, t * P : (t + 1) * P],
+                        lhsT=w_codes[:, places(t)].bitcast(FP8X4),
+                        lhsT_scale=w23_dealt_plane[SCALE_ROWS * j : P, places(t)],
                         rhs=codes[:].bitcast(FP8X4),
                         rhs_scale=plane[:],
                         start=(j == 0),
                         stop=(j == 1),
                     )
-            result[c] = sb("result%d" % c, [P, PACK, CHUNK], F32)
-            for t in range(PACK):
-                nc.scalar.copy(out=result[c][:, t, :], in_=accs[t][:])
+            result = sbuf("result%d" % c, [P, SLOTS, CHUNK], F32)
+            for t in range(SLOTS):
+                copy = nc.vector.tensor_copy if (c, t) == (LAST, VECTOR_SLOT) else nc.scalar.copy
+                copy(out=result[:, t, :], in_=accs[t][:])
                 if t % 2 == 1:
-                    nc.sync.dma_start(out=out_rows[:, t - 1 : t + 1, span], in_=result[c][:, t - 1 : t + 1, :])
+                    nc.sync.dma_start(out=out_rows[:, t - 1 : t + 1, columns(c)], in_=result[:, t - 1 : t + 1, :])
+            return result
 
-        def hand_on(c):
-            span = slice(c * CHUNK, (c + 1) * CHUNK)
-            rounded = sb("rounded%d" % c, [P, CHUNK * PACK], BF16)
-            dst, src = weave_views(rounded[:], result[c][:])
-            nc.vector.tensor_copy(out=dst, in_=src)
-            nc.vector.quantize_mx(out=out_codes[:, span].bitcast(FP8X4), scales=out_plane[:, span], in_=rounded[:])
-            nc.sync.dma_start(out=out_words[:, span], in_=out_codes[:, span].bitcast(I32))
+        def hand_on(c, result):
+            rounded = sbuf("rounded%d" % c, [P, CHUNK * SLOTS], BF16)
+            weave(nc.vector.tensor_copy, rounded, result)
+            nc.vector.quantize_mx(
+                out=out_codes[:, columns(c)].bitcast(FP8X4), scales=out_plane[:, columns(c)], in_=rounded[:]
+            )
+            nc.sync.dma_start(out=out_words[:, columns(c)], in_=out_codes[:, columns(c)].bitcast(I32))
 
-        second_products(0)
-        weave(1)
-        second_products(1)
-        hand_on(0)
-        hand_on(1)
+        quantised_last = quantise_orders(LAST, weave_orders(LAST, orders_last, nc.vector.tensor_copy))
+        results = [second_product(c, quantised) for c, quantised in enumerate((quantised_first, quantised_last))]
+        for c, result in enumerate(results):
+            hand_on(c, result)
 
-        for q in range(4):
+        for q in range(P // QUADRANT):
             queue = nc.scalar if q % 2 else nc.sync
             queue.dma_start(
-                out=out_2[0, 4 * q : 4 * q + 4, :].bitcast(I32),
-                in_=out_plane[32 * q : 32 * q + 4, :].bitcast(I32),
+                out=out_2[0, SCALE_ROWS * q : SCALE_ROWS * (q + 1), :].bitcast(I32),
+                in_=out_plane[QUADRANT * q : QUADRANT * q + SCALE_ROWS, :].bitcast(I32),
             )

@@ -22,9 +22,8 @@ SCALE_ROWS = 4
 GROUP = 16
 LINE = 16
 CHUNK = 256
-CHUNKS = S // CHUNK
-LAST = CHUNKS - 1
-VECTOR_SLOT = 2
+UNIT = 128
+KB = 1024
 
 
 def word_rows(words):
@@ -49,8 +48,8 @@ def deal_columns(nc, dealt, raw, element_bytes):
 
 def weave(copy, woven, planar):
     copy(
-        out=woven[:].rearrange("p (c i t) -> p c t i", t=SLOTS, i=4),
-        in_=planar[:].rearrange("p t (c i) -> p c t i", i=4),
+        out=woven.rearrange("p (c i t) -> p c t i", t=SLOTS, i=4),
+        in_=planar.rearrange("p t (c i) -> p c t i", i=4),
     )
 
 
@@ -59,25 +58,27 @@ def tile_picked_fisher8_none_po_kernel(
     offs, k1, out_0, out_1, out_2,
 ):
     nc = tc.nc
+    on_vector, on_scalar = nc.vector.tensor_copy, nc.scalar.copy
 
     with ExitStack() as ctx:
         keep = ctx.enter_context(tc.tile_pool(name="keep", bufs=1))
+        placed = ctx.enter_context(tc.tile_pool(name="placed", bufs=1))
         psum = ctx.enter_context(tc.psum_pool(name="psum", bufs=1))
 
         def sbuf(name, shape, dtype, tag=None):
             return keep.tile(shape, dtype, name=name, tag=tag or name, align_bytes=64)
 
-        def bank(c, t, name, shape):
-            return psum.tile(shape, F32, name=name, tag="bank%d" % (SLOTS * c + t))
+        def at(offset, name, shape, dtype):
+            return placed.tile(shape, dtype, name=name, tag=name, align_bytes=64, offset=offset)
 
-        def columns(c):
-            return slice(c * CHUNK, (c + 1) * CHUNK)
+        def bank(b, name, shape):
+            return psum.tile(shape, F32, name=name, tag="bank%d" % b)
 
-        def entries(list_tile, c):
-            return list_tile[:, c * CHUNK // GROUP : (c + 1) * CHUNK // GROUP]
+        def entries(list_tile, first, width):
+            return list_tile[:, first // GROUP : (first + width) // GROUP]
 
-        def places(t):
-            return slice(t * P, (t + 1) * P)
+        def part(i, width):
+            return slice(i * width, (i + 1) * width)
 
         offs_sb = sbuf("offs_sb", [P, S // GROUP], U16)
         k1_sb = sbuf("k1_sb", [P, S // GROUP], U16)
@@ -98,168 +99,234 @@ def tile_picked_fisher8_none_po_kernel(
         nc.vector.memset(w1_plane[:].bitcast(I32), 0)
         nc.gpsimd.memset(w23_plane[:].bitcast(I32), 0)
 
-        mu_rows = mu.rearrange("(p t) u -> p t u", t=SLOTS)
-        rs_rows = rs.rearrange("(p t) u -> p t u", t=SLOTS)
+        def load_table(tiles, table, t):
+            nc.sync.dma_start(out=tiles[t][:], in_=table.rearrange("(p t) u -> p t u", t=SLOTS)[:, t, :])
+
+        def load_words(raw, words):
+            nc.sync.dma_start(out=raw[:], in_=word_rows(words))
+
         nc.sync.dma_start(k1_sb[:], k1)
-        nc.sync.dma_start(out=mu_sb[0][:], in_=mu_rows[:, 0, :])
+        load_table(mu_sb, mu, 0)
         nc.sync.dma_start(offs_sb[:], offs)
         load_plane(nc, x_plane, 0, x_scales)
-        nc.sync.dma_start(out=x_sb[:], in_=word_rows(x_words))
-        nc.sync.dma_start(out=w1_raw[:], in_=word_rows(w1_words))
+        load_words(x_sb, x_words)
         load_plane(nc, w1_plane, 0, w1_scales)
-        for t in range(SLOTS):
-            if t + 1 < SLOTS:
-                nc.sync.dma_start(out=mu_sb[t + 1][:], in_=mu_rows[:, t + 1, :])
-            nc.sync.dma_start(out=rs_sb[t][:], in_=rs_rows[:, t, :])
-            if t == 0:
-                nc.sync.dma_start(out=g1_sb[:], in_=g1.rearrange("(p t) o -> p (t o)", t=SLOTS))
-                nc.sync.dma_start(out=g2_sb[:], in_=g2.rearrange("(p t) o -> p (t o)", t=SLOTS))
+        load_words(w1_raw, w1_words)
+        load_table(rs_sb, rs, 0)
+        load_table(mu_sb, mu, 1)
+        nc.sync.dma_start(out=g1_sb[:], in_=g1.rearrange("(p t) o -> p (t o)", t=SLOTS))
+        nc.sync.dma_start(out=g2_sb[:], in_=g2.rearrange("(p t) o -> p (t o)", t=SLOTS))
+        load_table(mu_sb, mu, 2)
+        load_table(rs_sb, rs, 1)
         load_plane(nc, w23_plane, 0, w2_scales)
+        load_table(mu_sb, mu, 3)
+        load_table(rs_sb, rs, 2)
+        load_words(w3_raw, w3_words)
         load_plane(nc, w23_plane, SCALE_ROWS, w3_scales)
-        nc.sync.dma_start(out=w2_raw[:], in_=word_rows(w2_words))
-        nc.sync.dma_start(out=w3_raw[:], in_=word_rows(w3_words))
+        load_table(rs_sb, rs, 3)
+        load_words(w2_raw, w2_words)
 
         mu0_picked = sbuf("mu0_picked", [P, S], F32)
-        for c in range(CHUNKS):
-            nc.vector.tensor_copy(out=mu0_picked[:, columns(c)], in_=mu_sb[0][:].indirect(entries(k1_sb, c)))
+        for c in range(2):
+            on_vector(out=mu0_picked[:, part(c, CHUNK)], in_=mu_sb[0][:].indirect(entries(k1_sb, c * CHUNK, CHUNK)))
         picked_plane = sbuf("picked_plane", [P, S], U8)
-        nc.vector.tensor_copy(out=picked_plane[:], in_=x_plane[:].indirect(offs_sb[:]))
+        on_vector(out=picked_plane[:], in_=x_plane[:].indirect(offs_sb[:]))
+
+        def pick(c, tag=None):
+            picked = sbuf("picked%d" % c, [P, CHUNK], U32, tag)
+            on_vector(out=picked[:], in_=x_sb[:].bitcast(U32).indirect(entries(offs_sb, c * CHUNK, CHUNK)))
+            return picked
+
         w1_codes = sbuf("w1_codes", [P, H], I32)
         w1_dealt_plane = sbuf("w1_dealt_plane", [P, H], U8)
-        deal_columns(nc, w1_codes, w1_raw, 4)
+        picked = [pick(0)]
         deal_columns(nc, w1_dealt_plane, w1_plane, 1)
+        deal_columns(nc, w1_codes, w1_raw, 4)
+        picked.append(pick(1, "w1_raw"))
 
         y = {}
 
-        def first_product(c):
-            picked = sbuf("picked%d" % c, [P, CHUNK], U32, "w1_plane" if c else None)
-            nc.vector.tensor_copy(out=picked[:], in_=x_sb[:].bitcast(U32).indirect(entries(offs_sb, c)))
-            for slots in ((0,), (1,), (2, 3)):
-                shape = [P, len(slots), CHUNK]
-                acc = bank(c, slots[0], "y%d_%d" % (c, slots[0]), shape)
-                held = sbuf("y_sb%d_%d" % (c, slots[0]), shape, F32) if slots[0] else acc
-                for j, t in enumerate(slots):
-                    nc.tensor.matmul_mx(
-                        out=acc[:, j, :],
-                        lhsT=w1_codes[:, places(t)].bitcast(FP8X4),
-                        lhsT_scale=w1_dealt_plane[:, places(t)],
-                        rhs=picked[:].bitcast(FP8X4),
-                        rhs_scale=picked_plane[:, columns(c)],
-                        start=True,
-                        stop=True,
-                    )
-                    y[c, t] = held[:, j, :]
-                if slots[0]:
-                    nc.scalar.copy(out=held[:], in_=acc[:])
+        def first_product(c, slots, b):
+            shape = [P, len(slots), CHUNK]
+            acc = bank(b, "y%d_%d" % (c, slots[0]), shape)
+            held = sbuf("y_sb%d_%d" % (c, slots[0]), shape, F32) if slots[0] else acc
+            for j, t in enumerate(slots):
+                nc.tensor.matmul_mx(
+                    out=acc[:, j, :],
+                    lhsT=w1_codes[:, part(t, P)].bitcast(FP8X4),
+                    lhsT_scale=w1_dealt_plane[:, part(t, P)],
+                    rhs=picked[c][:].bitcast(FP8X4),
+                    rhs_scale=picked_plane[:, part(c, CHUNK)],
+                    start=True,
+                    stop=True,
+                )
+                y[c, t] = held[:, j, :]
+            if slots[0]:
+                on_scalar(out=held[:], in_=acc[:])
 
-        for c in range(CHUNKS):
-            first_product(c)
+        for b, (c, slots) in enumerate(((0, (0,)), (0, (1,)), (0, (2,)), (0, (3,)), (1, (0,)), (1, (1,)), (1, (2, 3)))):
+            first_product(c, slots, b)
 
         neg_g1 = sbuf("neg_g1", [P, SLOTS], F32)
         neg_g2 = sbuf("neg_g2", [P, SLOTS], F32)
-        nc.gpsimd.tensor_scalar(neg_g1[:], g1_sb[:], -1.0, 0.0, ALU.mult, ALU.add)
-        nc.gpsimd.tensor_scalar(neg_g2[:], g2_sb[:], -1.0, 0.0, ALU.mult, ALU.add)
+        nc.scalar.activation(out=neg_g1[:], in_=g1_sb[:], func=ACT.Copy, scale=-1.0)
+        nc.scalar.activation(out=neg_g2[:], in_=g2_sb[:], func=ACT.Copy, scale=-1.0)
 
-        def two_orders(c):
-            z = sbuf("z_planar%d" % c, [P, SLOTS, CHUNK], BF16)
-            z2 = sbuf("z2_planar%d" % c, [P, SLOTS, CHUNK], BF16)
-            gap = sbuf("gap%d" % c, [P, SLOTS, CHUNK], F32, "gap")
+        def subtract(gap, c, t, lo=0, width=CHUNK):
+            means = mu_sb[t][:].indirect(entries(k1_sb, c * CHUNK + lo, width)) if t else mu0_picked[:, part(c, CHUNK)]
+            nc.vector.tensor_tensor(gap, means, y[c, t][:, lo : lo + width], ALU.subtract)
 
-            def subtract(t):
-                means = mu_sb[t][:].indirect(entries(k1_sb, c)) if t else mu0_picked[:, columns(c)]
-                nc.vector.tensor_tensor(gap[:, t, :], means, y[c, t], ALU.subtract)
+        def whiten(neg_d, gap, c, t, lo=0, width=CHUNK):
+            nc.vector.tensor_tensor(neg_d, rs_sb[t][:].indirect(entries(k1_sb, c * CHUNK + lo, width)), gap, ALU.mult)
 
-            groups = [(0, 1), (2,), (3,)] if c == LAST else [(0, 1), (2, 3)]
-            subtract(0)
-            for slots in groups:
-                shape = [P, len(slots), CHUNK]
-                neg_d = sbuf("neg_d%d_%d" % (c, slots[0]), shape, F32)
-                square = sbuf("square%d_%d" % (c, slots[0]), shape, F32)
-                for j, t in enumerate(slots):
-                    if t + 1 < SLOTS:
-                        subtract(t + 1)
-                    nc.vector.tensor_tensor(
-                        neg_d[:, j, :], rs_sb[t][:].indirect(entries(k1_sb, c)), gap[:, t, :], ALU.mult
-                    )
-                    if (c, t) == (LAST, SLOTS - 1):
-                        nc.vector.tensor_scalar(z[:, t, :], neg_d[:, j, :], neg_g1[:, t : t + 1], None, ALU.mult)
-                    else:
-                        nc.scalar.activation(
-                            out=z[:, t, :], in_=neg_d[:, j, :], func=ACT.Copy, scale=neg_g1[:, t : t + 1]
-                        )
-                nc.scalar.activation(out=square[:], in_=neg_d[:], func=ACT.Square)
-                for j, t in enumerate(slots):
-                    nc.scalar.activation(
-                        out=z2[:, t, :], in_=square[:, j, :], func=ACT.Identity,
-                        scale=g2_sb[:, t : t + 1], bias=neg_g2[:, t : t + 1],
-                    )
-            return z, z2
+        def square(out, neg_d):
+            nc.scalar.activation(out=out, in_=neg_d, func=ACT.Square)
 
-        def weave_orders(c, orders, copy):
-            woven = []
-            for j, planar in enumerate(orders):
-                woven.append(sbuf("woven%d_%d" % (c, j), [P, CHUNK * SLOTS], BF16))
-                weave(copy, woven[j], planar)
-            return woven
+        def first_order(z, neg_d, t):
+            nc.scalar.activation(out=z[:, t, :], in_=neg_d, func=ACT.Copy, scale=neg_g1[:, t : t + 1])
 
-        def quantise_orders(c, woven):
-            quantised = []
-            for j, values in enumerate(woven):
-                codes = sbuf("z_codes%d_%d" % (c, j), [P, CHUNK], U32)
-                plane = sbuf("z_plane%d_%d" % (c, j), [P, CHUNK], U8)
-                nc.vector.quantize_mx(out=codes[:].bitcast(FP8X4), scales=plane[:], in_=values[:])
-                quantised.append((codes, plane))
-            return quantised
+        def first_order_on_vector(z, neg_d, t):
+            nc.vector.tensor_scalar(z[:, t, :], neg_d, neg_g1[:, t : t + 1], None, ALU.mult)
 
-        woven_first = weave_orders(0, two_orders(0), nc.scalar.copy)
-        w2_codes = sbuf("w2_codes", [P, N], I32)
-        w3_codes = sbuf("w3_codes", [P, N], I32)
-        w23_dealt_plane = sbuf("w23_dealt_plane", [P, N], U8)
-        deal_columns(nc, w2_codes, w2_raw, 4)
-        deal_columns(nc, w3_codes, w3_raw, 4)
-        deal_columns(nc, w23_dealt_plane, w23_plane, 1)
-        quantised_first = quantise_orders(0, woven_first)
-        orders_last = two_orders(LAST)
+        def second_order(z2, squared, t):
+            nc.scalar.activation(
+                out=z2[:, t, :], in_=squared, func=ACT.Identity, scale=g2_sb[:, t : t + 1], bias=neg_g2[:, t : t + 1]
+            )
+
+        def quantise(codes, plane, woven):
+            nc.vector.quantize_mx(out=codes.bitcast(FP8X4), scales=plane, in_=woven)
 
         out_codes = sbuf("out_codes", [P, S], U32)
         out_plane = sbuf("out_plane", [P, S], U8)
         out_rows = out_0.rearrange("(p t) n -> p t n", t=SLOTS)
         out_words = word_rows(out_1)
 
-        def second_product(c, quantised):
-            accs = [bank(c, t, "out%d_%d" % (c, t), [P, CHUNK]) for t in range(SLOTS)]
-            for j, w_codes in enumerate((w2_codes, w3_codes)):
-                codes, plane = quantised[j]
-                for t in range(SLOTS):
-                    nc.tensor.matmul_mx(
-                        out=accs[t][:],
-                        lhsT=w_codes[:, places(t)].bitcast(FP8X4),
-                        lhsT_scale=w23_dealt_plane[SCALE_ROWS * j : P, places(t)],
-                        rhs=codes[:].bitcast(FP8X4),
-                        rhs_scale=plane[:],
-                        start=(j == 0),
-                        stop=(j == 1),
-                    )
-            result = sbuf("result%d" % c, [P, SLOTS, CHUNK], F32)
+        def passes(acc, u, j, codes, plane):
             for t in range(SLOTS):
-                copy = nc.vector.tensor_copy if (c, t) == (LAST, VECTOR_SLOT) else nc.scalar.copy
-                copy(out=result[:, t, :], in_=accs[t][:])
-                if t % 2 == 1:
-                    nc.sync.dma_start(out=out_rows[:, t - 1 : t + 1, columns(c)], in_=result[:, t - 1 : t + 1, :])
-            return result
+                nc.tensor.matmul_mx(
+                    out=acc[:, t, :],
+                    lhsT=w_codes[j][:, part(t, P)].bitcast(FP8X4),
+                    lhsT_scale=w23_dealt_plane[SCALE_ROWS * j : P, part(t, P)],
+                    rhs=codes[:, part(u % 2, UNIT)].bitcast(FP8X4),
+                    rhs_scale=plane[:, part(u % 2, UNIT)],
+                    start=(j == 0 and t == 0),
+                    stop=(j == 1 and t == SLOTS - 1),
+                )
 
-        def hand_on(c, result):
-            rounded = sbuf("rounded%d" % c, [P, CHUNK * SLOTS], BF16)
-            weave(nc.vector.tensor_copy, rounded, result)
-            nc.vector.quantize_mx(
-                out=out_codes[:, columns(c)].bitcast(FP8X4), scales=out_plane[:, columns(c)], in_=rounded[:]
-            )
-            nc.sync.dma_start(out=out_words[:, columns(c)], in_=out_codes[:, columns(c)].bitcast(I32))
+        def store_unit(copy, result, acc, u):
+            copy(out=result, in_=acc[:])
+            nc.sync.dma_start(out=out_rows[:, :, part(u, UNIT)], in_=result)
 
-        quantised_last = quantise_orders(LAST, weave_orders(LAST, orders_last, nc.vector.tensor_copy))
-        results = [second_product(c, quantised) for c, quantised in enumerate((quantised_first, quantised_last))]
-        for c, result in enumerate(results):
-            hand_on(c, result)
+        def hand_on(c, rounded):
+            quantise(out_codes[:, part(c, CHUNK)], out_plane[:, part(c, CHUNK)], rounded[:])
+            nc.sync.dma_start(out=out_words[:, part(c, CHUNK)], in_=out_codes[:, part(c, CHUNK)].bitcast(I32))
+
+        planar = [P, SLOTS, CHUNK]
+        row = [P, CHUNK]
+
+        z_first = at(4 * KB, "z_first", planar, BF16)
+        z2_first = sbuf("z2_first", planar, BF16)
+        gaps = [sbuf("gap0_%d" % t, row, F32)[:] for t in range(SLOTS - 1)]
+        last_gaps = [sbuf("gap0_3_%d" % i, [P, UNIT], F32)[:] for i in range(2)]
+        neg_d = [sbuf("neg_d0_%d" % t, row, F32)[:] for t in range(SLOTS)]
+        squares = [sbuf("square0_%d" % t, row, F32)[:] for t in range(SLOTS - 1)]
+        squares.append(at(24 * KB, "square0_3", row, F32)[:])
+
+        def orders_first(t):
+            square(squares[t], neg_d[t])
+            first_order(z_first, neg_d[t], t)
+            second_order(z2_first, squares[t], t)
+
+        subtract(gaps[0], 0, 0)
+        whiten(neg_d[0], gaps[0], 0, 0)
+        subtract(gaps[1], 0, 1)
+        orders_first(0)
+        subtract(gaps[2], 0, 2)
+        whiten(neg_d[1], gaps[1], 0, 1)
+        orders_first(1)
+        for i in range(2):
+            subtract(last_gaps[i], 0, 3, i * UNIT, UNIT)
+        whiten(neg_d[2], gaps[2], 0, 2)
+        orders_first(2)
+        for i in range(2):
+            whiten(neg_d[3][:, part(i, UNIT)], last_gaps[i], 0, 3, i * UNIT, UNIT)
+        orders_first(3)
+
+        woven = {(c, j): sbuf("woven%d_%d" % (c, j), [P, SLOTS * CHUNK], BF16) for c in range(2) for j in range(2)}
+        codes = {(c, j): sbuf("codes%d_%d" % (c, j), row, U32) for c in range(2) for j in range(2)}
+        planes = {(c, j): sbuf("plane%d_%d" % (c, j), row, U8) for c, j in ((0, 0), (0, 1), (1, 1))}
+        weave(on_scalar, woven[0, 0][:], z_first[:])
+        weave(on_scalar, woven[0, 1][:], z2_first[:])
+
+        work = sbuf("work", [P, 2 * SLOTS - 1, CHUNK], F32, "gap0_3_0")
+        neg_d = [work[:, t, :] for t in range(SLOTS - 1)]
+        gaps = [work[:, SLOTS - 1 + t, :] for t in range(SLOTS)]
+        subtract(gaps[0], 1, 0)
+        for t in range(SLOTS - 1):
+            subtract(gaps[t + 1], 1, t + 1)
+            whiten(neg_d[t], gaps[t], 1, t)
+
+        w23_dealt_plane = at(24 * KB + 256, "w23_dealt_plane", [P, N], U8)
+        w_codes = [at(22 * KB + 256, "w2_codes", [P, N], I32), sbuf("w3_codes", [P, N], I32, "neg_d0_3")]
+        deal_columns(nc, w23_dealt_plane, w23_plane, 1)
+        deal_columns(nc, w_codes[1], w3_raw, 4)
+        deal_columns(nc, w_codes[0], w2_raw, 4)
+        quantise(codes[0, 0][:], planes[0, 0][:], woven[0, 0][:])
+        neg_d.append(at(4 * KB + 256, "neg_d1_3", row, F32)[:])
+        whiten(neg_d[3], gaps[3], 1, 3)
+        quantise(codes[0, 1][:], planes[0, 1][:], woven[0, 1][:])
+        accs = [bank(u, "out%d" % u, [P, SLOTS, UNIT]) for u in range(2)]
+        for j in range(2):
+            for u in range(2):
+                passes(accs[u], u, j, codes[0, j], planes[0, j])
+
+        z_last = at(2 * KB + 256, "z_last", planar, BF16)
+        z2_last = sbuf("z2_last", planar, BF16)
+        squares = at(6 * KB - 256, "squares1", [P, SLOTS - 1, CHUNK], F32)
+        last_square = at(14 * KB, "square1_3", row, F32)
+        square(squares[:, 0:2, :], work[:, 0:2, :])
+        for t in range(2):
+            first_order(z_last, neg_d[t], t)
+        square(squares[:, 2, :], neg_d[2])
+        for t in range(2):
+            second_order(z2_last, squares[:, t, :], t)
+        square(last_square[:], neg_d[3])
+        second_order(z2_last, squares[:, 2, :], 2)
+        second_order(z2_last, last_square[:], 3)
+        for t in range(2, SLOTS):
+            first_order_on_vector(z_last, neg_d[t], t)
+
+        planes[1, 0] = at(14 * KB + 256, "plane1_0", row, U8)
+        accs = accs + [bank(u, "out%d" % u, [P, SLOTS, UNIT]) for u in range(2, 4)]
+        weave(on_vector, woven[1, 0][:], z_last[:])
+        weave(on_vector, woven[1, 1][:, part(0, SLOTS * UNIT)], z2_last[:, :, part(0, UNIT)])
+        quantise(codes[1, 0][:], planes[1, 0][:], woven[1, 0][:])
+        for u in range(2, 4):
+            passes(accs[u], u, 0, codes[1, 0], planes[1, 0])
+        weave(on_vector, woven[1, 1][:, part(1, SLOTS * UNIT)], z2_last[:, :, part(1, UNIT)])
+        for i in range(2):
+            quantise(codes[1, 1][:, part(i, UNIT)], planes[1, 1][:, part(i, UNIT)], woven[1, 1][:, part(i, SLOTS * UNIT)])
+        for u in range(2, 4):
+            passes(accs[u], u, 1, codes[1, 1], planes[1, 1])
+
+        first_results = at(10 * KB + 256, "first_results", [P, 2, SLOTS, UNIT], F32)
+        rounded = [at(15 * KB - 256, "rounded0", [P, SLOTS * CHUNK], BF16), sbuf("rounded1", [P, SLOTS * CHUNK], BF16)]
+        results = [first_results[:, u, :, :] for u in range(2)]
+        results = results + [sbuf("result%d" % u, [P, SLOTS, UNIT], F32)[:] for u in range(2, 4)]
+
+        def round_unit(copy, u, source):
+            weave(copy, rounded[u // 2][:, part(u % 2, SLOTS * UNIT)], source)
+
+        store_unit(on_scalar, results[0], accs[0], 0)
+        store_unit(on_scalar, results[1], accs[1], 1)
+        round_unit(on_scalar, 0, accs[0][:])
+        round_unit(on_vector, 1, results[1])
+        store_unit(on_scalar, results[2], accs[2], 2)
+        hand_on(0, rounded[0])
+        round_unit(on_vector, 3, accs[3][:])
+        round_unit(on_scalar, 2, accs[2][:])
+        store_unit(on_vector, results[3], accs[3], 3)
+        hand_on(1, rounded[1])
 
         for q in range(P // QUADRANT):
             queue = nc.scalar if q % 2 else nc.sync

@@ -105,6 +105,15 @@ def tile_picked_fisher8_none_po_kernel(
         def load_words(raw, words):
             nc.sync.dma_start(out=raw[:], in_=word_rows(words))
 
+        def load_scale_row(i):
+            first, scales, r = SCALE_ROWS * (i // SCALE_ROWS), (w2_scales, w3_scales)[i // SCALE_ROWS], i % SCALE_ROWS
+            nc.sync.dma_start(
+                out=w23_plane[first + r : P : QUADRANT, :].bitcast(I32),
+                in_=scales[0, r : SCALE_ROWS * (P // QUADRANT) : SCALE_ROWS, :].bitcast(I32),
+            )
+
+        nc.gpsimd.dma_start(out=g1_sb[:], in_=g1.rearrange("(p t) o -> p (t o)", t=SLOTS))
+        nc.gpsimd.dma_start(out=g2_sb[:], in_=g2.rearrange("(p t) o -> p (t o)", t=SLOTS))
         nc.sync.dma_start(k1_sb[:], k1)
         load_table(mu_sb, mu, 0)
         nc.sync.dma_start(offs_sb[:], offs)
@@ -114,16 +123,20 @@ def tile_picked_fisher8_none_po_kernel(
         load_words(w1_raw, w1_words)
         load_table(rs_sb, rs, 0)
         load_table(mu_sb, mu, 1)
-        nc.sync.dma_start(out=g1_sb[:], in_=g1.rearrange("(p t) o -> p (t o)", t=SLOTS))
-        nc.sync.dma_start(out=g2_sb[:], in_=g2.rearrange("(p t) o -> p (t o)", t=SLOTS))
+        load_scale_row(0)
         load_table(mu_sb, mu, 2)
+        load_scale_row(1)
         load_table(rs_sb, rs, 1)
-        load_plane(nc, w23_plane, 0, w2_scales)
+        load_scale_row(2)
         load_table(mu_sb, mu, 3)
+        load_scale_row(3)
         load_table(rs_sb, rs, 2)
+        load_scale_row(4)
         load_words(w3_raw, w3_words)
-        load_plane(nc, w23_plane, SCALE_ROWS, w3_scales)
+        load_scale_row(5)
+        load_scale_row(6)
         load_table(rs_sb, rs, 3)
+        load_scale_row(7)
         load_words(w2_raw, w2_words)
 
         mu0_picked = sbuf("mu0_picked", [P, S], F32)
@@ -201,21 +214,21 @@ def tile_picked_fisher8_none_po_kernel(
         out_rows = out_0.rearrange("(p t) n -> p t n", t=SLOTS)
         out_words = word_rows(out_1)
 
-        def passes(acc, u, j, codes, plane):
+        def passes(accs, j, codes, plane):
+            per = SLOTS // len(accs)
             for t in range(SLOTS):
                 nc.tensor.matmul_mx(
-                    out=acc[:, t, :],
+                    out=accs[t // per][:, t % per, :],
                     lhsT=w_codes[j][:, part(t, P)].bitcast(FP8X4),
                     lhsT_scale=w23_dealt_plane[SCALE_ROWS * j : P, part(t, P)],
-                    rhs=codes[:, part(u % 2, UNIT)].bitcast(FP8X4),
-                    rhs_scale=plane[:, part(u % 2, UNIT)],
-                    start=(j == 0 and t == 0),
-                    stop=(j == 1 and t == SLOTS - 1),
+                    rhs=codes[:].bitcast(FP8X4),
+                    rhs_scale=plane[:],
+                    start=(j == 0 and t % per == 0),
+                    stop=(j == 1 and t % per == per - 1),
                 )
 
-        def store_unit(copy, result, acc, u):
-            copy(out=result, in_=acc[:])
-            nc.sync.dma_start(out=out_rows[:, :, part(u, UNIT)], in_=result)
+        def store(result, c, slots):
+            nc.sync.dma_start(out=out_rows[:, slots, part(c, CHUNK)], in_=result[:, slots, :])
 
         def hand_on(c, rounded):
             quantise(out_codes[:, part(c, CHUNK)], out_plane[:, part(c, CHUNK)], rounded[:])
@@ -275,10 +288,9 @@ def tile_picked_fisher8_none_po_kernel(
         neg_d.append(at(4 * KB + 256, "neg_d1_3", row, F32)[:])
         whiten(neg_d[3], gaps[3], 1, 3)
         quantise(codes[0, 1][:], planes[0, 1][:], woven[0, 1][:])
-        accs = [bank(u, "out%d" % u, [P, SLOTS, UNIT]) for u in range(2)]
+        first_accs = [bank(b, "out0_%d" % b, [P, 2, CHUNK]) for b in range(2)]
         for j in range(2):
-            for u in range(2):
-                passes(accs[u], u, j, codes[0, j], planes[0, j])
+            passes(first_accs, j, codes[0, j], planes[0, j])
 
         z_last = at(2 * KB + 256, "z_last", planar, BF16)
         z2_last = sbuf("z2_last", planar, BF16)
@@ -297,35 +309,31 @@ def tile_picked_fisher8_none_po_kernel(
             first_order_on_vector(z_last, neg_d[t], t)
 
         planes[1, 0] = at(14 * KB + 256, "plane1_0", row, U8)
-        accs = accs + [bank(u, "out%d" % u, [P, SLOTS, UNIT]) for u in range(2, 4)]
+        last_accs = [bank(2 + t, "out1_%d" % t, [P, 1, CHUNK]) for t in range(SLOTS)]
         weave(on_vector, woven[1, 0][:], z_last[:])
-        weave(on_vector, woven[1, 1][:, part(0, SLOTS * UNIT)], z2_last[:, :, part(0, UNIT)])
-        quantise(codes[1, 0][:], planes[1, 0][:], woven[1, 0][:])
-        for u in range(2, 4):
-            passes(accs[u], u, 0, codes[1, 0], planes[1, 0])
-        weave(on_vector, woven[1, 1][:, part(1, SLOTS * UNIT)], z2_last[:, :, part(1, UNIT)])
-        for i in range(2):
-            quantise(codes[1, 1][:, part(i, UNIT)], planes[1, 1][:, part(i, UNIT)], woven[1, 1][:, part(i, SLOTS * UNIT)])
-        for u in range(2, 4):
-            passes(accs[u], u, 1, codes[1, 1], planes[1, 1])
+        weave(on_vector, woven[1, 1][:], z2_last[:])
+        for j in range(2):
+            quantise(codes[1, j][:], planes[1, j][:], woven[1, j][:])
+            passes(last_accs, j, codes[1, j], planes[1, j])
 
-        first_results = at(10 * KB + 256, "first_results", [P, 2, SLOTS, UNIT], F32)
+        results = [at(10 * KB + 256, "result0", planar, F32), sbuf("result1", planar, F32)]
         rounded = [at(15 * KB - 256, "rounded0", [P, SLOTS * CHUNK], BF16), sbuf("rounded1", [P, SLOTS * CHUNK], BF16)]
-        results = [first_results[:, u, :, :] for u in range(2)]
-        results = results + [sbuf("result%d" % u, [P, SLOTS, UNIT], F32)[:] for u in range(2, 4)]
 
-        def round_unit(copy, u, source):
-            weave(copy, rounded[u // 2][:, part(u % 2, SLOTS * UNIT)], source)
+        def round_columns(copy, c, lo, hi):
+            weave(copy, rounded[c][:, SLOTS * lo : SLOTS * hi], results[c][:, :, lo:hi])
 
-        store_unit(on_scalar, results[0], accs[0], 0)
-        store_unit(on_scalar, results[1], accs[1], 1)
-        round_unit(on_scalar, 0, accs[0][:])
-        round_unit(on_vector, 1, results[1])
-        store_unit(on_scalar, results[2], accs[2], 2)
+        for b in range(2):
+            on_scalar(out=results[0][:, part(b, 2), :], in_=first_accs[b][:])
+            store(results[0], 0, part(b, 2))
+        round_columns(on_scalar, 0, 0, 64)
+        round_columns(on_vector, 0, 64, CHUNK)
         hand_on(0, rounded[0])
-        round_unit(on_vector, 3, accs[3][:])
-        round_unit(on_scalar, 2, accs[2][:])
-        store_unit(on_vector, results[3], accs[3], 3)
+        for t in range(SLOTS):
+            (on_vector if t % 2 else on_scalar)(out=results[1][:, t : t + 1, :], in_=last_accs[t][:])
+            if t % 2:
+                store(results[1], 1, part(t // 2, 2))
+        round_columns(on_vector, 1, 0, 176)
+        round_columns(on_scalar, 1, 176, CHUNK)
         hand_on(1, rounded[1])
 
         for q in range(P // QUADRANT):

@@ -21,21 +21,36 @@ QUADRANT = 32
 SCALE_ROWS = 4
 GROUP = 16
 LINE = 16
+WEAVE_RUN = 4
 CHUNK = 256
-UNIT = 128
+HALF = CHUNK // 2
+SCALAR_ROUNDS_FIRST = 64
+VECTOR_ROUNDS_LAST = 176
+
 KB = 1024
+OVERLAP = 256
+Z_FIRST_AT = 4 * KB
+Z_LAST_AT = Z_FIRST_AT - 2 * KB + OVERLAP
+LAST_NEG_D_AT = Z_FIRST_AT + OVERLAP
+SQUARES_AT = Z_FIRST_AT + 2 * KB - OVERLAP
+LAST_SQUARE_AT = 14 * KB
+FIRST_RESULT_AT = LAST_SQUARE_AT - 4 * KB + OVERLAP
+LAST_Z_PLANE_AT = LAST_SQUARE_AT + OVERLAP
+FIRST_ROUNDED_AT = LAST_SQUARE_AT + KB - OVERLAP
+FIRST_SQUARE_AT = 24 * KB
+W2_CODES_AT = FIRST_SQUARE_AT - 2 * KB + OVERLAP
+W23_PLANE_AT = FIRST_SQUARE_AT + OVERLAP
 
 
 def word_rows(words):
     return words[0].rearrange("p c r -> p (c r)").bitcast(I32)
 
 
-def load_plane(nc, plane, first, scales):
-    for r in range(SCALE_ROWS):
-        nc.sync.dma_start(
-            out=plane[first + r : P : QUADRANT, :].bitcast(I32),
-            in_=scales[0, r : SCALE_ROWS * (P // QUADRANT) : SCALE_ROWS, :].bitcast(I32),
-        )
+def load_scale_row(nc, plane, first, scales, r):
+    nc.sync.dma_start(
+        out=plane[first + r : P : QUADRANT, :].bitcast(I32),
+        in_=scales[0, r : SCALE_ROWS * (P // QUADRANT) : SCALE_ROWS, :].bitcast(I32),
+    )
 
 
 def deal_columns(nc, dealt, raw, element_bytes):
@@ -48,8 +63,15 @@ def deal_columns(nc, dealt, raw, element_bytes):
 
 def weave(copy, woven, planar):
     copy(
-        out=woven.rearrange("p (c i t) -> p c t i", t=SLOTS, i=4),
-        in_=planar.rearrange("p t (c i) -> p c t i", i=4),
+        out=woven.rearrange("p (c i t) -> p c t i", t=SLOTS, i=WEAVE_RUN),
+        in_=planar.rearrange("p t (c i) -> p c t i", i=WEAVE_RUN),
+    )
+
+
+def weave_pairs(copy, dtype, woven, paired):
+    copy(
+        out=woven.bitcast(dtype).rearrange("p (c i u) -> p c u i", u=2, i=2),
+        in_=paired.rearrange("p u c e -> p u (c e)").bitcast(dtype).rearrange("p u (c i) -> p c u i", i=2),
     )
 
 
@@ -105,38 +127,31 @@ def tile_picked_fisher8_none_po_kernel(
         def load_words(raw, words):
             nc.sync.dma_start(out=raw[:], in_=word_rows(words))
 
-        def load_scale_row(i):
-            first, scales, r = SCALE_ROWS * (i // SCALE_ROWS), (w2_scales, w3_scales)[i // SCALE_ROWS], i % SCALE_ROWS
-            nc.sync.dma_start(
-                out=w23_plane[first + r : P : QUADRANT, :].bitcast(I32),
-                in_=scales[0, r : SCALE_ROWS * (P // QUADRANT) : SCALE_ROWS, :].bitcast(I32),
-            )
+        def load_w23_row(i):
+            j, r = divmod(i, SCALE_ROWS)
+            load_scale_row(nc, w23_plane, SCALE_ROWS * j, (w2_scales, w3_scales)[j], r)
 
         nc.gpsimd.dma_start(out=g1_sb[:], in_=g1.rearrange("(p t) o -> p (t o)", t=SLOTS))
         nc.gpsimd.dma_start(out=g2_sb[:], in_=g2.rearrange("(p t) o -> p (t o)", t=SLOTS))
         nc.sync.dma_start(k1_sb[:], k1)
         load_table(mu_sb, mu, 0)
         nc.sync.dma_start(offs_sb[:], offs)
-        load_plane(nc, x_plane, 0, x_scales)
+        for r in range(SCALE_ROWS):
+            load_scale_row(nc, x_plane, 0, x_scales, r)
         load_words(x_sb, x_words)
-        load_plane(nc, w1_plane, 0, w1_scales)
+        for r in range(SCALE_ROWS):
+            load_scale_row(nc, w1_plane, 0, w1_scales, r)
         load_words(w1_raw, w1_words)
         load_table(rs_sb, rs, 0)
-        load_table(mu_sb, mu, 1)
-        load_scale_row(0)
-        load_table(mu_sb, mu, 2)
-        load_scale_row(1)
-        load_table(rs_sb, rs, 1)
-        load_scale_row(2)
-        load_table(mu_sb, mu, 3)
-        load_scale_row(3)
-        load_table(rs_sb, rs, 2)
-        load_scale_row(4)
+        early_tables = ((mu_sb, mu, 1), (mu_sb, mu, 2), (rs_sb, rs, 1), (mu_sb, mu, 3), (rs_sb, rs, 2))
+        for i, (tiles, table, t) in enumerate(early_tables):
+            load_table(tiles, table, t)
+            load_w23_row(i)
         load_words(w3_raw, w3_words)
-        load_scale_row(5)
-        load_scale_row(6)
-        load_table(rs_sb, rs, 3)
-        load_scale_row(7)
+        for i in range(len(early_tables), 2 * SCALE_ROWS - 1):
+            load_w23_row(i)
+        load_table(rs_sb, rs, SLOTS - 1)
+        load_w23_row(2 * SCALE_ROWS - 1)
         load_words(w2_raw, w2_words)
 
         mu0_picked = sbuf("mu0_picked", [P, S], F32)
@@ -177,7 +192,8 @@ def tile_picked_fisher8_none_po_kernel(
             if slots[0]:
                 on_scalar(out=held[:], in_=acc[:])
 
-        for b, (c, slots) in enumerate(((0, (0,)), (0, (1,)), (0, (2,)), (0, (3,)), (1, (0,)), (1, (1,)), (1, (2, 3)))):
+        groups = [(0, (t,)) for t in range(SLOTS)] + [(1, (0,)), (1, (1,)), (1, (2, 3))]
+        for b, (c, slots) in enumerate(groups):
             first_product(c, slots, b)
 
         neg_g1 = sbuf("neg_g1", [P, SLOTS], F32)
@@ -196,14 +212,19 @@ def tile_picked_fisher8_none_po_kernel(
             nc.scalar.activation(out=out, in_=neg_d, func=ACT.Square)
 
         def first_order(z, neg_d, t):
-            nc.scalar.activation(out=z[:, t, :], in_=neg_d, func=ACT.Copy, scale=neg_g1[:, t : t + 1])
+            nc.scalar.activation(out=z[:, t // 2, :, t % 2], in_=neg_d, func=ACT.Copy, scale=neg_g1[:, t : t + 1])
 
         def first_order_on_vector(z, neg_d, t):
-            nc.vector.tensor_scalar(z[:, t, :], neg_d, neg_g1[:, t : t + 1], None, ALU.mult)
+            nc.vector.tensor_scalar(z[:, t // 2, :, t % 2], neg_d, neg_g1[:, t : t + 1], None, ALU.mult)
 
         def second_order(z2, squared, t):
             nc.scalar.activation(
-                out=z2[:, t, :], in_=squared, func=ACT.Identity, scale=g2_sb[:, t : t + 1], bias=neg_g2[:, t : t + 1]
+                out=z2[:, t // 2, :, t % 2], in_=squared, func=ACT.Identity, scale=g2_sb[:, t : t + 1], bias=neg_g2[:, t : t + 1]
+            )
+
+        def second_order_on_vector(z2, squared, t):
+            nc.vector.tensor_scalar(
+                z2[:, t // 2, :, t % 2], squared, g2_sb[:, t : t + 1], neg_g2[:, t : t + 1], ALU.mult, ALU.add
             )
 
         def quantise(codes, plane, woven):
@@ -230,20 +251,20 @@ def tile_picked_fisher8_none_po_kernel(
         def store(result, c, slots):
             nc.sync.dma_start(out=out_rows[:, slots, part(c, CHUNK)], in_=result[:, slots, :])
 
-        def hand_on(c, rounded):
-            quantise(out_codes[:, part(c, CHUNK)], out_plane[:, part(c, CHUNK)], rounded[:])
+        def store_words(c):
             nc.sync.dma_start(out=out_words[:, part(c, CHUNK)], in_=out_codes[:, part(c, CHUNK)].bitcast(I32))
 
         planar = [P, SLOTS, CHUNK]
+        paired = [P, 2, CHUNK, 2]
         row = [P, CHUNK]
 
-        z_first = at(4 * KB, "z_first", planar, BF16)
-        z2_first = sbuf("z2_first", planar, BF16)
+        z_first = at(Z_FIRST_AT, "z_first", paired, BF16)
+        z2_first = sbuf("z2_first", paired, BF16)
         gaps = [sbuf("gap0_%d" % t, row, F32)[:] for t in range(SLOTS - 1)]
-        last_gaps = [sbuf("gap0_3_%d" % i, [P, UNIT], F32)[:] for i in range(2)]
+        last_gaps = [sbuf("gap0_3_%d" % i, [P, HALF], F32)[:] for i in range(2)]
         neg_d = [sbuf("neg_d0_%d" % t, row, F32)[:] for t in range(SLOTS)]
         squares = [sbuf("square0_%d" % t, row, F32)[:] for t in range(SLOTS - 1)]
-        squares.append(at(24 * KB, "square0_3", row, F32)[:])
+        squares.append(at(FIRST_SQUARE_AT, "square0_3", row, F32)[:])
 
         def orders_first(t):
             square(squares[t], neg_d[t])
@@ -258,83 +279,87 @@ def tile_picked_fisher8_none_po_kernel(
         whiten(neg_d[1], gaps[1], 0, 1)
         orders_first(1)
         for i in range(2):
-            subtract(last_gaps[i], 0, 3, i * UNIT, UNIT)
+            subtract(last_gaps[i], 0, 3, i * HALF, HALF)
         whiten(neg_d[2], gaps[2], 0, 2)
         orders_first(2)
         for i in range(2):
-            whiten(neg_d[3][:, part(i, UNIT)], last_gaps[i], 0, 3, i * UNIT, UNIT)
+            whiten(neg_d[3][:, part(i, HALF)], last_gaps[i], 0, 3, i * HALF, HALF)
         orders_first(3)
 
         woven = {(c, j): sbuf("woven%d_%d" % (c, j), [P, SLOTS * CHUNK], BF16) for c in range(2) for j in range(2)}
         codes = {(c, j): sbuf("codes%d_%d" % (c, j), row, U32) for c in range(2) for j in range(2)}
-        planes = {(c, j): sbuf("plane%d_%d" % (c, j), row, U8) for c, j in ((0, 0), (0, 1), (1, 1))}
-        weave(on_scalar, woven[0, 0][:], z_first[:])
-        weave(on_scalar, woven[0, 1][:], z2_first[:])
+        planes = {(c, j): sbuf("plane%d_%d" % (c, j), row, U8) for c in range(2) for j in range(2)}
+        weave_pairs(on_scalar, U32, woven[0, 0][:], z_first[:])
+        weave_pairs(on_scalar, U32, woven[0, 1][:], z2_first[:])
 
-        work = sbuf("work", [P, 2 * SLOTS - 1, CHUNK], F32, "gap0_3_0")
-        neg_d = [work[:, t, :] for t in range(SLOTS - 1)]
-        gaps = [work[:, SLOTS - 1 + t, :] for t in range(SLOTS)]
+        work = sbuf("work", [P, 2 + SLOTS, CHUNK], F32, "gap0_3_0")
+        neg_d = [work[:, t, :] for t in range(2)]
+        gaps = [work[:, 2 + t, :] for t in range(SLOTS)]
         subtract(gaps[0], 1, 0)
-        for t in range(SLOTS - 1):
+        for t in range(2):
             subtract(gaps[t + 1], 1, t + 1)
             whiten(neg_d[t], gaps[t], 1, t)
+        subtract(gaps[3], 1, 3)
 
-        w23_dealt_plane = at(24 * KB + 256, "w23_dealt_plane", [P, N], U8)
-        w_codes = [at(22 * KB + 256, "w2_codes", [P, N], I32), sbuf("w3_codes", [P, N], I32, "neg_d0_3")]
+        w23_dealt_plane = at(W23_PLANE_AT, "w23_dealt_plane", [P, N], U8)
+        w_codes = [at(W2_CODES_AT, "w2_codes", [P, N], I32), sbuf("w3_codes", [P, N], I32, "neg_d0_3")]
         deal_columns(nc, w23_dealt_plane, w23_plane, 1)
         deal_columns(nc, w_codes[1], w3_raw, 4)
         deal_columns(nc, w_codes[0], w2_raw, 4)
-        quantise(codes[0, 0][:], planes[0, 0][:], woven[0, 0][:])
-        neg_d.append(at(4 * KB + 256, "neg_d1_3", row, F32)[:])
-        whiten(neg_d[3], gaps[3], 1, 3)
-        quantise(codes[0, 1][:], planes[0, 1][:], woven[0, 1][:])
         first_accs = [bank(b, "out0_%d" % b, [P, 2, CHUNK]) for b in range(2)]
         for j in range(2):
+            quantise(codes[0, j][:], planes[0, j][:], woven[0, j][:])
             passes(first_accs, j, codes[0, j], planes[0, j])
+        late = sbuf("late", [P, 2, CHUNK], F32, "z2_first")
+        for t in range(2, SLOTS):
+            neg_d.append(late[:, t - 2, :])
+            whiten(neg_d[t], gaps[t], 1, t)
 
-        z_last = at(2 * KB + 256, "z_last", planar, BF16)
-        z2_last = sbuf("z2_last", planar, BF16)
-        squares = at(6 * KB - 256, "squares1", [P, SLOTS - 1, CHUNK], F32)
-        last_square = at(14 * KB, "square1_3", row, F32)
+        z_last = at(Z_LAST_AT, "z_last", paired, BF16)
+        z2_last = sbuf("z2_last", paired, BF16)
+        squares = at(SQUARES_AT, "squares1", planar, F32)
         square(squares[:, 0:2, :], work[:, 0:2, :])
         for t in range(2):
             first_order(z_last, neg_d[t], t)
-        square(squares[:, 2, :], neg_d[2])
         for t in range(2):
             second_order(z2_last, squares[:, t, :], t)
-        square(last_square[:], neg_d[3])
-        second_order(z2_last, squares[:, 2, :], 2)
-        second_order(z2_last, last_square[:], 3)
         for t in range(2, SLOTS):
-            first_order_on_vector(z_last, neg_d[t], t)
+            square(squares[:, t, :], neg_d[t])
+        first_order_on_vector(z_last, neg_d[2], 2)
+        second_order_on_vector(z2_last, squares[:, 2, :], 2)
+        first_order_on_vector(z_last, neg_d[3], 3)
+        second_order_on_vector(z2_last, squares[:, 3, :], 3)
 
-        planes[1, 0] = at(14 * KB + 256, "plane1_0", row, U8)
         last_accs = [bank(2 + t, "out1_%d" % t, [P, 1, CHUNK]) for t in range(SLOTS)]
-        weave(on_vector, woven[1, 0][:], z_last[:])
-        weave(on_vector, woven[1, 1][:], z2_last[:])
+        weave_pairs(on_vector, I32, woven[1, 0][:], z_last[:])
+        weave_pairs(on_vector, I32, woven[1, 1][:], z2_last[:])
         for j in range(2):
             quantise(codes[1, j][:], planes[1, j][:], woven[1, j][:])
             passes(last_accs, j, codes[1, j], planes[1, j])
 
-        results = [at(10 * KB + 256, "result0", planar, F32), sbuf("result1", planar, F32)]
-        rounded = [at(15 * KB - 256, "rounded0", [P, SLOTS * CHUNK], BF16), sbuf("rounded1", [P, SLOTS * CHUNK], BF16)]
-
-        def round_columns(copy, c, lo, hi):
-            weave(copy, rounded[c][:, SLOTS * lo : SLOTS * hi], results[c][:, :, lo:hi])
+        results = [sbuf("result%d" % c, planar, F32) for c in range(2)]
+        first_rounded = [
+            sbuf("rounded0_0", [P, SLOTS * HALF], BF16),
+            sbuf("rounded0_1", [P, SLOTS * HALF], BF16, "woven1_0"),
+        ]
+        last_rounded = sbuf("rounded1", [P, SLOTS * CHUNK], BF16)
 
         for b in range(2):
             on_scalar(out=results[0][:, part(b, 2), :], in_=first_accs[b][:])
             store(results[0], 0, part(b, 2))
-        round_columns(on_scalar, 0, 0, 64)
-        round_columns(on_vector, 0, 64, CHUNK)
-        hand_on(0, rounded[0])
+        for i, copy in enumerate((on_scalar, on_vector)):
+            weave(copy, first_rounded[i][:], results[0][:, :, part(i, HALF)])
+        for i in (1, 0):
+            quantise(out_codes[:, part(i, HALF)], out_plane[:, part(i, HALF)], first_rounded[i][:])
+        store_words(0)
         for t in range(SLOTS):
-            (on_vector if t % 2 else on_scalar)(out=results[1][:, t : t + 1, :], in_=last_accs[t][:])
+            (on_vector if t in (1, 3) else on_scalar)(out=results[1][:, t : t + 1, :], in_=last_accs[t][:])
             if t % 2:
                 store(results[1], 1, part(t // 2, 2))
-        round_columns(on_vector, 1, 0, 176)
-        round_columns(on_scalar, 1, 176, CHUNK)
-        hand_on(1, rounded[1])
+        weave(on_vector, last_rounded[:, : SLOTS * VECTOR_ROUNDS_LAST], results[1][:, :, :VECTOR_ROUNDS_LAST])
+        weave(on_scalar, last_rounded[:, SLOTS * VECTOR_ROUNDS_LAST :], results[1][:, :, VECTOR_ROUNDS_LAST:])
+        quantise(out_codes[:, part(1, CHUNK)], out_plane[:, part(1, CHUNK)], last_rounded[:])
+        store_words(1)
 
         for q in range(P // QUADRANT):
             queue = nc.scalar if q % 2 else nc.sync

@@ -231,7 +231,6 @@ def tile_picked_fisher8_none_po_kernel(
             nc.vector.quantize_mx(out=codes.bitcast(FP8X4), scales=plane, in_=woven)
 
         out_codes = sbuf("out_codes", [P, S], U32)
-        out_plane = sbuf("out_plane", [P, S], U8)
         out_rows = out_0.rearrange("(p t) n -> p t n", t=SLOTS)
         out_words = word_rows(out_1)
 
@@ -286,7 +285,7 @@ def tile_picked_fisher8_none_po_kernel(
             whiten(neg_d[3][:, part(i, HALF)], last_gaps[i], 0, 3, i * HALF, HALF)
         orders_first(3)
 
-        woven = {(c, j): sbuf("woven%d_%d" % (c, j), [P, SLOTS * CHUNK], BF16) for c in range(2) for j in range(2)}
+        woven = {(c, j): sbuf("woven%d_%d" % (c, j), [P, SLOTS * CHUNK], BF16) for c, j in ((0, 0), (0, 1), (1, 1))}
         codes = {(c, j): sbuf("codes%d_%d" % (c, j), row, U32) for c in range(2) for j in range(2)}
         planes = {(c, j): sbuf("plane%d_%d" % (c, j), row, U8) for c in range(2) for j in range(2)}
         weave_pairs(on_scalar, U32, woven[0, 0][:], z_first[:])
@@ -307,13 +306,14 @@ def tile_picked_fisher8_none_po_kernel(
         deal_columns(nc, w_codes[1], w3_raw, 4)
         deal_columns(nc, w_codes[0], w2_raw, 4)
         first_accs = [bank(b, "out0_%d" % b, [P, 2, CHUNK]) for b in range(2)]
-        for j in range(2):
-            quantise(codes[0, j][:], planes[0, j][:], woven[0, j][:])
-            passes(first_accs, j, codes[0, j], planes[0, j])
-        late = sbuf("late", [P, 2, CHUNK], F32, "z2_first")
+        quantise(codes[0, 0][:], planes[0, 0][:], woven[0, 0][:])
+        passes(first_accs, 0, codes[0, 0], planes[0, 0])
+        neg_d.append(at(LAST_NEG_D_AT, "neg_d1_2", row, F32)[:])
+        neg_d.append(sbuf("neg_d1_3", row, F32, "z2_first")[:])
         for t in range(2, SLOTS):
-            neg_d.append(late[:, t - 2, :])
             whiten(neg_d[t], gaps[t], 1, t)
+        quantise(codes[0, 1][:], planes[0, 1][:], woven[0, 1][:])
+        passes(first_accs, 1, codes[0, 1], planes[0, 1])
 
         z_last = at(Z_LAST_AT, "z_last", paired, BF16)
         z2_last = sbuf("z2_last", paired, BF16)
@@ -325,12 +325,13 @@ def tile_picked_fisher8_none_po_kernel(
             second_order(z2_last, squares[:, t, :], t)
         for t in range(2, SLOTS):
             square(squares[:, t, :], neg_d[t])
-        first_order_on_vector(z_last, neg_d[2], 2)
-        second_order_on_vector(z2_last, squares[:, 2, :], 2)
-        first_order_on_vector(z_last, neg_d[3], 3)
-        second_order_on_vector(z2_last, squares[:, 3, :], 3)
+        for t in range(2, SLOTS):
+            first_order_on_vector(z_last, neg_d[t], t)
+        for t in range(2, SLOTS):
+            second_order_on_vector(z2_last, squares[:, t, :], t)
 
         last_accs = [bank(2 + t, "out1_%d" % t, [P, 1, CHUNK]) for t in range(SLOTS)]
+        woven[1, 0] = sbuf("woven1_0", [P, SLOTS * CHUNK], BF16, "z2_first")
         weave_pairs(on_vector, I32, woven[1, 0][:], z_last[:])
         weave_pairs(on_vector, I32, woven[1, 1][:], z2_last[:])
         for j in range(2):
@@ -338,24 +339,21 @@ def tile_picked_fisher8_none_po_kernel(
             passes(last_accs, j, codes[1, j], planes[1, j])
 
         results = [sbuf("result%d" % c, planar, F32) for c in range(2)]
-        first_rounded = [
-            sbuf("rounded0_0", [P, SLOTS * HALF], BF16),
-            sbuf("rounded0_1", [P, SLOTS * HALF], BF16, "woven1_0"),
-        ]
+        first_rounded = sbuf("rounded0", [P, SLOTS * CHUNK], BF16, "z2_first")
         last_rounded = sbuf("rounded1", [P, SLOTS * CHUNK], BF16)
 
         for b in range(2):
             on_scalar(out=results[0][:, part(b, 2), :], in_=first_accs[b][:])
             store(results[0], 0, part(b, 2))
-        for i, copy in enumerate((on_scalar, on_vector)):
-            weave(copy, first_rounded[i][:], results[0][:, :, part(i, HALF)])
-        for i in (1, 0):
-            quantise(out_codes[:, part(i, HALF)], out_plane[:, part(i, HALF)], first_rounded[i][:])
-        store_words(0)
+        weave(on_scalar, first_rounded[:, : SLOTS * SCALAR_ROUNDS_FIRST], results[0][:, :, :SCALAR_ROUNDS_FIRST])
+        weave(on_vector, first_rounded[:, SLOTS * SCALAR_ROUNDS_FIRST :], results[0][:, :, SCALAR_ROUNDS_FIRST:])
         for t in range(SLOTS):
             (on_vector if t in (1, 3) else on_scalar)(out=results[1][:, t : t + 1, :], in_=last_accs[t][:])
             if t % 2:
                 store(results[1], 1, part(t // 2, 2))
+        out_plane = sbuf("out_plane", [P, S], U8, "plane1_1")
+        quantise(out_codes[:, part(0, CHUNK)], out_plane[:, part(0, CHUNK)], first_rounded[:])
+        store_words(0)
         weave(on_vector, last_rounded[:, : SLOTS * VECTOR_ROUNDS_LAST], results[1][:, :, :VECTOR_ROUNDS_LAST])
         weave(on_scalar, last_rounded[:, SLOTS * VECTOR_ROUNDS_LAST :], results[1][:, :, VECTOR_ROUNDS_LAST:])
         quantise(out_codes[:, part(1, CHUNK)], out_plane[:, part(1, CHUNK)], last_rounded[:])

@@ -116,10 +116,8 @@ def tile_picked_fisher8_none_po_kernel(
         g1_sb = sbuf("g1_sb", [P, SLOTS], F32)
         g2_sb = sbuf("g2_sb", [P, SLOTS], F32)
 
-        nc.vector.memset(x_plane[:, : T // 2].bitcast(I32), 0)
-        nc.gpsimd.memset(x_plane[:, T // 2 :].bitcast(I32), 0)
-        nc.vector.memset(w1_plane[:].bitcast(I32), 0)
-        nc.gpsimd.memset(w23_plane[:].bitcast(I32), 0)
+        for plane in (x_plane, w1_plane, w23_plane):
+            nc.vector.memset(plane[:].bitcast(I32), 0)
 
         def load_table(tiles, table, t):
             nc.sync.dma_start(out=tiles[t][:], in_=table.rearrange("(p t) u -> p t u", t=SLOTS)[:, t, :])
@@ -131,8 +129,6 @@ def tile_picked_fisher8_none_po_kernel(
             j, r = divmod(i, SCALE_ROWS)
             load_scale_row(nc, w23_plane, SCALE_ROWS * j, (w2_scales, w3_scales)[j], r)
 
-        nc.gpsimd.dma_start(out=g1_sb[:], in_=g1.rearrange("(p t) o -> p (t o)", t=SLOTS))
-        nc.gpsimd.dma_start(out=g2_sb[:], in_=g2.rearrange("(p t) o -> p (t o)", t=SLOTS))
         nc.sync.dma_start(k1_sb[:], k1)
         load_table(mu_sb, mu, 0)
         nc.sync.dma_start(offs_sb[:], offs)
@@ -146,6 +142,9 @@ def tile_picked_fisher8_none_po_kernel(
         early_tables = ((mu_sb, mu, 1), (mu_sb, mu, 2), (rs_sb, rs, 1), (mu_sb, mu, 3), (rs_sb, rs, 2))
         for i, (tiles, table, t) in enumerate(early_tables):
             load_table(tiles, table, t)
+            if i == 0:
+                nc.sync.dma_start(out=g1_sb[:], in_=g1.rearrange("(p t) o -> p (t o)", t=SLOTS))
+                nc.sync.dma_start(out=g2_sb[:], in_=g2.rearrange("(p t) o -> p (t o)", t=SLOTS))
             load_w23_row(i)
         load_words(w3_raw, w3_words)
         for i in range(len(early_tables), 2 * SCALE_ROWS - 1):

@@ -146,11 +146,10 @@ def tile_picked_fisher8_none_po_kernel(
                 nc.sync.dma_start(out=g1_sb[:], in_=g1.rearrange("(p t) o -> p (t o)", t=SLOTS))
                 nc.sync.dma_start(out=g2_sb[:], in_=g2.rearrange("(p t) o -> p (t o)", t=SLOTS))
             load_w23_row(i)
-        load_words(w3_raw, w3_words)
-        for i in range(len(early_tables), 2 * SCALE_ROWS - 1):
+        for i in range(len(early_tables), 2 * SCALE_ROWS):
             load_w23_row(i)
         load_table(rs_sb, rs, SLOTS - 1)
-        load_w23_row(2 * SCALE_ROWS - 1)
+        load_words(w3_raw, w3_words)
         load_words(w2_raw, w2_words)
 
         mu0_picked = sbuf("mu0_picked", [P, S], F32)
@@ -347,7 +346,7 @@ def tile_picked_fisher8_none_po_kernel(
         weave(on_scalar, first_rounded[:, : SLOTS * SCALAR_ROUNDS_FIRST], results[0][:, :, :SCALAR_ROUNDS_FIRST])
         weave(on_vector, first_rounded[:, SLOTS * SCALAR_ROUNDS_FIRST :], results[0][:, :, SCALAR_ROUNDS_FIRST:])
         for t in range(SLOTS):
-            (on_vector if t in (1, 3) else on_scalar)(out=results[1][:, t : t + 1, :], in_=last_accs[t][:])
+            (on_scalar if t % 2 else on_vector)(out=results[1][:, t : t + 1, :], in_=last_accs[t][:])
             if t % 2:
                 store(results[1], 1, part(t // 2, 2))
         out_plane = sbuf("out_plane", [P, S], U8, "plane1_1")

@@ -21,58 +21,37 @@ QUADRANT = 32
 SCALE_ROWS = 4
 GROUP = 16
 LINE = 16
-WEAVE_RUN = 4
 CHUNK = 256
-HALF = CHUNK // 2
-SCALAR_ROUNDS_FIRST = 64
+WIDE = 2 * U
 VECTOR_ROUNDS_LAST = 176
-
-KB = 1024
-OVERLAP = 256
-Z_FIRST_AT = 4 * KB
-Z_LAST_AT = Z_FIRST_AT - 2 * KB + OVERLAP
-LAST_NEG_D_AT = Z_FIRST_AT + OVERLAP
-SQUARES_AT = Z_FIRST_AT + 2 * KB - OVERLAP
-LAST_SQUARE_AT = 14 * KB
-FIRST_RESULT_AT = LAST_SQUARE_AT - 4 * KB + OVERLAP
-LAST_Z_PLANE_AT = LAST_SQUARE_AT + OVERLAP
-FIRST_ROUNDED_AT = LAST_SQUARE_AT + KB - OVERLAP
-FIRST_SQUARE_AT = 24 * KB
-W2_CODES_AT = FIRST_SQUARE_AT - 2 * KB + OVERLAP
-W23_PLANE_AT = FIRST_SQUARE_AT + OVERLAP
 
 
 def word_rows(words):
     return words[0].rearrange("p c r -> p (c r)").bitcast(I32)
 
 
-def load_scale_row(nc, plane, first, scales, r):
-    nc.sync.dma_start(
-        out=plane[first + r : P : QUADRANT, :].bitcast(I32),
-        in_=scales[0, r : SCALE_ROWS * (P // QUADRANT) : SCALE_ROWS, :].bitcast(I32),
-    )
+def load_scale_rows(nc, plane, first, scales):
+    for r in range(SCALE_ROWS):
+        nc.sync.dma_start(
+            out=plane[first + r : P : QUADRANT, :].bitcast(I32),
+            in_=scales[0, r : SCALE_ROWS * (P // QUADRANT) : SCALE_ROWS, :].bitcast(I32),
+        )
 
 
-def deal_columns(nc, dealt, raw, element_bytes):
+def deal_columns(copy, dealt, raw, element_bytes):
     run = LINE // element_bytes
-    nc.vector.tensor_copy(
-        out=dealt[:].rearrange("p (t c i) -> p c t i", t=SLOTS, i=run),
-        in_=raw[:].rearrange("p (c i t) -> p c t i", t=SLOTS, i=run),
-    )
-
-
-def weave(copy, woven, planar):
     copy(
-        out=woven.rearrange("p (c i t) -> p c t i", t=SLOTS, i=WEAVE_RUN),
-        in_=planar.rearrange("p t (c i) -> p c t i", i=WEAVE_RUN),
+        out=dealt.rearrange("p (t c i) -> p c t i", t=SLOTS, i=run),
+        in_=raw.rearrange("p (c i t) -> p c t i", t=SLOTS, i=run),
     )
 
 
-def weave_pairs(copy, dtype, woven, paired):
-    copy(
-        out=woven.bitcast(dtype).rearrange("p (c i u) -> p c u i", u=2, i=2),
-        in_=paired.rearrange("p u c e -> p u (c e)").bitcast(dtype).rearrange("p u (c i) -> p c u i", i=2),
-    )
+def as_woven(woven, run):
+    return woven.rearrange("p (c i t) -> p c t i", t=SLOTS, i=run)
+
+
+def as_planar(planar, run):
+    return planar.rearrange("p t (c i) -> p c t i", i=run)
 
 
 def tile_picked_fisher8_none_po_kernel(
@@ -84,20 +63,16 @@ def tile_picked_fisher8_none_po_kernel(
 
     with ExitStack() as ctx:
         keep = ctx.enter_context(tc.tile_pool(name="keep", bufs=1))
-        placed = ctx.enter_context(tc.tile_pool(name="placed", bufs=1))
         psum = ctx.enter_context(tc.psum_pool(name="psum", bufs=1))
 
         def sbuf(name, shape, dtype, tag=None):
             return keep.tile(shape, dtype, name=name, tag=tag or name, align_bytes=64)
 
-        def at(offset, name, shape, dtype):
-            return placed.tile(shape, dtype, name=name, tag=name, align_bytes=64, offset=offset)
-
         def bank(b, name, shape):
             return psum.tile(shape, F32, name=name, tag="bank%d" % b)
 
-        def entries(list_tile, first, width):
-            return list_tile[:, first // GROUP : (first + width) // GROUP]
+        def entries(list_tile, c):
+            return list_tile[:, c * CHUNK // GROUP : (c + 1) * CHUNK // GROUP]
 
         def part(i, width):
             return slice(i * width, (i + 1) * width)
@@ -111,8 +86,8 @@ def tile_picked_fisher8_none_po_kernel(
         w1_raw = sbuf("w1_raw", [P, H], I32)
         w2_raw = sbuf("w2_raw", [P, N], I32)
         w3_raw = sbuf("w3_raw", [P, N], I32)
-        mu_sb = [sbuf("mu%d" % t, [P, U], F32) for t in range(SLOTS)]
-        rs_sb = [sbuf("rs%d" % t, [P, U], F32) for t in range(SLOTS)]
+        mu_sb = [sbuf("mu%d" % t, [P, U if t % 2 else WIDE], F32) for t in range(SLOTS)]
+        rs_sb = [sbuf("rs%d" % t, [P, WIDE if t == 3 else U], F32) for t in range(SLOTS)]
         g1_sb = sbuf("g1_sb", [P, SLOTS], F32)
         g2_sb = sbuf("g2_sb", [P, SLOTS], F32)
 
@@ -120,242 +95,195 @@ def tile_picked_fisher8_none_po_kernel(
             nc.vector.memset(plane[:].bitcast(I32), 0)
 
         def load_table(tiles, table, t):
-            nc.sync.dma_start(out=tiles[t][:], in_=table.rearrange("(p t) u -> p t u", t=SLOTS)[:, t, :])
+            nc.sync.dma_start(out=tiles[t][:, :U], in_=table.rearrange("(p t) u -> p t u", t=SLOTS)[:, t, :])
 
         def load_words(raw, words):
             nc.sync.dma_start(out=raw[:], in_=word_rows(words))
 
-        def load_w23_row(i):
-            j, r = divmod(i, SCALE_ROWS)
-            load_scale_row(nc, w23_plane, SCALE_ROWS * j, (w2_scales, w3_scales)[j], r)
-
         nc.sync.dma_start(k1_sb[:], k1)
         load_table(mu_sb, mu, 0)
         nc.sync.dma_start(offs_sb[:], offs)
-        for r in range(SCALE_ROWS):
-            load_scale_row(nc, x_plane, 0, x_scales, r)
+        load_scale_rows(nc, x_plane, 0, x_scales)
         load_words(x_sb, x_words)
-        for r in range(SCALE_ROWS):
-            load_scale_row(nc, w1_plane, 0, w1_scales, r)
+        load_scale_rows(nc, w1_plane, 0, w1_scales)
         load_words(w1_raw, w1_words)
-        load_table(rs_sb, rs, 0)
-        early_tables = ((mu_sb, mu, 1), (mu_sb, mu, 2), (rs_sb, rs, 1), (mu_sb, mu, 3), (rs_sb, rs, 2))
-        for i, (tiles, table, t) in enumerate(early_tables):
+        for tiles, table, t in (
+            (mu_sb, mu, 1), (rs_sb, rs, 0), (mu_sb, mu, 2), (mu_sb, mu, 3), (rs_sb, rs, 1), (rs_sb, rs, 3), (rs_sb, rs, 2)
+        ):
             load_table(tiles, table, t)
-            if i == 0:
-                nc.sync.dma_start(out=g1_sb[:], in_=g1.rearrange("(p t) o -> p (t o)", t=SLOTS))
-                nc.sync.dma_start(out=g2_sb[:], in_=g2.rearrange("(p t) o -> p (t o)", t=SLOTS))
-            load_w23_row(i)
-        for i in range(len(early_tables), 2 * SCALE_ROWS):
-            load_w23_row(i)
-        load_table(rs_sb, rs, SLOTS - 1)
-        load_words(w3_raw, w3_words)
         load_words(w2_raw, w2_words)
+        load_words(w3_raw, w3_words)
+        load_scale_rows(nc, w23_plane, 0, w2_scales)
+        load_scale_rows(nc, w23_plane, SCALE_ROWS, w3_scales)
+        nc.sync.dma_start(out=g1_sb[:], in_=g1.rearrange("(p t) o -> p (t o)", t=SLOTS))
+        nc.sync.dma_start(out=g2_sb[:], in_=g2.rearrange("(p t) o -> p (t o)", t=SLOTS))
 
-        mu0_picked = sbuf("mu0_picked", [P, S], F32)
-        for c in range(2):
-            on_vector(out=mu0_picked[:, part(c, CHUNK)], in_=mu_sb[0][:].indirect(entries(k1_sb, c * CHUNK, CHUNK)))
+        means = sbuf("means", [P, SLOTS, S], F32)
+        last_rs = sbuf("last_rs", [P, S], F32)
+        w1_codes = sbuf("w1_codes", [P, H], U32)
+        for t in range(SLOTS):
+            if t % 2:
+                for c in range(2):
+                    nc.scalar.activation(out=means[:, t, part(c, CHUNK)], in_=mu_sb[t][:].indirect(entries(k1_sb, c)), func=ACT.Copy)
+            else:
+                nc.scalar.activation(out=means[:, t, :], in_=mu_sb[t][:].indirect(k1_sb[:]), func=ACT.Copy)
+            if t == 0:
+                deal_columns(on_scalar, w1_codes[:], w1_raw[:].bitcast(U32), 4)
+        nc.scalar.activation(out=last_rs[:], in_=rs_sb[3][:].indirect(k1_sb[:]), func=ACT.Copy)
+        w_codes = [sbuf("w2_codes", [P, N], U32), sbuf("w3_codes", [P, N], U32)]
+        deal_columns(on_scalar, w_codes[0][:], w2_raw[:].bitcast(U32), 4)
+        deal_columns(on_scalar, w_codes[1][:], w3_raw[:].bitcast(U32), 4)
+
         picked_plane = sbuf("picked_plane", [P, S], U8)
         on_vector(out=picked_plane[:], in_=x_plane[:].indirect(offs_sb[:]))
 
         def pick(c, tag=None):
-            picked = sbuf("picked%d" % c, [P, CHUNK], U32, tag)
-            on_vector(out=picked[:], in_=x_sb[:].bitcast(U32).indirect(entries(offs_sb, c * CHUNK, CHUNK)))
-            return picked
+            words = sbuf("picked%d" % c, [P, CHUNK], U32, tag)
+            on_vector(out=words[:], in_=x_sb[:].bitcast(U32).indirect(entries(offs_sb, c)))
+            return words
 
-        w1_codes = sbuf("w1_codes", [P, H], I32)
         w1_dealt_plane = sbuf("w1_dealt_plane", [P, H], U8)
         picked = [pick(0)]
-        deal_columns(nc, w1_dealt_plane, w1_plane, 1)
-        deal_columns(nc, w1_codes, w1_raw, 4)
-        picked.append(pick(1, "w1_raw"))
+        deal_columns(on_vector, w1_dealt_plane[:], w1_plane[:], 1)
+        picked.append(pick(1, "w1_plane"))
 
+        def first_product(out, c, t):
+            nc.tensor.matmul_mx(
+                out=out,
+                lhsT=w1_codes[:, part(t, P)].bitcast(FP8X4),
+                lhsT_scale=w1_dealt_plane[:, part(t, P)],
+                rhs=picked[c][:].bitcast(FP8X4),
+                rhs_scale=picked_plane[:, part(c, CHUNK)],
+                start=True,
+                stop=True,
+            )
+
+        units = ((0, (0,)), (0, (1,)), (1, (0, 1)), (0, (2, 3)), (1, (2, 3)))
         y = {}
-
-        def first_product(c, slots, b):
-            shape = [P, len(slots), CHUNK]
-            acc = bank(b, "y%d_%d" % (c, slots[0]), shape)
-            held = sbuf("y_sb%d_%d" % (c, slots[0]), shape, F32) if slots[0] else acc
+        for b, (c, slots) in enumerate(units):
+            y[c, slots[0]] = bank(b, "y%d_%d" % (c, slots[0]), [P, len(slots), CHUNK])
             for j, t in enumerate(slots):
-                nc.tensor.matmul_mx(
-                    out=acc[:, j, :],
-                    lhsT=w1_codes[:, part(t, P)].bitcast(FP8X4),
-                    lhsT_scale=w1_dealt_plane[:, part(t, P)],
-                    rhs=picked[c][:].bitcast(FP8X4),
-                    rhs_scale=picked_plane[:, part(c, CHUNK)],
-                    start=True,
-                    stop=True,
-                )
-                y[c, t] = held[:, j, :]
-            if slots[0]:
-                on_scalar(out=held[:], in_=acc[:])
+                first_product(y[c, slots[0]][:, j, :], c, t)
 
-        groups = [(0, (t,)) for t in range(SLOTS)] + [(1, (0,)), (1, (1,)), (1, (2, 3))]
-        for b, (c, slots) in enumerate(groups):
-            first_product(c, slots, b)
+        gap = sbuf("gap", [P, 2, S], F32)
+        late_gap = sbuf("late_gap", [P, 2, 2, CHUNK], F32)
+        d = sbuf("d", [P, 2, SLOTS, CHUNK], F32)
 
-        neg_g1 = sbuf("neg_g1", [P, SLOTS], F32)
-        neg_g2 = sbuf("neg_g2", [P, SLOTS], F32)
-        nc.scalar.activation(out=neg_g1[:], in_=g1_sb[:], func=ACT.Copy, scale=-1.0)
-        nc.scalar.activation(out=neg_g2[:], in_=g2_sb[:], func=ACT.Copy, scale=-1.0)
+        def subtract(c, first, slots):
+            cols = part(c, CHUNK)
+            out = late_gap[:, c, :, :] if first == 2 else gap[:, slots, cols]
+            held = y[c, first][:, slots.start - first : slots.stop - first, :]
+            nc.vector.tensor_tensor(out, held, means[:, slots, cols], ALU.subtract)
 
-        def subtract(gap, c, t, lo=0, width=CHUNK):
-            means = mu_sb[t][:].indirect(entries(k1_sb, c * CHUNK + lo, width)) if t else mu0_picked[:, part(c, CHUNK)]
-            nc.vector.tensor_tensor(gap, means, y[c, t][:, lo : lo + width], ALU.subtract)
+        def whiten(c, t):
+            cols = part(c, CHUNK)
+            factor = rs_sb[t][:].indirect(entries(k1_sb, c))
+            nc.vector.tensor_tensor(d[:, c, t, :], factor, gap[:, t, cols] if t < 2 else late_gap[:, c, t - 2, :], ALU.mult)
 
-        def whiten(neg_d, gap, c, t, lo=0, width=CHUNK):
-            nc.vector.tensor_tensor(neg_d, rs_sb[t][:].indirect(entries(k1_sb, c * CHUNK + lo, width)), gap, ALU.mult)
+        both_squares = sbuf("squares", [P, 2, SLOTS * CHUNK], F32, "w3_raw")
+        squares = [both_squares[:, c, :] for c in range(2)]
+        woven = {(c, j): sbuf("woven%d_%d" % (c, j), [P, SLOTS * CHUNK], BF16) for c in range(2) for j in range(2)}
+        pairs = sbuf("pairs", [P, 2, CHUNK, 2], BF16)
+        codes = {(c, j): sbuf("codes%d_%d" % (c, j), [P, CHUNK], U32) for c in range(2) for j in range(2)}
+        planes = {(c, j): sbuf("plane%d_%d" % (c, j), [P, CHUNK], U8) for c in range(2) for j in range(2)}
 
-        def square(out, neg_d):
-            nc.scalar.activation(out=out, in_=neg_d, func=ACT.Square)
+        def square(c):
+            nc.scalar.activation(out=as_woven(squares[c], 2), in_=as_planar(d[:, c, :, :], 2), func=ACT.Square)
 
-        def first_order(z, neg_d, t):
-            nc.scalar.activation(out=z[:, t // 2, :, t % 2], in_=neg_d, func=ACT.Copy, scale=neg_g1[:, t : t + 1])
+        def first_order(c):
+            gain = g1_sb[:].unsqueeze(1).unsqueeze(3).broadcast_to([P, CHUNK // 2, SLOTS, 2])
+            nc.vector.tensor_tensor(as_woven(woven[c, 0][:], 2), as_planar(d[:, c, :, :], 2), gain, ALU.mult)
 
-        def first_order_on_vector(z, neg_d, t):
-            nc.vector.tensor_scalar(z[:, t // 2, :, t % 2], neg_d, neg_g1[:, t : t + 1], None, ALU.mult)
-
-        def second_order(z2, squared, t):
-            nc.scalar.activation(
-                out=z2[:, t // 2, :, t % 2], in_=squared, func=ACT.Identity, scale=g2_sb[:, t : t + 1], bias=neg_g2[:, t : t + 1]
+        def second_order(c):
+            gain = g2_sb[:].unsqueeze(1).broadcast_to([P, CHUNK, SLOTS])
+            nc.vector.scalar_tensor_tensor(
+                woven[c, 1][:].rearrange("p (c t) -> p c t", t=SLOTS),
+                squares[c].rearrange("p (c t) -> p c t", t=SLOTS),
+                -1.0, gain, ALU.add, ALU.mult,
             )
 
-        def second_order_on_vector(z2, squared, t):
-            nc.vector.tensor_scalar(
-                z2[:, t // 2, :, t % 2], squared, g2_sb[:, t : t + 1], neg_g2[:, t : t + 1], ALU.mult, ALU.add
-            )
+        accs = [
+            [bank(5 + b, "out0_%d" % b, [P, 2, CHUNK]) for b in range(2)],
+            [bank((7 + t) % 8, "out1_%d" % t, [P, 1, CHUNK]) for t in range(SLOTS)],
+        ]
+        w23_dealt_plane = sbuf("w23_dealt_plane", [P, N], U8)
 
-        def quantise(codes, plane, woven):
-            nc.vector.quantize_mx(out=codes.bitcast(FP8X4), scales=plane, in_=woven)
+        def quantise(out_codes, plane, values):
+            nc.vector.quantize_mx(out=out_codes.bitcast(FP8X4), scales=plane, in_=values)
 
-        out_codes = sbuf("out_codes", [P, S], U32)
-        out_rows = out_0.rearrange("(p t) n -> p t n", t=SLOTS)
-        out_words = word_rows(out_1)
-
-        def passes(accs, j, codes, plane):
-            per = SLOTS // len(accs)
+        def product(c, j):
+            quantise(codes[c, j][:], planes[c, j][:], woven[c, j][:])
+            per = SLOTS // len(accs[c])
             for t in range(SLOTS):
                 nc.tensor.matmul_mx(
-                    out=accs[t // per][:, t % per, :],
+                    out=accs[c][t // per][:, t % per, :],
                     lhsT=w_codes[j][:, part(t, P)].bitcast(FP8X4),
                     lhsT_scale=w23_dealt_plane[SCALE_ROWS * j : P, part(t, P)],
-                    rhs=codes[:].bitcast(FP8X4),
-                    rhs_scale=plane[:],
+                    rhs=codes[c, j][:].bitcast(FP8X4),
+                    rhs_scale=planes[c, j][:],
                     start=(j == 0 and t % per == 0),
                     stop=(j == 1 and t % per == per - 1),
                 )
 
-        def store(result, c, slots):
-            nc.sync.dma_start(out=out_rows[:, slots, part(c, CHUNK)], in_=result[:, slots, :])
+        subtract(0, 0, slice(0, 1))
+        subtract(0, 1, slice(1, 2))
+        subtract(1, 0, slice(0, 2))
+        whiten(0, 0)
+        whiten(1, 0)
+        for c in range(2):
+            subtract(c, 2, slice(2, 4))
+        for c in range(2):
+            whiten(c, 1)
+        nc.vector.tensor_tensor(
+            d[:, :, 3, :], last_rs[:].rearrange("p (c n) -> p c n", c=2), late_gap[:, :, 1, :], ALU.mult
+        )
+        for c in range(2):
+            whiten(c, 2)
+            square(c)
+        for t in range(SLOTS):
+            nc.scalar.activation(out=pairs[:, t // 2, :, t % 2], in_=d[:, 1, t, :], func=ACT.Copy, scale=g1_sb[:, t : t + 1])
+        on_scalar(
+            out=woven[1, 0][:].bitcast(U32).rearrange("p (c i u) -> p c u i", u=2, i=2),
+            in_=pairs[:].rearrange("p u c e -> p u (c e)").bitcast(U32).rearrange("p u (c i) -> p c u i", i=2),
+        )
+        deal_columns(on_vector, w23_dealt_plane[:], w23_plane[:], 1)
+        first_order(0)
+        second_order(0)
+        product(0, 0)
+        product(0, 1)
+        second_order(1)
+        product(1, 0)
+        product(1, 1)
 
-        def store_words(c):
+        out_codes = sbuf("out_codes", [P, S], U32)
+        out_plane = sbuf("out_plane", [P, S], U8, "plane1_1")
+        out_rows = out_0.rearrange("(p t) n -> p t n", t=SLOTS)
+        out_words = word_rows(out_1)
+        results = [sbuf("result%d" % c, [P, SLOTS, CHUNK], F32) for c in range(2)]
+        rounded = [sbuf("rounded0", [P, SLOTS * CHUNK], BF16, "woven1_1"), sbuf("rounded1", [P, SLOTS * CHUNK], BF16)]
+
+        def store(c, slots):
+            nc.sync.dma_start(out=out_rows[:, slots, part(c, CHUNK)], in_=results[c][:, slots, :])
+
+        def weave(copy, c, lo, hi):
+            copy(out=as_woven(rounded[c][:, SLOTS * lo : SLOTS * hi], 4), in_=as_planar(results[c][:, :, lo:hi], 4))
+
+        def hand_on(c):
+            quantise(out_codes[:, part(c, CHUNK)], out_plane[:, part(c, CHUNK)], rounded[c][:])
             nc.sync.dma_start(out=out_words[:, part(c, CHUNK)], in_=out_codes[:, part(c, CHUNK)].bitcast(I32))
 
-        planar = [P, SLOTS, CHUNK]
-        paired = [P, 2, CHUNK, 2]
-        row = [P, CHUNK]
-
-        z_first = at(Z_FIRST_AT, "z_first", paired, BF16)
-        z2_first = sbuf("z2_first", paired, BF16)
-        gaps = [sbuf("gap0_%d" % t, row, F32)[:] for t in range(SLOTS - 1)]
-        last_gaps = [sbuf("gap0_3_%d" % i, [P, HALF], F32)[:] for i in range(2)]
-        neg_d = [sbuf("neg_d0_%d" % t, row, F32)[:] for t in range(SLOTS)]
-        squares = [sbuf("square0_%d" % t, row, F32)[:] for t in range(SLOTS - 1)]
-        squares.append(at(FIRST_SQUARE_AT, "square0_3", row, F32)[:])
-
-        def orders_first(t):
-            square(squares[t], neg_d[t])
-            first_order(z_first, neg_d[t], t)
-            second_order(z2_first, squares[t], t)
-
-        subtract(gaps[0], 0, 0)
-        whiten(neg_d[0], gaps[0], 0, 0)
-        subtract(gaps[1], 0, 1)
-        orders_first(0)
-        subtract(gaps[2], 0, 2)
-        whiten(neg_d[1], gaps[1], 0, 1)
-        orders_first(1)
-        for i in range(2):
-            subtract(last_gaps[i], 0, 3, i * HALF, HALF)
-        whiten(neg_d[2], gaps[2], 0, 2)
-        orders_first(2)
-        for i in range(2):
-            whiten(neg_d[3][:, part(i, HALF)], last_gaps[i], 0, 3, i * HALF, HALF)
-        orders_first(3)
-
-        woven = {(c, j): sbuf("woven%d_%d" % (c, j), [P, SLOTS * CHUNK], BF16) for c, j in ((0, 0), (0, 1), (1, 1))}
-        codes = {(c, j): sbuf("codes%d_%d" % (c, j), row, U32) for c in range(2) for j in range(2)}
-        planes = {(c, j): sbuf("plane%d_%d" % (c, j), row, U8) for c in range(2) for j in range(2)}
-        weave_pairs(on_scalar, U32, woven[0, 0][:], z_first[:])
-        weave_pairs(on_scalar, U32, woven[0, 1][:], z2_first[:])
-
-        work = sbuf("work", [P, 2 + SLOTS, CHUNK], F32, "gap0_3_0")
-        neg_d = [work[:, t, :] for t in range(2)]
-        gaps = [work[:, 2 + t, :] for t in range(SLOTS)]
-        subtract(gaps[0], 1, 0)
-        for t in range(2):
-            subtract(gaps[t + 1], 1, t + 1)
-            whiten(neg_d[t], gaps[t], 1, t)
-        subtract(gaps[3], 1, 3)
-
-        w23_dealt_plane = at(W23_PLANE_AT, "w23_dealt_plane", [P, N], U8)
-        w_codes = [at(W2_CODES_AT, "w2_codes", [P, N], I32), sbuf("w3_codes", [P, N], I32, "neg_d0_3")]
-        deal_columns(nc, w23_dealt_plane, w23_plane, 1)
-        deal_columns(nc, w_codes[1], w3_raw, 4)
-        deal_columns(nc, w_codes[0], w2_raw, 4)
-        first_accs = [bank(b, "out0_%d" % b, [P, 2, CHUNK]) for b in range(2)]
-        quantise(codes[0, 0][:], planes[0, 0][:], woven[0, 0][:])
-        passes(first_accs, 0, codes[0, 0], planes[0, 0])
-        neg_d.append(at(LAST_NEG_D_AT, "neg_d1_2", row, F32)[:])
-        neg_d.append(sbuf("neg_d1_3", row, F32, "z2_first")[:])
-        for t in range(2, SLOTS):
-            whiten(neg_d[t], gaps[t], 1, t)
-        quantise(codes[0, 1][:], planes[0, 1][:], woven[0, 1][:])
-        passes(first_accs, 1, codes[0, 1], planes[0, 1])
-
-        z_last = at(Z_LAST_AT, "z_last", paired, BF16)
-        z2_last = sbuf("z2_last", paired, BF16)
-        squares = at(SQUARES_AT, "squares1", planar, F32)
-        square(squares[:, 0:2, :], work[:, 0:2, :])
-        for t in range(2):
-            first_order(z_last, neg_d[t], t)
-        for t in range(2):
-            second_order(z2_last, squares[:, t, :], t)
-        for t in range(2, SLOTS):
-            square(squares[:, t, :], neg_d[t])
-        for t in range(2, SLOTS):
-            first_order_on_vector(z_last, neg_d[t], t)
-        for t in range(2, SLOTS):
-            second_order_on_vector(z2_last, squares[:, t, :], t)
-
-        last_accs = [bank(2 + t, "out1_%d" % t, [P, 1, CHUNK]) for t in range(SLOTS)]
-        woven[1, 0] = sbuf("woven1_0", [P, SLOTS * CHUNK], BF16, "z2_first")
-        weave_pairs(on_vector, I32, woven[1, 0][:], z_last[:])
-        weave_pairs(on_vector, I32, woven[1, 1][:], z2_last[:])
-        for j in range(2):
-            quantise(codes[1, j][:], planes[1, j][:], woven[1, j][:])
-            passes(last_accs, j, codes[1, j], planes[1, j])
-
-        results = [sbuf("result%d" % c, planar, F32) for c in range(2)]
-        first_rounded = sbuf("rounded0", [P, SLOTS * CHUNK], BF16, "z2_first")
-        last_rounded = sbuf("rounded1", [P, SLOTS * CHUNK], BF16)
-
         for b in range(2):
-            on_scalar(out=results[0][:, part(b, 2), :], in_=first_accs[b][:])
-            store(results[0], 0, part(b, 2))
-        weave(on_scalar, first_rounded[:, : SLOTS * SCALAR_ROUNDS_FIRST], results[0][:, :, :SCALAR_ROUNDS_FIRST])
-        weave(on_vector, first_rounded[:, SLOTS * SCALAR_ROUNDS_FIRST :], results[0][:, :, SCALAR_ROUNDS_FIRST:])
+            on_scalar(out=results[0][:, part(b, 2), :], in_=accs[0][b][:])
+            store(0, part(b, 2))
+        weave(on_vector, 0, 0, CHUNK)
         for t in range(SLOTS):
-            (on_scalar if t % 2 else on_vector)(out=results[1][:, t : t + 1, :], in_=last_accs[t][:])
+            (on_scalar if t % 2 else on_vector)(out=results[1][:, t : t + 1, :], in_=accs[1][t][:])
             if t % 2:
-                store(results[1], 1, part(t // 2, 2))
-        out_plane = sbuf("out_plane", [P, S], U8, "plane1_1")
-        quantise(out_codes[:, part(0, CHUNK)], out_plane[:, part(0, CHUNK)], first_rounded[:])
-        store_words(0)
-        weave(on_vector, last_rounded[:, : SLOTS * VECTOR_ROUNDS_LAST], results[1][:, :, :VECTOR_ROUNDS_LAST])
-        weave(on_scalar, last_rounded[:, SLOTS * VECTOR_ROUNDS_LAST :], results[1][:, :, VECTOR_ROUNDS_LAST:])
-        quantise(out_codes[:, part(1, CHUNK)], out_plane[:, part(1, CHUNK)], last_rounded[:])
-        store_words(1)
+                store(1, part(t // 2, 2))
+        hand_on(0)
+        weave(on_vector, 1, 0, VECTOR_ROUNDS_LAST)
+        weave(on_scalar, 1, VECTOR_ROUNDS_LAST, CHUNK)
+        hand_on(1)
 
         for q in range(P // QUADRANT):
             queue = nc.scalar if q % 2 else nc.sync

@@ -30,8 +30,8 @@ def word_rows(words):
     return words[0].rearrange("p c r -> p (c r)").bitcast(I32)
 
 
-def load_scale_rows(nc, plane, first, scales):
-    for r in range(SCALE_ROWS):
+def load_scale_rows(nc, plane, first, scales, rows=range(SCALE_ROWS)):
+    for r in rows:
         nc.sync.dma_start(
             out=plane[first + r : P : QUADRANT, :].bitcast(I32),
             in_=scales[0, r : SCALE_ROWS * (P // QUADRANT) : SCALE_ROWS, :].bitcast(I32),
@@ -87,7 +87,7 @@ def tile_picked_fisher8_none_po_kernel(
         w2_raw = sbuf("w2_raw", [P, N], I32)
         w3_raw = sbuf("w3_raw", [P, N], I32)
         mu_sb = [sbuf("mu%d" % t, [P, U if t % 2 else WIDE], F32) for t in range(SLOTS)]
-        rs_sb = [sbuf("rs%d" % t, [P, WIDE if t == 3 else U], F32) for t in range(SLOTS)]
+        rs_sb = [sbuf("rs%d" % t, [P, WIDE if t == 2 else U], F32) for t in range(SLOTS)]
         g1_sb = sbuf("g1_sb", [P, SLOTS], F32)
         g2_sb = sbuf("g2_sb", [P, SLOTS], F32)
 
@@ -108,18 +108,19 @@ def tile_picked_fisher8_none_po_kernel(
         load_scale_rows(nc, w1_plane, 0, w1_scales)
         load_words(w1_raw, w1_words)
         for tiles, table, t in (
-            (mu_sb, mu, 1), (rs_sb, rs, 0), (mu_sb, mu, 2), (mu_sb, mu, 3), (rs_sb, rs, 1), (rs_sb, rs, 3), (rs_sb, rs, 2)
+            (mu_sb, mu, 1), (rs_sb, rs, 0), (mu_sb, mu, 2), (mu_sb, mu, 3), (rs_sb, rs, 1), (rs_sb, rs, 2), (rs_sb, rs, 3)
         ):
             load_table(tiles, table, t)
         load_words(w2_raw, w2_words)
         load_words(w3_raw, w3_words)
         load_scale_rows(nc, w23_plane, 0, w2_scales)
-        load_scale_rows(nc, w23_plane, SCALE_ROWS, w3_scales)
+        load_scale_rows(nc, w23_plane, SCALE_ROWS, w3_scales, range(SCALE_ROWS - 1))
         nc.sync.dma_start(out=g1_sb[:], in_=g1.rearrange("(p t) o -> p (t o)", t=SLOTS))
+        load_scale_rows(nc, w23_plane, SCALE_ROWS, w3_scales, (SCALE_ROWS - 1,))
         nc.sync.dma_start(out=g2_sb[:], in_=g2.rearrange("(p t) o -> p (t o)", t=SLOTS))
 
         means = sbuf("means", [P, SLOTS, S], F32)
-        last_rs = sbuf("last_rs", [P, S], F32)
+        late_rs = sbuf("late_rs", [P, 2, S], F32)
         w1_codes = sbuf("w1_codes", [P, H], U32)
         for t in range(SLOTS):
             if t % 2:
@@ -129,7 +130,9 @@ def tile_picked_fisher8_none_po_kernel(
                 nc.scalar.activation(out=means[:, t, :], in_=mu_sb[t][:].indirect(k1_sb[:]), func=ACT.Copy)
             if t == 0:
                 deal_columns(on_scalar, w1_codes[:], w1_raw[:].bitcast(U32), 4)
-        nc.scalar.activation(out=last_rs[:], in_=rs_sb[3][:].indirect(k1_sb[:]), func=ACT.Copy)
+        nc.scalar.activation(out=late_rs[:, 0, :], in_=rs_sb[2][:].indirect(k1_sb[:]), func=ACT.Copy)
+        for c in range(2):
+            nc.scalar.activation(out=late_rs[:, 1, part(c, CHUNK)], in_=rs_sb[3][:].indirect(entries(k1_sb, c)), func=ACT.Copy)
         w_codes = [sbuf("w2_codes", [P, N], U32), sbuf("w3_codes", [P, N], U32)]
         deal_columns(on_scalar, w_codes[0][:], w2_raw[:].bitcast(U32), 4)
         deal_columns(on_scalar, w_codes[1][:], w3_raw[:].bitcast(U32), 4)
@@ -178,10 +181,9 @@ def tile_picked_fisher8_none_po_kernel(
         def whiten(c, t):
             cols = part(c, CHUNK)
             factor = rs_sb[t][:].indirect(entries(k1_sb, c))
-            nc.vector.tensor_tensor(d[:, c, t, :], factor, gap[:, t, cols] if t < 2 else late_gap[:, c, t - 2, :], ALU.mult)
+            nc.vector.tensor_tensor(d[:, c, t, :], factor, gap[:, t, cols], ALU.mult)
 
-        both_squares = sbuf("squares", [P, 2, SLOTS * CHUNK], F32, "w3_raw")
-        squares = [both_squares[:, c, :] for c in range(2)]
+        squares = [sbuf("squares%d" % c, [P, SLOTS * CHUNK], F32, "w%d_raw" % (2 + c))[:] for c in range(2)]
         woven = {(c, j): sbuf("woven%d_%d" % (c, j), [P, SLOTS * CHUNK], BF16) for c in range(2) for j in range(2)}
         pairs = sbuf("pairs", [P, 2, CHUNK, 2], BF16)
         codes = {(c, j): sbuf("codes%d_%d" % (c, j), [P, CHUNK], U32) for c in range(2) for j in range(2)}
@@ -194,11 +196,11 @@ def tile_picked_fisher8_none_po_kernel(
             gain = g1_sb[:].unsqueeze(1).unsqueeze(3).broadcast_to([P, CHUNK // 2, SLOTS, 2])
             nc.vector.tensor_tensor(as_woven(woven[c, 0][:], 2), as_planar(d[:, c, :, :], 2), gain, ALU.mult)
 
-        def second_order(c):
-            gain = g2_sb[:].unsqueeze(1).broadcast_to([P, CHUNK, SLOTS])
+        def second_order(c, lo=0, hi=CHUNK):
+            gain = g2_sb[:].unsqueeze(1).broadcast_to([P, hi - lo, SLOTS])
             nc.vector.scalar_tensor_tensor(
-                woven[c, 1][:].rearrange("p (c t) -> p c t", t=SLOTS),
-                squares[c].rearrange("p (c t) -> p c t", t=SLOTS),
+                woven[c, 1][:, SLOTS * lo : SLOTS * hi].rearrange("p (c t) -> p c t", t=SLOTS),
+                squares[c][:, SLOTS * lo : SLOTS * hi].rearrange("p (c t) -> p c t", t=SLOTS),
                 -1.0, gain, ALU.add, ALU.mult,
             )
 
@@ -221,8 +223,8 @@ def tile_picked_fisher8_none_po_kernel(
                     lhsT_scale=w23_dealt_plane[SCALE_ROWS * j : P, part(t, P)],
                     rhs=codes[c, j][:].bitcast(FP8X4),
                     rhs_scale=planes[c, j][:],
-                    start=(j == 0 and t % per == 0),
-                    stop=(j == 1 and t % per == per - 1),
+                    start=(j == c and t % per == 0),
+                    stop=(j == 1 - c and t % per == per - 1),
                 )
 
         subtract(0, 0, slice(0, 1))
@@ -234,33 +236,31 @@ def tile_picked_fisher8_none_po_kernel(
             subtract(c, 2, slice(2, 4))
         for c in range(2):
             whiten(c, 1)
-        nc.vector.tensor_tensor(
-            d[:, :, 3, :], last_rs[:].rearrange("p (c n) -> p c n", c=2), late_gap[:, :, 1, :], ALU.mult
-        )
         for c in range(2):
-            whiten(c, 2)
+            nc.vector.tensor_tensor(d[:, c, 2:, :], late_rs[:, :, part(c, CHUNK)], late_gap[:, c, :, :], ALU.mult)
             square(c)
         for t in range(SLOTS):
             nc.scalar.activation(out=pairs[:, t // 2, :, t % 2], in_=d[:, 1, t, :], func=ACT.Copy, scale=g1_sb[:, t : t + 1])
-        on_scalar(
-            out=woven[1, 0][:].bitcast(U32).rearrange("p (c i u) -> p c u i", u=2, i=2),
-            in_=pairs[:].rearrange("p u c e -> p u (c e)").bitcast(U32).rearrange("p u (c i) -> p c u i", i=2),
-        )
-        deal_columns(on_vector, w23_dealt_plane[:], w23_plane[:], 1)
         first_order(0)
-        second_order(0)
+        deal_columns(on_vector, w23_dealt_plane[:], w23_plane[:], 1)
         product(0, 0)
+        second_order(0)
         product(0, 1)
-        second_order(1)
-        product(1, 0)
+        second_order(1, 0, CHUNK // 2)
+        second_order(1, CHUNK // 2, CHUNK)
+        on_vector(
+            out=woven[1, 0][:].bitcast(I32).rearrange("p (c i u) -> p c u i", u=2, i=2),
+            in_=pairs[:].rearrange("p u c e -> p u (c e)").bitcast(I32).rearrange("p u (c i) -> p c u i", i=2),
+        )
         product(1, 1)
+        product(1, 0)
 
         out_codes = sbuf("out_codes", [P, S], U32)
-        out_plane = sbuf("out_plane", [P, S], U8, "plane1_1")
+        out_plane = sbuf("out_plane", [P, S], U8, "plane1_0")
         out_rows = out_0.rearrange("(p t) n -> p t n", t=SLOTS)
         out_words = word_rows(out_1)
         results = [sbuf("result%d" % c, [P, SLOTS, CHUNK], F32) for c in range(2)]
-        rounded = [sbuf("rounded0", [P, SLOTS * CHUNK], BF16, "woven1_1"), sbuf("rounded1", [P, SLOTS * CHUNK], BF16)]
+        rounded = [sbuf("rounded0", [P, SLOTS * CHUNK], BF16, "woven1_0"), sbuf("rounded1", [P, SLOTS * CHUNK], BF16)]
 
         def store(c, slots):
             nc.sync.dma_start(out=out_rows[:, slots, part(c, CHUNK)], in_=results[c][:, slots, :])
@@ -277,7 +277,7 @@ def tile_picked_fisher8_none_po_kernel(
             store(0, part(b, 2))
         weave(on_vector, 0, 0, CHUNK)
         for t in range(SLOTS):
-            (on_scalar if t % 2 else on_vector)(out=results[1][:, t : t + 1, :], in_=accs[1][t][:])
+            (on_vector if t == SLOTS - 1 else on_scalar)(out=results[1][:, t : t + 1, :], in_=accs[1][t][:])
             if t % 2:
                 store(1, part(t // 2, 2))
         hand_on(0)

@@ -87,7 +87,7 @@ def tile_picked_fisher8_none_po_kernel(
         w2_raw = sbuf("w2_raw", [P, N], I32)
         w3_raw = sbuf("w3_raw", [P, N], I32)
         mu_sb = [sbuf("mu%d" % t, [P, U if t % 2 else WIDE], F32) for t in range(SLOTS)]
-        rs_sb = [sbuf("rs%d" % t, [P, WIDE if t == 2 else U], F32) for t in range(SLOTS)]
+        rs_sb = [sbuf("rs%d" % t, [P, U], F32) for t in range(SLOTS)]
         g1_sb = sbuf("g1_sb", [P, SLOTS], F32)
         g2_sb = sbuf("g2_sb", [P, SLOTS], F32)
 
@@ -120,19 +120,15 @@ def tile_picked_fisher8_none_po_kernel(
         nc.sync.dma_start(out=g2_sb[:], in_=g2.rearrange("(p t) o -> p (t o)", t=SLOTS))
 
         means = sbuf("means", [P, SLOTS, S], F32)
-        late_rs = sbuf("late_rs", [P, 2, S], F32)
-        w1_codes = sbuf("w1_codes", [P, H], U32)
+        late_rs = sbuf("late_rs", [P, 3, CHUNK], F32)
         for t in range(SLOTS):
             if t % 2:
                 for c in range(2):
                     nc.scalar.activation(out=means[:, t, part(c, CHUNK)], in_=mu_sb[t][:].indirect(entries(k1_sb, c)), func=ACT.Copy)
             else:
                 nc.scalar.activation(out=means[:, t, :], in_=mu_sb[t][:].indirect(k1_sb[:]), func=ACT.Copy)
-            if t == 0:
-                deal_columns(on_scalar, w1_codes[:], w1_raw[:].bitcast(U32), 4)
-        nc.scalar.activation(out=late_rs[:, 0, :], in_=rs_sb[2][:].indirect(k1_sb[:]), func=ACT.Copy)
-        for c in range(2):
-            nc.scalar.activation(out=late_rs[:, 1, part(c, CHUNK)], in_=rs_sb[3][:].indirect(entries(k1_sb, c)), func=ACT.Copy)
+        for i, (c, t) in enumerate(((0, 2), (0, 3), (1, 3))):
+            nc.scalar.activation(out=late_rs[:, i, :], in_=rs_sb[t][:].indirect(entries(k1_sb, c)), func=ACT.Copy)
         w_codes = [sbuf("w2_codes", [P, N], U32), sbuf("w3_codes", [P, N], U32)]
         deal_columns(on_scalar, w_codes[0][:], w2_raw[:].bitcast(U32), 4)
         deal_columns(on_scalar, w_codes[1][:], w3_raw[:].bitcast(U32), 4)
@@ -148,7 +144,9 @@ def tile_picked_fisher8_none_po_kernel(
         w1_dealt_plane = sbuf("w1_dealt_plane", [P, H], U8)
         picked = [pick(0)]
         deal_columns(on_vector, w1_dealt_plane[:], w1_plane[:], 1)
-        picked.append(pick(1, "w1_plane"))
+        w1_codes = sbuf("w1_codes", [P, H], I32)
+        deal_columns(on_vector, w1_codes[:], w1_raw[:], 4)
+        picked.append(pick(1, "w1_raw"))
 
         def first_product(out, c, t):
             nc.tensor.matmul_mx(
@@ -181,7 +179,7 @@ def tile_picked_fisher8_none_po_kernel(
         def whiten(c, t):
             cols = part(c, CHUNK)
             factor = rs_sb[t][:].indirect(entries(k1_sb, c))
-            nc.vector.tensor_tensor(d[:, c, t, :], factor, gap[:, t, cols], ALU.mult)
+            nc.vector.tensor_tensor(d[:, c, t, :], factor, gap[:, t, cols] if t < 2 else late_gap[:, c, 0, :], ALU.mult)
 
         squares = [sbuf("squares%d" % c, [P, SLOTS * CHUNK], F32, "w%d_raw" % (2 + c))[:] for c in range(2)]
         woven = {(c, j): sbuf("woven%d_%d" % (c, j), [P, SLOTS * CHUNK], BF16) for c in range(2) for j in range(2)}
@@ -236,9 +234,11 @@ def tile_picked_fisher8_none_po_kernel(
             subtract(c, 2, slice(2, 4))
         for c in range(2):
             whiten(c, 1)
-        for c in range(2):
-            nc.vector.tensor_tensor(d[:, c, 2:, :], late_rs[:, :, part(c, CHUNK)], late_gap[:, c, :, :], ALU.mult)
-            square(c)
+        whiten(1, 2)
+        nc.vector.tensor_tensor(d[:, 0, 2:, :], late_rs[:, :2, :], late_gap[:, 0, :, :], ALU.mult)
+        square(0)
+        nc.vector.tensor_tensor(d[:, 1, 3, :], late_rs[:, 2, :], late_gap[:, 1, 1, :], ALU.mult)
+        square(1)
         for t in range(SLOTS):
             nc.scalar.activation(out=pairs[:, t // 2, :, t % 2], in_=d[:, 1, t, :], func=ACT.Copy, scale=g1_sb[:, t : t + 1])
         first_order(0)
@@ -246,8 +246,8 @@ def tile_picked_fisher8_none_po_kernel(
         product(0, 0)
         second_order(0)
         product(0, 1)
-        second_order(1, 0, CHUNK // 2)
-        second_order(1, CHUNK // 2, CHUNK)
+        second_order(1, 0, CHUNK // 4)
+        second_order(1, CHUNK // 4, CHUNK)
         on_vector(
             out=woven[1, 0][:].bitcast(I32).rearrange("p (c i u) -> p c u i", u=2, i=2),
             in_=pairs[:].rearrange("p u c e -> p u (c e)").bitcast(I32).rearrange("p u (c i) -> p c u i", i=2),

@@ -107,16 +107,16 @@ def tile_picked_fisher8_none_po_kernel(
         load_words(x_sb, x_words)
         load_scale_rows(nc, w1_plane, 0, w1_scales)
         load_words(w1_raw, w1_words)
-        for tiles, table, t in (
-            (mu_sb, mu, 1), (rs_sb, rs, 0), (mu_sb, mu, 2), (mu_sb, mu, 3), (rs_sb, rs, 1), (rs_sb, rs, 2), (rs_sb, rs, 3)
-        ):
+        for tiles, table, t in ((mu_sb, mu, 1), (rs_sb, rs, 0), (mu_sb, mu, 2), (mu_sb, mu, 3)):
             load_table(tiles, table, t)
+        load_scale_rows(nc, w23_plane, 0, w2_scales, range(SCALE_ROWS - 1))
+        for t in range(1, SLOTS):
+            load_table(rs_sb, rs, t)
         load_words(w2_raw, w2_words)
         load_words(w3_raw, w3_words)
-        load_scale_rows(nc, w23_plane, 0, w2_scales)
-        load_scale_rows(nc, w23_plane, SCALE_ROWS, w3_scales, range(SCALE_ROWS - 1))
+        load_scale_rows(nc, w23_plane, SCALE_ROWS, w3_scales)
         nc.sync.dma_start(out=g1_sb[:], in_=g1.rearrange("(p t) o -> p (t o)", t=SLOTS))
-        load_scale_rows(nc, w23_plane, SCALE_ROWS, w3_scales, (SCALE_ROWS - 1,))
+        load_scale_rows(nc, w23_plane, 0, w2_scales, (SCALE_ROWS - 1,))
         nc.sync.dma_start(out=g2_sb[:], in_=g2.rearrange("(p t) o -> p (t o)", t=SLOTS))
 
         means = sbuf("means", [P, SLOTS, S], F32)

@@ -1,6 +1,7 @@
 from contextlib import ExitStack
 
 import concourse.mybir as mybir
+from concourse.masks import make_identity
 
 K, T, S, N, H, U = 512, 2048, 512, 512, 512, 512
 FLOPS = 2 * S * (K * H + 2 * H * N)
@@ -24,6 +25,7 @@ LINE = 16
 CHUNK = 256
 WIDE = 2 * U
 VECTOR_ROUNDS_LAST = 176
+G2_COLUMN = 8
 
 
 def word_rows(words):
@@ -88,11 +90,12 @@ def tile_picked_fisher8_none_po_kernel(
         w3_raw = sbuf("w3_raw", [P, N], I32)
         mu_sb = [sbuf("mu%d" % t, [P, U if t % 2 else WIDE], F32) for t in range(SLOTS)]
         rs_sb = [sbuf("rs%d" % t, [P, U], F32) for t in range(SLOTS)]
-        g1_sb = sbuf("g1_sb", [P, SLOTS], F32)
-        g2_sb = sbuf("g2_sb", [P, SLOTS], F32)
+        gains = sbuf("gains", [P, P], F32)
+        g1_sb, g2_sb = gains[:, :SLOTS], gains[:, G2_COLUMN : G2_COLUMN + SLOTS]
 
         for plane in (x_plane, w1_plane, w23_plane):
             nc.vector.memset(plane[:].bitcast(I32), 0)
+        nc.vector.memset(gains[:], 0.0)
 
         def load_table(tiles, table, t):
             nc.sync.dma_start(out=tiles[t][:, :U], in_=table.rearrange("(p t) u -> p t u", t=SLOTS)[:, t, :])
@@ -109,29 +112,29 @@ def tile_picked_fisher8_none_po_kernel(
         load_words(w1_raw, w1_words)
         for tiles, table, t in ((mu_sb, mu, 1), (rs_sb, rs, 0), (mu_sb, mu, 2), (mu_sb, mu, 3)):
             load_table(tiles, table, t)
-        load_scale_rows(nc, w23_plane, 0, w2_scales, range(SCALE_ROWS - 1))
+        nc.sync.dma_start(out=g1_sb, in_=g1.rearrange("(p t) o -> p (t o)", t=SLOTS))
+        nc.sync.dma_start(out=g2_sb, in_=g2.rearrange("(p t) o -> p (t o)", t=SLOTS))
+        load_scale_rows(nc, w23_plane, 0, w2_scales, range(1))
         for t in range(1, SLOTS):
             load_table(rs_sb, rs, t)
         load_words(w2_raw, w2_words)
         load_words(w3_raw, w3_words)
+        load_scale_rows(nc, w23_plane, 0, w2_scales, range(1, SCALE_ROWS))
         load_scale_rows(nc, w23_plane, SCALE_ROWS, w3_scales)
-        nc.sync.dma_start(out=g1_sb[:], in_=g1.rearrange("(p t) o -> p (t o)", t=SLOTS))
-        load_scale_rows(nc, w23_plane, 0, w2_scales, (SCALE_ROWS - 1,))
-        nc.sync.dma_start(out=g2_sb[:], in_=g2.rearrange("(p t) o -> p (t o)", t=SLOTS))
 
         means = sbuf("means", [P, SLOTS, S], F32)
-        late_rs = sbuf("late_rs", [P, 3, CHUNK], F32)
+        late_rs = sbuf("late_rs", [P, CHUNK], F32)
+        d = [sbuf("d0", [P, SLOTS, CHUNK], F32), sbuf("d1", [P, SLOTS + 1, CHUNK], F32)]
         for t in range(SLOTS):
             if t % 2:
                 for c in range(2):
                     nc.scalar.activation(out=means[:, t, part(c, CHUNK)], in_=mu_sb[t][:].indirect(entries(k1_sb, c)), func=ACT.Copy)
             else:
                 nc.scalar.activation(out=means[:, t, :], in_=mu_sb[t][:].indirect(k1_sb[:]), func=ACT.Copy)
-        for i, (c, t) in enumerate(((0, 2), (0, 3), (1, 3))):
-            nc.scalar.activation(out=late_rs[:, i, :], in_=rs_sb[t][:].indirect(entries(k1_sb, c)), func=ACT.Copy)
-        w_codes = [sbuf("w2_codes", [P, N], U32), sbuf("w3_codes", [P, N], U32)]
-        deal_columns(on_scalar, w_codes[0][:], w2_raw[:].bitcast(U32), 4)
-        deal_columns(on_scalar, w_codes[1][:], w3_raw[:].bitcast(U32), 4)
+        for out, c, t in ((d[1][:, 2, :], 0, 2), (d[1][:, SLOTS, :], 0, 3), (late_rs[:], 1, 3)):
+            nc.scalar.activation(out=out, in_=rs_sb[t][:].indirect(entries(k1_sb, c)), func=ACT.Copy)
+        identity = sbuf("identity", [P, P], F32, "mu0")
+        make_identity(nc, identity[:])
 
         picked_plane = sbuf("picked_plane", [P, S], U8)
         on_vector(out=picked_plane[:], in_=x_plane[:].indirect(offs_sb[:]))
@@ -168,7 +171,6 @@ def tile_picked_fisher8_none_po_kernel(
 
         gap = sbuf("gap", [P, 2, S], F32)
         late_gap = sbuf("late_gap", [P, 2, 2, CHUNK], F32)
-        d = sbuf("d", [P, 2, SLOTS, CHUNK], F32)
 
         def subtract(c, first, slots):
             cols = part(c, CHUNK)
@@ -179,23 +181,22 @@ def tile_picked_fisher8_none_po_kernel(
         def whiten(c, t):
             cols = part(c, CHUNK)
             factor = rs_sb[t][:].indirect(entries(k1_sb, c))
-            nc.vector.tensor_tensor(d[:, c, t, :], factor, gap[:, t, cols] if t < 2 else late_gap[:, c, 0, :], ALU.mult)
+            nc.vector.tensor_tensor(d[c][:, t, :], factor, gap[:, t, cols] if t < 2 else late_gap[:, c, 0, :], ALU.mult)
 
-        squares = [sbuf("squares%d" % c, [P, SLOTS * CHUNK], F32, "w%d_raw" % (2 + c))[:] for c in range(2)]
+        squares = [sbuf("squares%d" % c, [P, SLOTS * CHUNK], F32)[:] for c in range(2)]
         woven = {(c, j): sbuf("woven%d_%d" % (c, j), [P, SLOTS * CHUNK], BF16) for c in range(2) for j in range(2)}
-        pairs = sbuf("pairs", [P, 2, CHUNK, 2], BF16)
         codes = {(c, j): sbuf("codes%d_%d" % (c, j), [P, CHUNK], U32) for c in range(2) for j in range(2)}
         planes = {(c, j): sbuf("plane%d_%d" % (c, j), [P, CHUNK], U8) for c in range(2) for j in range(2)}
 
         def square(c):
-            nc.scalar.activation(out=as_woven(squares[c], 2), in_=as_planar(d[:, c, :, :], 2), func=ACT.Square)
+            nc.scalar.activation(out=as_woven(squares[c], 2), in_=as_planar(d[c][:, :SLOTS, :], 2), func=ACT.Square)
 
         def first_order(c):
-            gain = g1_sb[:].unsqueeze(1).unsqueeze(3).broadcast_to([P, CHUNK // 2, SLOTS, 2])
-            nc.vector.tensor_tensor(as_woven(woven[c, 0][:], 2), as_planar(d[:, c, :, :], 2), gain, ALU.mult)
+            gain = gains_psum[:, :SLOTS].unsqueeze(1).unsqueeze(3).broadcast_to([P, CHUNK // 2, SLOTS, 2])
+            nc.vector.tensor_tensor(as_woven(woven[c, 0][:], 2), as_planar(d[c][:, :SLOTS, :], 2), gain, ALU.mult)
 
         def second_order(c, lo=0, hi=CHUNK):
-            gain = g2_sb[:].unsqueeze(1).broadcast_to([P, hi - lo, SLOTS])
+            gain = gains_psum[:, G2_COLUMN : G2_COLUMN + SLOTS].unsqueeze(1).broadcast_to([P, hi - lo, SLOTS])
             nc.vector.scalar_tensor_tensor(
                 woven[c, 1][:, SLOTS * lo : SLOTS * hi].rearrange("p (c t) -> p c t", t=SLOTS),
                 squares[c][:, SLOTS * lo : SLOTS * hi].rearrange("p (c t) -> p c t", t=SLOTS),
@@ -204,17 +205,18 @@ def tile_picked_fisher8_none_po_kernel(
 
         accs = [
             [bank(5 + b, "out0_%d" % b, [P, 2, CHUNK]) for b in range(2)],
-            [bank((7 + t) % 8, "out1_%d" % t, [P, 1, CHUNK]) for t in range(SLOTS)],
+            [bank((3 + t) % 4, "out1_%d" % t, [P, 1, CHUNK]) for t in range(SLOTS)],
         ]
-        w23_dealt_plane = sbuf("w23_dealt_plane", [P, N], U8)
 
         def quantise(out_codes, plane, values):
             nc.vector.quantize_mx(out=out_codes.bitcast(FP8X4), scales=plane, in_=values)
 
-        def product(c, j):
+        def operand(c, j):
             quantise(codes[c, j][:], planes[c, j][:], woven[c, j][:])
+
+        def passes(c, j, slots):
             per = SLOTS // len(accs[c])
-            for t in range(SLOTS):
+            for t in slots:
                 nc.tensor.matmul_mx(
                     out=accs[c][t // per][:, t % per, :],
                     lhsT=w_codes[j][:, part(t, P)].bitcast(FP8X4),
@@ -232,28 +234,43 @@ def tile_picked_fisher8_none_po_kernel(
         whiten(1, 0)
         for c in range(2):
             subtract(c, 2, slice(2, 4))
+        turns = bank(7, "turns", [P, 2, P])
+        turned = sbuf("turned", [P, P], F32)
+        nc.tensor.transpose(turns[:, 0, :], gains[:], identity[:])
+        on_scalar(out=turned[:], in_=turns[:, 0, :])
+        nc.tensor.transpose(turns[:, 1, :], turned[:], identity[:])
+        gains_psum = turns[:, 1, :]
         for c in range(2):
             whiten(c, 1)
-        whiten(1, 2)
-        nc.vector.tensor_tensor(d[:, 0, 2:, :], late_rs[:, :2, :], late_gap[:, 0, :, :], ALU.mult)
+        nc.vector.tensor_tensor(d[0][:, 2:, :], d[1][:, 2 : SLOTS + 1 : 2, :], late_gap[:, 0, :, :], ALU.mult)
         square(0)
-        nc.vector.tensor_tensor(d[:, 1, 3, :], late_rs[:, 2, :], late_gap[:, 1, 1, :], ALU.mult)
+        nc.vector.tensor_tensor(d[1][:, 3, :], late_rs[:], late_gap[:, 1, 1, :], ALU.mult)
+        whiten(1, 2)
         square(1)
-        for t in range(SLOTS):
-            nc.scalar.activation(out=pairs[:, t // 2, :, t % 2], in_=d[:, 1, t, :], func=ACT.Copy, scale=g1_sb[:, t : t + 1])
+        w_dealt = sbuf("w_dealt", [P, 2, N], I32, "rs2")
+        w_codes = [w_dealt[:, 0, :], w_dealt[:, 1, :]]
+        w23_dealt_plane = sbuf("w23_dealt_plane", [P, N], U8, "late_gap")
+        deal_columns(nc.gpsimd.tensor_copy, w_codes[0], w2_raw[:], 4)
+        deal_columns(nc.gpsimd.tensor_copy, w23_dealt_plane[:], w23_plane[:], 1)
+        deal_columns(nc.gpsimd.tensor_copy, w_codes[1], w3_raw[:], 4)
         first_order(0)
-        deal_columns(on_vector, w23_dealt_plane[:], w23_plane[:], 1)
-        product(0, 0)
         second_order(0)
-        product(0, 1)
-        second_order(1, 0, CHUNK // 4)
-        second_order(1, CHUNK // 4, CHUNK)
-        on_vector(
-            out=woven[1, 0][:].bitcast(I32).rearrange("p (c i u) -> p c u i", u=2, i=2),
-            in_=pairs[:].rearrange("p u c e -> p u (c e)").bitcast(I32).rearrange("p u (c i) -> p c u i", i=2),
+        pairs = sbuf("pairs", [P, 2, CHUNK, 2], BF16, "d0")
+        for t in range(SLOTS):
+            nc.scalar.activation(out=pairs[:, t // 2, :, t % 2], in_=d[1][:, t, :], func=ACT.Copy, scale=g1_sb[:, t : t + 1])
+        operand(0, 0)
+        operand(0, 1)
+        for b in range(2):
+            for j in range(2):
+                passes(0, j, range(2 * b, 2 * b + 2))
+        second_order(1)
+        on_scalar(
+            out=woven[1, 0][:].bitcast(U32).rearrange("p (c i u) -> p c u i", u=2, i=2),
+            in_=pairs[:].rearrange("p u c e -> p u (c e)").bitcast(U32).rearrange("p u (c i) -> p c u i", i=2),
         )
-        product(1, 1)
-        product(1, 0)
+        for j in (1, 0):
+            operand(1, j)
+            passes(1, j, range(SLOTS))
 
         out_codes = sbuf("out_codes", [P, S], U32)
         out_plane = sbuf("out_plane", [P, S], U8, "plane1_0")

@@ -115,9 +115,9 @@ def tile_picked_fisher8_none_po_kernel(
         nc.sync.dma_start(out=g1_sb, in_=g1.rearrange("(p t) o -> p (t o)", t=SLOTS))
         nc.sync.dma_start(out=g2_sb, in_=g2.rearrange("(p t) o -> p (t o)", t=SLOTS))
         load_scale_rows(nc, w23_plane, 0, w2_scales, range(1))
+        load_words(w2_raw, w2_words)
         for t in range(1, SLOTS):
             load_table(rs_sb, rs, t)
-        load_words(w2_raw, w2_words)
         load_words(w3_raw, w3_words)
         load_scale_rows(nc, w23_plane, 0, w2_scales, range(1, SCALE_ROWS))
         load_scale_rows(nc, w23_plane, SCALE_ROWS, w3_scales)
@@ -232,6 +232,8 @@ def tile_picked_fisher8_none_po_kernel(
         subtract(1, 0, slice(0, 2))
         whiten(0, 0)
         whiten(1, 0)
+        w_codes = [sbuf("w2_codes", [P, N], I32, "rs0")[:]]
+        deal_columns(nc.gpsimd.tensor_copy, w_codes[0], w2_raw[:], 4)
         for c in range(2):
             subtract(c, 2, slice(2, 4))
         turns = bank(7, "turns", [P, 2, P])
@@ -247,23 +249,22 @@ def tile_picked_fisher8_none_po_kernel(
         nc.vector.tensor_tensor(d[1][:, 3, :], late_rs[:], late_gap[:, 1, 1, :], ALU.mult)
         whiten(1, 2)
         square(1)
-        w_dealt = sbuf("w_dealt", [P, 2, N], I32, "rs2")
-        w_codes = [w_dealt[:, 0, :], w_dealt[:, 1, :]]
+        w_codes.append(sbuf("w3_codes", [P, N], I32, "rs2")[:])
         w23_dealt_plane = sbuf("w23_dealt_plane", [P, N], U8, "late_gap")
-        deal_columns(nc.gpsimd.tensor_copy, w_codes[0], w2_raw[:], 4)
-        deal_columns(nc.gpsimd.tensor_copy, w23_dealt_plane[:], w23_plane[:], 1)
         deal_columns(nc.gpsimd.tensor_copy, w_codes[1], w3_raw[:], 4)
+        deal_columns(nc.gpsimd.tensor_copy, w23_dealt_plane[:], w23_plane[:], 1)
         first_order(0)
-        second_order(0)
+        second_order(0, 0, CHUNK // 4)
         pairs = sbuf("pairs", [P, 2, CHUNK, 2], BF16, "d0")
         for t in range(SLOTS):
             nc.scalar.activation(out=pairs[:, t // 2, :, t % 2], in_=d[1][:, t, :], func=ACT.Copy, scale=g1_sb[:, t : t + 1])
         operand(0, 0)
+        passes(0, 0, range(SLOTS))
+        second_order(0, CHUNK // 4, CHUNK)
+        second_order(1, 0, CHUNK // 4)
         operand(0, 1)
-        for b in range(2):
-            for j in range(2):
-                passes(0, j, range(2 * b, 2 * b + 2))
-        second_order(1)
+        passes(0, 1, range(SLOTS))
+        second_order(1, CHUNK // 4, CHUNK)
         on_scalar(
             out=woven[1, 0][:].bitcast(U32).rearrange("p (c i u) -> p c u i", u=2, i=2),
             in_=pairs[:].rearrange("p u c e -> p u (c e)").bitcast(U32).rearrange("p u (c i) -> p c u i", i=2),

@@ -23,6 +23,7 @@ SCALE_ROWS = 4
 GROUP = 16
 LINE = 16
 CHUNK = 256
+UNIT = 128
 WIDE = 2 * U
 VECTOR_ROUNDS_LAST = 176
 G2_COLUMN = 8
@@ -204,28 +205,31 @@ def tile_picked_fisher8_none_po_kernel(
             )
 
         accs = [
-            [bank(5 + b, "out0_%d" % b, [P, 2, CHUNK]) for b in range(2)],
+            [bank(5 + a, "out0_%d" % a, [P, SLOTS, UNIT]) for a in range(2)],
             [bank((3 + t) % 4, "out1_%d" % t, [P, 1, CHUNK]) for t in range(SLOTS)],
         ]
 
         def quantise(out_codes, plane, values):
             nc.vector.quantize_mx(out=out_codes.bitcast(FP8X4), scales=plane, in_=values)
 
-        def operand(c, j):
-            quantise(codes[c, j][:], planes[c, j][:], woven[c, j][:])
+        def operand(c, j, cols=slice(0, CHUNK)):
+            values = woven[c, j][:, SLOTS * cols.start : SLOTS * cols.stop]
+            quantise(codes[c, j][:, cols], planes[c, j][:, cols], values)
 
-        def passes(c, j, slots):
-            per = SLOTS // len(accs[c])
-            for t in slots:
+        def passes(outs, c, j, cols, opens, shared):
+            for t in range(SLOTS):
                 nc.tensor.matmul_mx(
-                    out=accs[c][t // per][:, t % per, :],
+                    out=outs[t],
                     lhsT=w_codes[j][:, part(t, P)].bitcast(FP8X4),
                     lhsT_scale=w23_dealt_plane[SCALE_ROWS * j : P, part(t, P)],
-                    rhs=codes[c, j][:].bitcast(FP8X4),
-                    rhs_scale=planes[c, j][:],
-                    start=(j == c and t % per == 0),
-                    stop=(j == 1 - c and t % per == per - 1),
+                    rhs=codes[c, j][:, cols].bitcast(FP8X4),
+                    rhs_scale=planes[c, j][:, cols],
+                    start=(opens and (t == 0 or not shared)),
+                    stop=(not opens and (t == SLOTS - 1 or not shared)),
                 )
+
+        def unit_passes(a, j):
+            passes([accs[0][a][:, t, :] for t in range(SLOTS)], 0, j, part(a, UNIT), j == 0, True)
 
         subtract(0, 0, slice(0, 1))
         subtract(0, 1, slice(1, 2))
@@ -254,16 +258,19 @@ def tile_picked_fisher8_none_po_kernel(
         deal_columns(nc.gpsimd.tensor_copy, w_codes[1], w3_raw[:], 4)
         deal_columns(nc.gpsimd.tensor_copy, w23_dealt_plane[:], w23_plane[:], 1)
         first_order(0)
-        second_order(0, 0, CHUNK // 4)
+        second_order(0, 0, UNIT)
         pairs = sbuf("pairs", [P, 2, CHUNK, 2], BF16, "d0")
         for t in range(SLOTS):
             nc.scalar.activation(out=pairs[:, t // 2, :, t % 2], in_=d[1][:, t, :], func=ACT.Copy, scale=g1_sb[:, t : t + 1])
         operand(0, 0)
-        passes(0, 0, range(SLOTS))
-        second_order(0, CHUNK // 4, CHUNK)
+        unit_passes(0, 0)
+        second_order(0, UNIT, CHUNK)
+        operand(0, 1, part(0, UNIT))
+        unit_passes(0, 1)
+        unit_passes(1, 0)
         second_order(1, 0, CHUNK // 4)
-        operand(0, 1)
-        passes(0, 1, range(SLOTS))
+        operand(0, 1, part(1, UNIT))
+        unit_passes(1, 1)
         second_order(1, CHUNK // 4, CHUNK)
         on_scalar(
             out=woven[1, 0][:].bitcast(U32).rearrange("p (c i u) -> p c u i", u=2, i=2),
@@ -271,13 +278,14 @@ def tile_picked_fisher8_none_po_kernel(
         )
         for j in (1, 0):
             operand(1, j)
-            passes(1, j, range(SLOTS))
+            passes([accs[1][t][:, 0, :] for t in range(SLOTS)], 1, j, slice(0, CHUNK), j == 1, False)
 
         out_codes = sbuf("out_codes", [P, S], U32)
         out_plane = sbuf("out_plane", [P, S], U8, "plane1_0")
         out_rows = out_0.rearrange("(p t) n -> p t n", t=SLOTS)
         out_words = word_rows(out_1)
-        results = [sbuf("result%d" % c, [P, SLOTS, CHUNK], F32) for c in range(2)]
+        early = sbuf("early", [P, 2, SLOTS, UNIT], F32)
+        results = [None, sbuf("result1", [P, SLOTS, CHUNK], F32)]
         rounded = [sbuf("rounded0", [P, SLOTS * CHUNK], BF16, "woven1_0"), sbuf("rounded1", [P, SLOTS * CHUNK], BF16)]
 
         def store(c, slots):
@@ -290,10 +298,11 @@ def tile_picked_fisher8_none_po_kernel(
             quantise(out_codes[:, part(c, CHUNK)], out_plane[:, part(c, CHUNK)], rounded[c][:])
             nc.sync.dma_start(out=out_words[:, part(c, CHUNK)], in_=out_codes[:, part(c, CHUNK)].bitcast(I32))
 
-        for b in range(2):
-            on_scalar(out=results[0][:, part(b, 2), :], in_=accs[0][b][:])
-            store(0, part(b, 2))
-        weave(on_vector, 0, 0, CHUNK)
+        for a in range(2):
+            on_scalar(out=early[:, a, :, :], in_=accs[0][a][:])
+            nc.sync.dma_start(out=out_rows[:, :, part(a, UNIT)], in_=early[:, a, :, :])
+        for a in range(2):
+            on_vector(out=as_woven(rounded[0][:, part(a, SLOTS * UNIT)], 4), in_=as_planar(early[:, a, :, :], 4))
         for t in range(SLOTS):
             (on_vector if t == SLOTS - 1 else on_scalar)(out=results[1][:, t : t + 1, :], in_=accs[1][t][:])
             if t % 2:

from contextlib import ExitStack

import concourse.mybir as mybir
from concourse.masks import make_identity

K, T, S, N, H, U = 512, 2048, 512, 512, 512, 512
FLOPS = 2 * S * (K * H + 2 * H * N)

F32 = mybir.dt.float32
BF16 = mybir.dt.bfloat16
I32 = mybir.dt.int32
U32 = mybir.dt.uint32
U16 = mybir.dt.uint16
U8 = mybir.dt.uint8
FP8X4 = mybir.dt.float8_e4m3fn_x4
ALU = mybir.AluOpType
ACT = mybir.ActivationFunctionType

P = 128
SLOTS = 4
QUADRANT = 32
SCALE_ROWS = 4
GROUP = 16
LINE = 16
CHUNK = 256
UNIT = 128
WIDE = 2 * U
VECTOR_ROUNDS_LAST = 176
G2_COLUMN = 8


def word_rows(words):
    return words[0].rearrange("p c r -> p (c r)").bitcast(I32)


def load_scale_rows(nc, plane, first, scales, rows=range(SCALE_ROWS)):
    for r in rows:
        nc.sync.dma_start(
            out=plane[first + r : P : QUADRANT, :].bitcast(I32),
            in_=scales[0, r : SCALE_ROWS * (P // QUADRANT) : SCALE_ROWS, :].bitcast(I32),
        )


def deal_columns(copy, dealt, raw, element_bytes):
    run = LINE // element_bytes
    copy(
        out=dealt.rearrange("p (t c i) -> p c t i", t=SLOTS, i=run),
        in_=raw.rearrange("p (c i t) -> p c t i", t=SLOTS, i=run),
    )


def as_woven(woven, run):
    return woven.rearrange("p (c i t) -> p c t i", t=SLOTS, i=run)


def as_planar(planar, run):
    return planar.rearrange("p t (c i) -> p c t i", i=run)


def tile_picked_fisher8_none_po_kernel(
    tc, x_words, x_scales, w1_words, w1_scales, mu, rs, g1, g2, w2_words, w2_scales, w3_words, w3_scales,
    offs, k1, out_0, out_1, out_2,
):
    nc = tc.nc
    on_vector, on_scalar = nc.vector.tensor_copy, nc.scalar.copy

    with ExitStack() as ctx:
        keep = ctx.enter_context(tc.tile_pool(name="keep", bufs=1))
        psum = ctx.enter_context(tc.psum_pool(name="psum", bufs=1))

        def sbuf(name, shape, dtype, tag=None):
            return keep.tile(shape, dtype, name=name, tag=tag or name, align_bytes=64)

        def bank(b, name, shape):
            return psum.tile(shape, F32, name=name, tag="bank%d" % b)

        def entries(list_tile, c):
            return list_tile[:, c * CHUNK // GROUP : (c + 1) * CHUNK // GROUP]

        def part(i, width):
            return slice(i * width, (i + 1) * width)

        offs_sb = sbuf("offs_sb", [P, S // GROUP], U16)
        k1_sb = sbuf("k1_sb", [P, S // GROUP], U16)
        x_plane = sbuf("x_plane", [P, T], U8)
        w1_plane = sbuf("w1_plane", [P, H], U8)
        w23_plane = sbuf("w23_plane", [P, N], U8)
        x_sb = sbuf("x_sb", [P, T], I32)
        w1_raw = sbuf("w1_raw", [P, H], I32)
        w2_raw = sbuf("w2_raw", [P, N], I32)
        w3_raw = sbuf("w3_raw", [P, N], I32)
        mu_sb = [sbuf("mu%d" % t, [P, U if t % 2 else WIDE], F32) for t in range(SLOTS)]
        rs_sb = [sbuf("rs%d" % t, [P, U], F32) for t in range(SLOTS)]
        gains = sbuf("gains", [P, P], F32)
        g1_sb, g2_sb = gains[:, :SLOTS], gains[:, G2_COLUMN : G2_COLUMN + SLOTS]

        for plane in (x_plane, w1_plane, w23_plane):
            nc.vector.memset(plane[:].bitcast(I32), 0)
        nc.vector.memset(gains[:], 0.0)

        def load_table(tiles, table, t):
            nc.sync.dma_start(out=tiles[t][:, :U], in_=table.rearrange("(p t) u -> p t u", t=SLOTS)[:, t, :])

        def load_words(raw, words):
            nc.sync.dma_start(out=raw[:], in_=word_rows(words))

        nc.sync.dma_start(k1_sb[:], k1)
        load_table(mu_sb, mu, 0)
        nc.sync.dma_start(offs_sb[:], offs)
        load_scale_rows(nc, x_plane, 0, x_scales)
        load_words(x_sb, x_words)
        load_scale_rows(nc, w1_plane, 0, w1_scales)
        load_words(w1_raw, w1_words)
        for tiles, table, t in ((mu_sb, mu, 1), (rs_sb, rs, 0), (mu_sb, mu, 2), (mu_sb, mu, 3)):
            load_table(tiles, table, t)
        nc.sync.dma_start(out=g1_sb, in_=g1.rearrange("(p t) o -> p (t o)", t=SLOTS))
        nc.sync.dma_start(out=g2_sb, in_=g2.rearrange("(p t) o -> p (t o)", t=SLOTS))
        load_scale_rows(nc, w23_plane, 0, w2_scales, range(1))
        load_words(w2_raw, w2_words)
        for t in range(1, SLOTS):
            load_table(rs_sb, rs, t)
        load_words(w3_raw, w3_words)
        load_scale_rows(nc, w23_plane, 0, w2_scales, range(1, SCALE_ROWS))
        load_scale_rows(nc, w23_plane, SCALE_ROWS, w3_scales)

        means = sbuf("means", [P, SLOTS, S], F32)
        late_rs = sbuf("late_rs", [P, CHUNK], F32)
        d = [sbuf("d0", [P, SLOTS, CHUNK], F32), sbuf("d1", [P, SLOTS + 1, CHUNK], F32)]
        for t in range(SLOTS):
            if t % 2:
                for c in range(2):
                    nc.scalar.activation(out=means[:, t, part(c, CHUNK)], in_=mu_sb[t][:].indirect(entries(k1_sb, c)), func=ACT.Copy)
            else:
                nc.scalar.activation(out=means[:, t, :], in_=mu_sb[t][:].indirect(k1_sb[:]), func=ACT.Copy)
        for out, c, t in ((d[1][:, 2, :], 0, 2), (d[1][:, SLOTS, :], 0, 3), (late_rs[:], 1, 3)):
            nc.scalar.activation(out=out, in_=rs_sb[t][:].indirect(entries(k1_sb, c)), func=ACT.Copy)
        identity = sbuf("identity", [P, P], F32, "mu0")
        make_identity(nc, identity[:])

        picked_plane = sbuf("picked_plane", [P, S], U8)
        on_vector(out=picked_plane[:], in_=x_plane[:].indirect(offs_sb[:]))

        def pick(c, tag=None):
            words = sbuf("picked%d" % c, [P, CHUNK], U32, tag)
            on_vector(out=words[:], in_=x_sb[:].bitcast(U32).indirect(entries(offs_sb, c)))
            return words

        w1_dealt_plane = sbuf("w1_dealt_plane", [P, H], U8)
        picked = [pick(0)]
        deal_columns(on_vector, w1_dealt_plane[:], w1_plane[:], 1)
        w1_codes = sbuf("w1_codes", [P, H], I32)
        deal_columns(on_vector, w1_codes[:], w1_raw[:], 4)
        picked.append(pick(1, "w1_raw"))

        def first_product(out, c, t):
            nc.tensor.matmul_mx(
                out=out,
                lhsT=w1_codes[:, part(t, P)].bitcast(FP8X4),
                lhsT_scale=w1_dealt_plane[:, part(t, P)],
                rhs=picked[c][:].bitcast(FP8X4),
                rhs_scale=picked_plane[:, part(c, CHUNK)],
                start=True,
                stop=True,
            )

        units = ((0, (0,)), (0, (1,)), (1, (0, 1)), (0, (2, 3)), (1, (2, 3)))
        y = {}
        for b, (c, slots) in enumerate(units):
            y[c, slots[0]] = bank(b, "y%d_%d" % (c, slots[0]), [P, len(slots), CHUNK])
            for j, t in enumerate(slots):
                first_product(y[c, slots[0]][:, j, :], c, t)

        gap = sbuf("gap", [P, 2, S], F32)
        late_gap = sbuf("late_gap", [P, 2, 2, CHUNK], F32)

        def subtract(c, first, slots):
            cols = part(c, CHUNK)
            out = late_gap[:, c, :, :] if first == 2 else gap[:, slots, cols]
            held = y[c, first][:, slots.start - first : slots.stop - first, :]
            nc.vector.tensor_tensor(out, held, means[:, slots, cols], ALU.subtract)

        def whiten(c, t):
            cols = part(c, CHUNK)
            factor = rs_sb[t][:].indirect(entries(k1_sb, c))
            nc.vector.tensor_tensor(d[c][:, t, :], factor, gap[:, t, cols] if t < 2 else late_gap[:, c, 0, :], ALU.mult)

        squares = [sbuf("squares%d" % c, [P, SLOTS * CHUNK], F32)[:] for c in range(2)]
        woven = {(c, j): sbuf("woven%d_%d" % (c, j), [P, SLOTS * CHUNK], BF16) for c in range(2) for j in range(2)}
        codes = {(c, j): sbuf("codes%d_%d" % (c, j), [P, CHUNK], U32) for c in range(2) for j in range(2)}
        planes = {(c, j): sbuf("plane%d_%d" % (c, j), [P, CHUNK], U8) for c in range(2) for j in range(2)}

        def square(c):
            nc.scalar.activation(out=as_woven(squares[c], 2), in_=as_planar(d[c][:, :SLOTS, :], 2), func=ACT.Square)

        def first_order(c):
            gain = gains_psum[:, :SLOTS].unsqueeze(1).unsqueeze(3).broadcast_to([P, CHUNK // 2, SLOTS, 2])
            nc.vector.tensor_tensor(as_woven(woven[c, 0][:], 2), as_planar(d[c][:, :SLOTS, :], 2), gain, ALU.mult)

        def second_order(c, lo=0, hi=CHUNK):
            gain = gains_psum[:, G2_COLUMN : G2_COLUMN + SLOTS].unsqueeze(1).broadcast_to([P, hi - lo, SLOTS])
            nc.vector.scalar_tensor_tensor(
                woven[c, 1][:, SLOTS * lo : SLOTS * hi].rearrange("p (c t) -> p c t", t=SLOTS),
                squares[c][:, SLOTS * lo : SLOTS * hi].rearrange("p (c t) -> p c t", t=SLOTS),
                -1.0, gain, ALU.add, ALU.mult,
            )

        accs = [
            [bank(5 + a, "out0_%d" % a, [P, SLOTS, UNIT]) for a in range(2)],
            [bank((3 + t) % 4, "out1_%d" % t, [P, 1, CHUNK]) for t in range(SLOTS)],
        ]

        def quantise(out_codes, plane, values):
            nc.vector.quantize_mx(out=out_codes.bitcast(FP8X4), scales=plane, in_=values)

        def operand(c, j, cols=slice(0, CHUNK)):
            values = woven[c, j][:, SLOTS * cols.start : SLOTS * cols.stop]
            quantise(codes[c, j][:, cols], planes[c, j][:, cols], values)

        def passes(outs, c, j, cols, opens, shared):
            for t in range(SLOTS):
                nc.tensor.matmul_mx(
                    out=outs[t],
                    lhsT=w_codes[j][:, part(t, P)].bitcast(FP8X4),
                    lhsT_scale=w23_dealt_plane[SCALE_ROWS * j : P, part(t, P)],
                    rhs=codes[c, j][:, cols].bitcast(FP8X4),
                    rhs_scale=planes[c, j][:, cols],
                    start=(opens and (t == 0 or not shared)),
                    stop=(not opens and (t == SLOTS - 1 or not shared)),
                )

        def unit_passes(a, j):
            passes([accs[0][a][:, t, :] for t in range(SLOTS)], 0, j, part(a, UNIT), j == 0, True)

        subtract(0, 0, slice(0, 1))
        subtract(0, 1, slice(1, 2))
        subtract(1, 0, slice(0, 2))
        whiten(0, 0)
        whiten(1, 0)
        w_codes = [sbuf("w2_codes", [P, N], I32, "rs0")[:]]
        deal_columns(nc.gpsimd.tensor_copy, w_codes[0], w2_raw[:], 4)
        for c in range(2):
            subtract(c, 2, slice(2, 4))
        turns = bank(7, "turns", [P, 2, P])
        turned = sbuf("turned", [P, P], F32)
        nc.tensor.transpose(turns[:, 0, :], gains[:], identity[:])
        on_scalar(out=turned[:], in_=turns[:, 0, :])
        nc.tensor.transpose(turns[:, 1, :], turned[:], identity[:])
        gains_psum = turns[:, 1, :]
        for c in range(2):
            whiten(c, 1)
        nc.vector.tensor_tensor(d[0][:, 2:, :], d[1][:, 2 : SLOTS + 1 : 2, :], late_gap[:, 0, :, :], ALU.mult)
        square(0)
        nc.vector.tensor_tensor(d[1][:, 3, :], late_rs[:], late_gap[:, 1, 1, :], ALU.mult)
        whiten(1, 2)
        square(1)
        w_codes.append(sbuf("w3_codes", [P, N], I32, "rs2")[:])
        w23_dealt_plane = sbuf("w23_dealt_plane", [P, N], U8, "late_gap")
        deal_columns(nc.gpsimd.tensor_copy, w_codes[1], w3_raw[:], 4)
        deal_columns(nc.gpsimd.tensor_copy, w23_dealt_plane[:], w23_plane[:], 1)
        first_order(0)
        second_order(0, 0, UNIT)
        pairs = sbuf("pairs", [P, 2, CHUNK, 2], BF16, "d0")
        for t in range(SLOTS):
            nc.scalar.activation(out=pairs[:, t // 2, :, t % 2], in_=d[1][:, t, :], func=ACT.Copy, scale=g1_sb[:, t : t + 1])
        operand(0, 0)
        unit_passes(0, 0)
        second_order(0, UNIT, CHUNK)
        operand(0, 1, part(0, UNIT))
        unit_passes(0, 1)
        unit_passes(1, 0)
        second_order(1, 0, CHUNK // 4)
        operand(0, 1, part(1, UNIT))
        unit_passes(1, 1)
        second_order(1, CHUNK // 4, CHUNK)
        on_scalar(
            out=woven[1, 0][:].bitcast(U32).rearrange("p (c i u) -> p c u i", u=2, i=2),
            in_=pairs[:].rearrange("p u c e -> p u (c e)").bitcast(U32).rearrange("p u (c i) -> p c u i", i=2),
        )
        for j in (1, 0):
            operand(1, j)
            passes([accs[1][t][:, 0, :] for t in range(SLOTS)], 1, j, slice(0, CHUNK), j == 1, False)

        out_codes = sbuf("out_codes", [P, S], U32)
        out_plane = sbuf("out_plane", [P, S], U8, "plane1_0")
        out_rows = out_0.rearrange("(p t) n -> p t n", t=SLOTS)
        out_words = word_rows(out_1)
        early = sbuf("early", [P, 2, SLOTS, UNIT], F32)
        results = [None, sbuf("result1", [P, SLOTS, CHUNK], F32)]
        rounded = [sbuf("rounded0", [P, SLOTS * CHUNK], BF16, "woven1_0"), sbuf("rounded1", [P, SLOTS * CHUNK], BF16)]

        def store(c, slots):
            nc.sync.dma_start(out=out_rows[:, slots, part(c, CHUNK)], in_=results[c][:, slots, :])

        def weave(copy, c, lo, hi):
            copy(out=as_woven(rounded[c][:, SLOTS * lo : SLOTS * hi], 4), in_=as_planar(results[c][:, :, lo:hi], 4))

        def hand_on(c):
            quantise(out_codes[:, part(c, CHUNK)], out_plane[:, part(c, CHUNK)], rounded[c][:])
            nc.sync.dma_start(out=out_words[:, part(c, CHUNK)], in_=out_codes[:, part(c, CHUNK)].bitcast(I32))

        for a in range(2):
            on_scalar(out=early[:, a, :, :], in_=accs[0][a][:])
            nc.sync.dma_start(out=out_rows[:, :, part(a, UNIT)], in_=early[:, a, :, :])
        for a in range(2):
            on_vector(out=as_woven(rounded[0][:, part(a, SLOTS * UNIT)], 4), in_=as_planar(early[:, a, :, :], 4))
        for t in range(SLOTS):
            (on_vector if t == SLOTS - 1 else on_scalar)(out=results[1][:, t : t + 1, :], in_=accs[1][t][:])
            if t % 2:
                store(1, part(t // 2, 2))
        hand_on(0)
        weave(on_vector, 1, 0, VECTOR_ROUNDS_LAST)
        weave(on_scalar, 1, VECTOR_ROUNDS_LAST, CHUNK)
        hand_on(1)

        for q in range(P // QUADRANT):
            queue = nc.scalar if q % 2 else nc.sync
            queue.dma_start(
                out=out_2[0, SCALE_ROWS * q : SCALE_ROWS * (q + 1), :].bitcast(I32),
                in_=out_plane[QUADRANT * q : QUADRANT * q + SCALE_ROWS, :].bitcast(I32),
            )
